import numpy as np
import ml_dtypes


def mxq(x, axis, fmt="e4m3"):
    dtype, down = {"e4m3": (ml_dtypes.float8_e4m3fn, 7), "e5m2": (ml_dtypes.float8_e5m2, 14)}[fmt]
    v = np.moveaxis(np.asarray(x, np.float32).astype(ml_dtypes.bfloat16).astype(np.float64), axis, -1)
    blocks = v.reshape(v.shape[:-1] + (-1, 32))
    amax = np.abs(blocks).max(-1, keepdims=True)
    byte = np.maximum(np.where(amax > 0, np.frexp(amax)[1] - 1 + 127, 0) - down, 1)
    scale = np.exp2(byte - 127.0)
    codes = (blocks / scale).astype(np.float32).astype(dtype).astype(np.float64)
    return np.moveaxis((codes * scale).reshape(v.shape), -1, axis)


WIDE = False


def mx_kscale(k):
    if not WIDE:
        return np.ones(k)
    levels = np.array([10, -10, 5, -5, 0])
    if k % 512:
        return np.exp2(np.random.permutation(np.resize(levels, k // 32))).repeat(32)
    a = np.empty((k // 512, 16))
    for p in range(k // 512):
        a[p, :8] = np.random.permutation(np.resize(levels, 8))
        for g in range(8):
            far = levels[np.abs(levels - a[p, g]) >= 10]
            a[p, g + 8] = far[np.random.randint(len(far))]
    return np.exp2(a.ravel()).repeat(32)


def f64(x):
    return np.asarray(x).astype(np.float64)


def striped(idx):
    return np.tile(idx.reshape(-1, 16).T, (8, 1)).astype(np.uint16)


def unstriped(offs):
    return offs[:16].T.reshape(-1).astype(np.int64)


E2M1 = np.array([0.0, 0.5, 1.0, 1.5, 2.0, 3.0, 4.0, 6.0, -0.0, -0.5, -1.0, -1.5, -2.0, -3.0, -4.0, -6.0])


def pack_weight(w, fmt):
    k, n = w.shape
    w = f64(np.asarray(w, np.float32).astype(ml_dtypes.bfloat16)).reshape(k // 32, 32, n)
    amax = np.abs(w).max(1)
    if fmt == "e4m3":
        byte = np.frexp(amax)[1] - 1 + 127 - 7
    else:
        mant, ex = np.frexp(amax / 6.0)
        byte = np.where(mant > 0.5, ex, ex - 1) + 127
    byte = np.clip(np.where(amax > 0, byte, 1), 1, 254)
    scaled = (w * np.exp2(127.0 - byte)[:, None, :]).reshape(k, n).astype(np.float32)
    by_word = np.ascontiguousarray(scaled.reshape(k // 512, 128, 4, n).transpose(0, 1, 3, 2))
    if fmt == "e4m3":
        words = by_word.astype(ml_dtypes.float8_e4m3fn).view(np.uint8)
    else:
        c = by_word.astype(ml_dtypes.float4_e2m1fn).view(np.uint8) & 0xF
        words = (c[..., 0::2] | (c[..., 1::2] << 4)).reshape(k // 512, 128, 2 * n)
    return np.ascontiguousarray(words), np.ascontiguousarray(byte.astype(np.uint8).reshape(k // 512, 16, n))


def unpack_weight(words, scales, fmt):
    g, _, n = scales.shape
    words = np.ascontiguousarray(words).reshape(g, 128, n, -1)
    if fmt == "e4m3":
        vals = words.view(ml_dtypes.float8_e4m3fn).astype(np.float64)
    else:
        nib = np.empty((g, 128, n, 4), np.uint8)
        nib[..., 0::2] = words & 0xF
        nib[..., 1::2] = words >> 4
        vals = E2M1[nib]
    vals = vals * np.repeat(np.exp2(scales.astype(np.float64) - 127.0), 8, axis=1)[..., None]
    return vals.transpose(0, 1, 3, 2).reshape(g * 512, n)


def silu(v):
    return v / (1.0 + np.exp(-np.maximum(v, -700.0)))


K, T, E, C, H, N, HOT = 1536, 768, 6, 128, 512, 256, 1


def by_expert(wq, xq):
    return np.concatenate([wq[e].T @ xq[:, e * C:(e + 1) * C] for e in range(E)], axis=1)


def setup_inputs():
    n = np.random.standard_normal
    s = mx_kscale(K)
    u = mx_kscale(H)
    slot_token = np.concatenate([np.random.permutation(T)[:C] for e in range(E)])
    x = pack_weight(n((K, T)) * s[:, None], "e4m3")
    w1h = [pack_weight(m, "e4m3") for m in n((HOT, K, H)) / np.sqrt(K) / s[None, :, None] * u]
    w2h = [pack_weight(m, "e4m3") for m in n((HOT, H, N)) / np.sqrt(H) / u[None, :, None]]
    w1c = [pack_weight(m, "e2m1") for m in n((E - HOT, K, H)) / np.sqrt(K) / s[None, :, None] * u]
    w2c = [pack_weight(m, "e2m1") for m in n((E - HOT, H, N)) / np.sqrt(H) / u[None, :, None]]
    return {
        "x_words": x[0],
        "x_scales": x[1],
        "w1h_words": np.stack([m[0] for m in w1h]),
        "w1h_scales": np.stack([m[1] for m in w1h]),
        "w2h_words": np.stack([m[0] for m in w2h]),
        "w2h_scales": np.stack([m[1] for m in w2h]),
        "w1c_words": np.stack([m[0] for m in w1c]),
        "w1c_scales": np.stack([m[1] for m in w1c]),
        "w2c_words": np.stack([m[0] for m in w2c]),
        "w2c_scales": np.stack([m[1] for m in w2c]),
        "offs": striped(slot_token),
    }


def reference(x_words, x_scales, w1h_words, w1h_scales, w2h_words, w2h_scales, w1c_words, w1c_scales, w2c_words, w2c_scales, offs):
    w1h = np.stack([unpack_weight(w1h_words[e], w1h_scales[e], "e4m3") for e in range(HOT)])
    w2h = np.stack([unpack_weight(w2h_words[e], w2h_scales[e], "e4m3") for e in range(HOT)])
    w1c = np.stack([unpack_weight(w1c_words[e], w1c_scales[e], "e2m1") for e in range(E - HOT)])
    w2c = np.stack([unpack_weight(w2c_words[e], w2c_scales[e], "e2m1") for e in range(E - HOT)])
    idx = unstriped(offs)
    xq = unpack_weight(x_words, x_scales, "e4m3")[:, idx]
    w1 = [*w1h, *w1c]
    w2 = [*w2h, *w2c]
    h = silu(by_expert(w1, xq))
    y = by_expert(w2, mxq(h, 0, "e4m3"))
    out = y
    return out

@@ -1,0 +1,164 @@
+from contextlib import ExitStack
+
+import concourse.mybir as mybir
+from concourse.masks import make_identity
+
+K, T, E, C, H, N = 1536, 768, 6, 128, 512, 256
+FLOPS = 2 * E * C * (K * H + H * N)
+
+F32 = mybir.dt.float32
+BF16 = mybir.dt.bfloat16
+I32 = mybir.dt.int32
+U32 = mybir.dt.uint32
+U16 = mybir.dt.uint16
+U8 = mybir.dt.uint8
+FP8X4 = mybir.dt.float8_e4m3fn_x4
+FP4X4 = mybir.dt.float4_e2m1fn_x4
+SILU = mybir.ActivationFunctionType.Silu
+
+P = 128
+PASSES = K // 512
+COLD = E - 1
+GROUPS = ((0,), (1, 2), (3, 4), (5,))
+
+
+def tile_moe_hot_s_mlp_silu_kernel(
+    tc, x_words, x_scales, w1h_words, w1h_scales, w2h_words, w2h_scales,
+    w1c_words, w1c_scales, w2c_words, w2c_scales, offs, out,
+):
+    nc = tc.nc
+    with ExitStack() as ctx:
+        keep = ctx.enter_context(tc.tile_pool(name="keep", bufs=1))
+        psum = ctx.enter_context(tc.psum_pool(name="psum", bufs=1))
+
+        offsets = keep.tile([P, E * C // 16], U16, name="offsets")
+        xw = [keep.tile([P, T], I32, name="xw%d" % s, align_bytes=64) for s in range(PASSES)]
+        xs = keep.tile([P, PASSES, T], U8, name="xs", align_bytes=64)
+        w1 = [keep.tile([P, PASSES, H * (4 if e == 0 else 2)], U8, name="w1_%d" % e, align_bytes=64) for e in range(E)]
+        s1h = keep.tile([P, PASSES, H], U8, name="s1h", align_bytes=64)
+        s1c = keep.tile([P, COLD * PASSES, H], U8, name="s1c", align_bytes=64)
+        w2h = keep.tile([P, N * 4], U8, name="w2h", align_bytes=64)
+        w2c = keep.tile([P, COLD, N * 2], U8, name="w2c", align_bytes=64)
+        s2h = keep.tile([P, 1, N], U8, name="s2h", align_bytes=64)
+        s2c = keep.tile([P, COLD, N], U8, name="s2c", align_bytes=64)
+        ident = keep.tile([P, P], F32, name="ident")
+        warm = keep.tile([P, 8], F32, name="warm")
+
+        for plane in (xs, s1h, s1c, s2h, s2c):
+            nc.vector.memset(plane[:].bitcast(I32), 0)
+        make_identity(nc, ident[:])
+        nc.scalar.activation(out=warm[:, 0:1], in_=ident[:, 0:1], func=SILU)
+
+        def load_scales(plane, rows):
+            by_row = rows.bitcast(I32).rearrange("a (q r) c -> r q a c", r=4)
+            for r in range(4):
+                nc.sync.dma_start(out=plane[r:P:32, :, :].bitcast(I32), in_=by_row[r])
+
+        def load_x(s):
+            nc.sync.dma_start(out=xw[s][:], in_=x_words[s].rearrange("p t d -> p (t d)").bitcast(I32))
+
+        def load_w1(e):
+            if e == 0:
+                src = w1h_words[0].rearrange("s p i d -> p s (i d)")
+            else:
+                src = w1c_words[e - 1].rearrange("s p b -> p s b")
+            nc.sync.dma_start(out=w1[e][:].bitcast(I32), in_=src.bitcast(I32))
+
+        nc.sync.dma_start(offsets[:], offs)
+        for s in range(PASSES):
+            load_x(s)
+        load_scales(xs, x_scales)
+        load_w1(0)
+        load_scales(s1h, w1h_scales[0])
+        load_w1(1)
+        load_scales(s1c, w1c_scales.rearrange("f s b i -> (f s) b i"))
+        load_w1(2)
+        load_w1(3)
+        nc.sync.dma_start(out=w2h[:].bitcast(I32), in_=w2h_words[0, 0].rearrange("p n d -> p (n d)").bitcast(I32))
+        load_scales(s2h, w2h_scales[0])
+        load_w1(4)
+        load_w1(5)
+        nc.sync.dma_start(out=w2c[:].bitcast(I32), in_=w2c_words.rearrange("f s p b -> p (f s) b").bitcast(I32))
+        load_scales(s2c, w2c_scales.rearrange("f s b n -> (f s) b n"))
+
+        gathered = {}
+
+        def gather(group):
+            n = C * len(group)
+            words = keep.tile([P, PASSES, n], U32, name="gw%d" % group[0], align_bytes=64)
+            scales = keep.tile([P, PASSES, n], U8, name="gs%d" % group[0], align_bytes=64)
+            picks = offsets[:, group[0] * C // 16 : (group[-1] + 1) * C // 16]
+            for s in range(PASSES):
+                nc.vector.tensor_copy(out=words[:, s, :], in_=xw[s][:].bitcast(U32).indirect(picks))
+                nc.vector.tensor_copy(out=scales[:, s, :], in_=xs[:, s, :].indirect(picks))
+            for j, e in enumerate(group):
+                gathered[e] = (words, scales, slice(j * C, (j + 1) * C))
+
+        hidden = {}
+
+        def first_layer(e):
+            words, scales, cols = gathered[e]
+            pre = psum.tile([P, H], F32, name="pre%d" % (e % 2))
+            for s in range(PASSES):
+                nc.tensor.matmul_mx(
+                    out=pre[:],
+                    lhsT=words[:, s, cols].bitcast(FP8X4),
+                    lhsT_scale=scales[:, s, cols],
+                    rhs=w1[e][:, s, :].bitcast(FP8X4 if e == 0 else FP4X4),
+                    rhs_scale=s1h[:, s, :] if e == 0 else s1c[:, (e - 1) * PASSES + s, :],
+                    start=(s == 0),
+                    stop=(s == PASSES - 1),
+                )
+            h_rows = keep.tile([P, H], BF16, name="h_rows%d" % e, align_bytes=64)
+            nc.scalar.activation(
+                out=h_rows[:].rearrange("j (u p v) -> j u p v", u=2, v=2),
+                in_=pre[:].rearrange("j (p u v) -> j u p v", u=2, v=2),
+                func=SILU,
+            )
+            turned = psum.tile([P, 2, C], F32, name="turned%d" % (e % 2))
+            pairs = h_rows[:].bitcast(F32)
+            for u in range(2):
+                nc.tensor.transpose(turned[:, u, :], pairs[:, u * P : (u + 1) * P], ident[:])
+            h_cols = keep.tile([P, 4 * C], BF16, name="h_cols%d" % e, align_bytes=64)
+            nc.scalar.copy(
+                out=h_cols[:].bitcast(F32).rearrange("p (j u) -> p j u", u=2),
+                in_=turned[:].rearrange("p u j -> p j u"),
+            )
+            hidden[e] = h_cols
+
+        def second_layer(e):
+            codes = keep.tile([P, C], U32, name="h_codes%d" % e, align_bytes=64)
+            scales = keep.tile([P, C], U8, name="h_scales%d" % e, align_bytes=64)
+            nc.vector.quantize_mx(out=codes[:].bitcast(FP8X4), scales=scales[:], in_=hidden[e][:])
+            y = psum.tile([P, 2, C], F32, name="y%d" % (e % 2))
+            for m in range(2):
+                if e == 0:
+                    lhsT = w2h[:, m * 4 * P : (m + 1) * 4 * P].bitcast(FP8X4)
+                    lhsT_scale = s2h[:, 0, m * P : (m + 1) * P]
+                else:
+                    lhsT = w2c[:, e - 1, m * 2 * P : (m + 1) * 2 * P].bitcast(FP4X4)
+                    lhsT_scale = s2c[:, e - 1, m * P : (m + 1) * P]
+                nc.tensor.matmul_mx(
+                    out=y[:, m, :], lhsT=lhsT, lhsT_scale=lhsT_scale,
+                    rhs=codes[:].bitcast(FP8X4), rhs_scale=scales[:], start=True, stop=True,
+                )
+            result = keep.tile([P, 2, C], F32, name="result%d" % e)
+            nc.scalar.copy(out=result[:], in_=y[:])
+            nc.sync.dma_start(out=out.rearrange("(m p) j -> p m j", p=P)[:, :, e * C : (e + 1) * C], in_=result[:])
+
+        gather(GROUPS[0])
+        gather(GROUPS[1])
+        first_layer(0)
+        gather(GROUPS[2])
+        first_layer(1)
+        second_layer(0)
+        first_layer(2)
+        second_layer(1)
+        gather(GROUPS[3])
+        first_layer(3)
+        second_layer(2)
+        first_layer(4)
+        second_layer(3)
+        first_layer(5)
+        second_layer(4)
+        second_layer(5)

@@ -19,7 +19,10 @@ SILU = mybir.ActivationFunctionType.Silu
 P = 128
 PASSES = K // 512
 COLD = E - 1
-GROUPS = ((0,), (1, 2), (3, 4), (5,))
+GROUPS = ((1, 2), (3, 4), (5,), (0,))
+ORDER = (1, 2, 3, 4, 5, 0)
+EARLY = 2
+XS_SPLIT = 320
 
 
 def tile_moe_hot_s_mlp_silu_kernel(
@@ -32,11 +35,12 @@ def tile_moe_hot_s_mlp_silu_kernel(
         psum = ctx.enter_context(tc.psum_pool(name="psum", bufs=1))
 
         offsets = keep.tile([P, E * C // 16], U16, name="offsets")
-        xw = [keep.tile([P, T], I32, name="xw%d" % s, align_bytes=64) for s in range(PASSES)]
+        xw = keep.tile([P, PASSES, T], I32, name="xw", align_bytes=64)
         xs = keep.tile([P, PASSES, T], U8, name="xs", align_bytes=64)
         w1 = [keep.tile([P, PASSES, H * (4 if e == 0 else 2)], U8, name="w1_%d" % e, align_bytes=64) for e in range(E)]
         s1h = keep.tile([P, PASSES, H], U8, name="s1h", align_bytes=64)
-        s1c = keep.tile([P, COLD * PASSES, H], U8, name="s1c", align_bytes=64)
+        s1a = keep.tile([P, EARLY * PASSES, H], U8, name="s1a", align_bytes=64)
+        s1b = keep.tile([P, (COLD - EARLY) * PASSES, H], U8, name="s1b", align_bytes=64)
         w2h = keep.tile([P, N * 4], U8, name="w2h", align_bytes=64)
         w2c = keep.tile([P, COLD, N * 2], U8, name="w2c", align_bytes=64)
         s2h = keep.tile([P, 1, N], U8, name="s2h", align_bytes=64)
@@ -44,42 +48,40 @@ def tile_moe_hot_s_mlp_silu_kernel(
         ident = keep.tile([P, P], F32, name="ident")
         warm = keep.tile([P, 8], F32, name="warm")
 
-        for plane in (xs, s1h, s1c, s2h, s2c):
+        xs_flat = xs[:].rearrange("p s t -> p (s t)").bitcast(I32)
+        nc.vector.memset(xs_flat[:, 0:XS_SPLIT], 0)
+        nc.gpsimd.memset(xs_flat[:, XS_SPLIT:], 0)
+        for plane in (s1a, s2c, s1b, s1h, s2h):
             nc.vector.memset(plane[:].bitcast(I32), 0)
         make_identity(nc, ident[:])
-        nc.scalar.activation(out=warm[:, 0:1], in_=ident[:, 0:1], func=SILU)
 
-        def load_scales(plane, rows):
+        def load_scales(plane, rows, queue=nc.sync):
             by_row = rows.bitcast(I32).rearrange("a (q r) c -> r q a c", r=4)
             for r in range(4):
-                nc.sync.dma_start(out=plane[r:P:32, :, :].bitcast(I32), in_=by_row[r])
+                queue.dma_start(out=plane[r:P:32, :, :].bitcast(I32), in_=by_row[r])
 
-        def load_x(s):
-            nc.sync.dma_start(out=xw[s][:], in_=x_words[s].rearrange("p t d -> p (t d)").bitcast(I32))
-
-        def load_w1(e):
-            if e == 0:
-                src = w1h_words[0].rearrange("s p i d -> p s (i d)")
-            else:
-                src = w1c_words[e - 1].rearrange("s p b -> p s b")
+        def load_w1_cold(e):
+            src = w1c_words[e - 1].rearrange("s p b -> p s b")
             nc.sync.dma_start(out=w1[e][:].bitcast(I32), in_=src.bitcast(I32))
 
         nc.sync.dma_start(offsets[:], offs)
-        for s in range(PASSES):
-            load_x(s)
-        load_scales(xs, x_scales)
-        load_w1(0)
-        load_scales(s1h, w1h_scales[0])
-        load_w1(1)
-        load_scales(s1c, w1c_scales.rearrange("f s b i -> (f s) b i"))
-        load_w1(2)
-        load_w1(3)
+        load_scales(xs, x_scales, nc.scalar)
+        nc.scalar.activation(out=warm[:, 0:1], in_=ident[:, 0:1], func=SILU)
         nc.sync.dma_start(out=w2h[:].bitcast(I32), in_=w2h_words[0, 0].rearrange("p n d -> p (n d)").bitcast(I32))
-        load_scales(s2h, w2h_scales[0])
-        load_w1(4)
-        load_w1(5)
-        nc.sync.dma_start(out=w2c[:].bitcast(I32), in_=w2c_words.rearrange("f s p b -> p (f s) b").bitcast(I32))
+        nc.sync.dma_start(out=xw[:], in_=x_words.rearrange("s p t d -> p s (t d)").bitcast(I32))
+        load_scales(s1a, w1c_scales[0:EARLY].rearrange("f s b i -> (f s) b i"))
         load_scales(s2c, w2c_scales.rearrange("f s b n -> (f s) b n"))
+        load_w1_cold(1)
+        load_w1_cold(2)
+        load_scales(s1b, w1c_scales[EARLY:COLD].rearrange("f s b i -> (f s) b i"))
+        load_scales(s1h, w1h_scales[0])
+        load_w1_cold(3)
+        load_w1_cold(4)
+        load_w1_cold(5)
+        for s in range(PASSES):
+            nc.sync.dma_start(out=w1[0][:, s, :].bitcast(I32), in_=w1h_words[0, s].rearrange("p i d -> p (i d)").bitcast(I32))
+        nc.sync.dma_start(out=w2c[:].bitcast(I32), in_=w2c_words.rearrange("f s p b -> p (f s) b").bitcast(I32))
+        load_scales(s2h, w2h_scales[0])
 
         gathered = {}
 
@@ -88,24 +90,38 @@ def tile_moe_hot_s_mlp_silu_kernel(
             words = keep.tile([P, PASSES, n], U32, name="gw%d" % group[0], align_bytes=64)
             scales = keep.tile([P, PASSES, n], U8, name="gs%d" % group[0], align_bytes=64)
             picks = offsets[:, group[0] * C // 16 : (group[-1] + 1) * C // 16]
-            for s in range(PASSES):
-                nc.vector.tensor_copy(out=words[:, s, :], in_=xw[s][:].bitcast(U32).indirect(picks))
-                nc.vector.tensor_copy(out=scales[:, s, :], in_=xs[:, s, :].indirect(picks))
+            steps = [(s, sort) for s in range(PASSES) for sort in ("scales", "words")]
+            if group == GROUPS[0]:
+                steps = sorted(steps, key=lambda step: step[1])
+            for s, sort in steps:
+                if sort == "scales":
+                    nc.vector.tensor_copy(out=scales[:, s, :], in_=xs[:, s, :].indirect(picks))
+                else:
+                    nc.vector.tensor_copy(out=words[:, s, :], in_=xw[:, s, :].bitcast(U32).indirect(picks))
             for j, e in enumerate(group):
                 gathered[e] = (words, scales, slice(j * C, (j + 1) * C))
 
         hidden = {}
+        rows = {}
+        packed = {}
+
+        def w1_scale(e, s):
+            if e == 0:
+                return s1h[:, s, :]
+            if e <= EARLY:
+                return s1a[:, (e - 1) * PASSES + s, :]
+            return s1b[:, (e - 1 - EARLY) * PASSES + s, :]
 
         def first_layer(e):
             words, scales, cols = gathered[e]
-            pre = psum.tile([P, H], F32, name="pre%d" % (e % 2))
+            pre = psum.tile([P, H], F32, name="pre%d" % (ORDER.index(e) % 3))
             for s in range(PASSES):
                 nc.tensor.matmul_mx(
                     out=pre[:],
                     lhsT=words[:, s, cols].bitcast(FP8X4),
                     lhsT_scale=scales[:, s, cols],
                     rhs=w1[e][:, s, :].bitcast(FP8X4 if e == 0 else FP4X4),
-                    rhs_scale=s1h[:, s, :] if e == 0 else s1c[:, (e - 1) * PASSES + s, :],
+                    rhs_scale=w1_scale(e, s),
                     start=(s == 0),
                     stop=(s == PASSES - 1),
                 )
@@ -115,6 +131,10 @@ def tile_moe_hot_s_mlp_silu_kernel(
                 in_=pre[:].rearrange("j (p u v) -> j u p v", u=2, v=2),
                 func=SILU,
             )
+            rows[e] = h_rows
+
+        def turn(e):
+            h_rows = rows[e]
             turned = psum.tile([P, 2, C], F32, name="turned%d" % (e % 2))
             pairs = h_rows[:].bitcast(F32)
             for u in range(2):
@@ -126,39 +146,58 @@ def tile_moe_hot_s_mlp_silu_kernel(
             )
             hidden[e] = h_cols
 
-        def second_layer(e):
+        def quantize(e):
             codes = keep.tile([P, C], U32, name="h_codes%d" % e, align_bytes=64)
             scales = keep.tile([P, C], U8, name="h_scales%d" % e, align_bytes=64)
             nc.vector.quantize_mx(out=codes[:].bitcast(FP8X4), scales=scales[:], in_=hidden[e][:])
-            y = psum.tile([P, 2, C], F32, name="y%d" % (e % 2))
-            for m in range(2):
-                if e == 0:
-                    lhsT = w2h[:, m * 4 * P : (m + 1) * 4 * P].bitcast(FP8X4)
-                    lhsT_scale = s2h[:, 0, m * P : (m + 1) * P]
-                else:
-                    lhsT = w2c[:, e - 1, m * 2 * P : (m + 1) * 2 * P].bitcast(FP4X4)
-                    lhsT_scale = s2c[:, e - 1, m * P : (m + 1) * P]
-                nc.tensor.matmul_mx(
-                    out=y[:, m, :], lhsT=lhsT, lhsT_scale=lhsT_scale,
-                    rhs=codes[:].bitcast(FP8X4), rhs_scale=scales[:], start=True, stop=True,
-                )
-            result = keep.tile([P, 2, C], F32, name="result%d" % e)
-            nc.scalar.copy(out=result[:], in_=y[:])
-            nc.sync.dma_start(out=out.rearrange("(m p) j -> p m j", p=P)[:, :, e * C : (e + 1) * C], in_=result[:])
+            packed[e] = (codes, scales)
 
-        gather(GROUPS[0])
-        gather(GROUPS[1])
-        first_layer(0)
-        gather(GROUPS[2])
-        first_layer(1)
-        second_layer(0)
-        first_layer(2)
-        second_layer(1)
-        gather(GROUPS[3])
-        first_layer(3)
-        second_layer(2)
-        first_layer(4)
-        second_layer(3)
-        first_layer(5)
-        second_layer(4)
-        second_layer(5)
+        def second_matmul(e, m, y):
+            codes, scales = packed[e]
+            if e == 0:
+                lhsT = w2h[:, m * 4 * P : (m + 1) * 4 * P].bitcast(FP8X4)
+                lhsT_scale = s2h[:, 0, m * P : (m + 1) * P]
+            else:
+                lhsT = w2c[:, e - 1, m * 2 * P : (m + 1) * 2 * P].bitcast(FP4X4)
+                lhsT_scale = s2c[:, e - 1, m * P : (m + 1) * P]
+            nc.tensor.matmul_mx(
+                out=y, lhsT=lhsT, lhsT_scale=lhsT_scale,
+                rhs=codes[:].bitcast(FP8X4), rhs_scale=scales[:], start=True, stop=True,
+            )
+
+        out_rows = out.rearrange("(m p) j -> p m j", p=P)
+
+        def second_layer(group):
+            n = len(group) * C
+            y = psum.tile([P, 2, n], F32, name="y%d" % (GROUPS.index(group) % 2))
+            for j, e in enumerate(group):
+                for m in range(2):
+                    second_matmul(e, m, y[:, m, j * C : (j + 1) * C])
+            result = keep.tile([P, 2, n], F32, name="result%d" % group[0])
+            nc.vector.tensor_copy(out=result[:], in_=y[:])
+            nc.sync.dma_start(out=out_rows[:, :, group[0] * C : group[0] * C + n], in_=result[:])
+
+        def last_second_layer(e):
+            for m in range(2):
+                y = psum.tile([P, C], F32, name="pre%d" % m)
+                second_matmul(e, m, y[:])
+                result = keep.tile([P, C], F32, name="result_last%d" % m)
+                if m == 0:
+                    nc.scalar.copy(out=result[:], in_=y[:])
+                    nc.scalar.dma_start(out=out_rows[:, m, e * C : (e + 1) * C], in_=result[:])
+                else:
+                    nc.vector.tensor_copy(out=result[:], in_=y[:])
+                    nc.sync.dma_start(out=out_rows[:, m, e * C : (e + 1) * C], in_=result[:])
+
+        for group in GROUPS:
+            gather(group)
+        for step in range(E + 1):
+            if step >= 1:
+                turn(ORDER[step - 1])
+            if step < E:
+                first_layer(ORDER[step])
+        for e in ORDER:
+            quantize(e)
+        last_second_layer(ORDER[-1])
+        for group in GROUPS[:-1]:
+            second_layer(group)

@@ -55,24 +55,23 @@ def tile_moe_hot_s_mlp_silu_kernel(
             nc.vector.memset(plane[:].bitcast(I32), 0)
         make_identity(nc, ident[:])
 
-        def load_scales(plane, rows, queue=nc.sync):
+        def load_scales(plane, rows):
             by_row = rows.bitcast(I32).rearrange("a (q r) c -> r q a c", r=4)
             for r in range(4):
-                queue.dma_start(out=plane[r:P:32, :, :].bitcast(I32), in_=by_row[r])
+                nc.sync.dma_start(out=plane[r:P:32, :, :].bitcast(I32), in_=by_row[r])
 
         def load_w1_cold(e):
             src = w1c_words[e - 1].rearrange("s p b -> p s b")
             nc.sync.dma_start(out=w1[e][:].bitcast(I32), in_=src.bitcast(I32))
 
         nc.sync.dma_start(offsets[:], offs)
-        load_scales(xs, x_scales, nc.scalar)
+        load_scales(xs, x_scales)
         nc.scalar.activation(out=warm[:, 0:1], in_=ident[:, 0:1], func=SILU)
-        nc.sync.dma_start(out=w2h[:].bitcast(I32), in_=w2h_words[0, 0].rearrange("p n d -> p (n d)").bitcast(I32))
         nc.sync.dma_start(out=xw[:], in_=x_words.rearrange("s p t d -> p s (t d)").bitcast(I32))
         load_scales(s1a, w1c_scales[0:EARLY].rearrange("f s b i -> (f s) b i"))
-        load_scales(s2c, w2c_scales.rearrange("f s b n -> (f s) b n"))
         load_w1_cold(1)
         load_w1_cold(2)
+        load_scales(s2c, w2c_scales.rearrange("f s b n -> (f s) b n"))
         load_scales(s1b, w1c_scales[EARLY:COLD].rearrange("f s b i -> (f s) b i"))
         load_scales(s1h, w1h_scales[0])
         load_w1_cold(3)
@@ -81,25 +80,32 @@ def tile_moe_hot_s_mlp_silu_kernel(
         for s in range(PASSES):
             nc.sync.dma_start(out=w1[0][:, s, :].bitcast(I32), in_=w1h_words[0, s].rearrange("p i d -> p (i d)").bitcast(I32))
         nc.sync.dma_start(out=w2c[:].bitcast(I32), in_=w2c_words.rearrange("f s p b -> p (f s) b").bitcast(I32))
+        nc.sync.dma_start(out=w2h[:].bitcast(I32), in_=w2h_words[0, 0].rearrange("p n d -> p (n d)").bitcast(I32))
         load_scales(s2h, w2h_scales[0])
 
-        gathered = {}
+        slot_words = {}
+        slot_scales = {}
 
-        def gather(group):
-            n = C * len(group)
-            words = keep.tile([P, PASSES, n], U32, name="gw%d" % group[0], align_bytes=64)
-            scales = keep.tile([P, PASSES, n], U8, name="gs%d" % group[0], align_bytes=64)
-            picks = offsets[:, group[0] * C // 16 : (group[-1] + 1) * C // 16]
-            steps = [(s, sort) for s in range(PASSES) for sort in ("scales", "words")]
-            if group == GROUPS[0]:
-                steps = sorted(steps, key=lambda step: step[1])
-            for s, sort in steps:
-                if sort == "scales":
-                    nc.vector.tensor_copy(out=scales[:, s, :], in_=xs[:, s, :].indirect(picks))
-                else:
-                    nc.vector.tensor_copy(out=words[:, s, :], in_=xw[:, s, :].bitcast(U32).indirect(picks))
+        def picks(group):
+            return offsets[:, group[0] * C // 16 : (group[-1] + 1) * C // 16]
+
+        def gather_scales(groups, tag):
+            scales = keep.tile([P, PASSES, 2 * C], U8, name=tag, align_bytes=64)
+            first = 0
+            for group in groups:
+                n = C * len(group)
+                for s in range(PASSES):
+                    nc.vector.tensor_copy(out=scales[:, s, first : first + n], in_=xs[:, s, :].indirect(picks(group)))
+                for j, e in enumerate(group):
+                    slot_scales[e] = (scales, slice(first + j * C, first + (j + 1) * C))
+                first += n
+
+        def gather_words(group):
+            words = keep.tile([P, PASSES, C * len(group)], U32, name="gw%d" % group[0], align_bytes=64)
+            for s in range(PASSES):
+                nc.vector.tensor_copy(out=words[:, s, :], in_=xw[:, s, :].bitcast(U32).indirect(picks(group)))
             for j, e in enumerate(group):
-                gathered[e] = (words, scales, slice(j * C, (j + 1) * C))
+                slot_words[e] = (words, slice(j * C, (j + 1) * C))
 
         hidden = {}
         rows = {}
@@ -113,34 +119,38 @@ def tile_moe_hot_s_mlp_silu_kernel(
             return s1b[:, (e - 1 - EARLY) * PASSES + s, :]
 
         def first_layer(e):
-            words, scales, cols = gathered[e]
+            words, cols = slot_words[e]
+            scales, scale_cols = slot_scales[e]
             pre = psum.tile([P, H], F32, name="pre%d" % (ORDER.index(e) % 3))
             for s in range(PASSES):
                 nc.tensor.matmul_mx(
                     out=pre[:],
                     lhsT=words[:, s, cols].bitcast(FP8X4),
-                    lhsT_scale=scales[:, s, cols],
+                    lhsT_scale=scales[:, s, scale_cols],
                     rhs=w1[e][:, s, :].bitcast(FP8X4 if e == 0 else FP4X4),
                     rhs_scale=w1_scale(e, s),
                     start=(s == 0),
                     stop=(s == PASSES - 1),
                 )
             h_rows = keep.tile([P, H], BF16, name="h_rows%d" % e, align_bytes=64)
-            nc.scalar.activation(
-                out=h_rows[:].rearrange("j (u p v) -> j u p v", u=2, v=2),
-                in_=pre[:].rearrange("j (p u v) -> j u p v", u=2, v=2),
-                func=SILU,
-            )
+            h_view = h_rows[:].rearrange("j (u p v) -> j u p v", u=2, v=2)
+            pre_view = pre[:].rearrange("j (p u v) -> j u p v", u=2, v=2)
+            if e == ORDER[-1]:
+                for u in range(2):
+                    nc.scalar.activation(out=h_view[:, u, :, :], in_=pre_view[:, u, :, :], func=SILU)
+            else:
+                nc.scalar.activation(out=h_view, in_=pre_view, func=SILU)
             rows[e] = h_rows
 
         def turn(e):
             h_rows = rows[e]
-            turned = psum.tile([P, 2, C], F32, name="turned%d" % (e % 2))
+            turned = psum.tile([P, 2, C], F32, name="pre2" if e == ORDER[1] else "turned%d" % (e % 2))
             pairs = h_rows[:].bitcast(F32)
             for u in range(2):
                 nc.tensor.transpose(turned[:, u, :], pairs[:, u * P : (u + 1) * P], ident[:])
             h_cols = keep.tile([P, 4 * C], BF16, name="h_cols%d" % e, align_bytes=64)
-            nc.scalar.copy(
+            copy = nc.vector.tensor_copy if e == ORDER[-2] else nc.scalar.copy
+            copy(
                 out=h_cols[:].bitcast(F32).rearrange("p (j u) -> p j u", u=2),
                 in_=turned[:].rearrange("p u j -> p j u"),
             )
@@ -174,7 +184,8 @@ def tile_moe_hot_s_mlp_silu_kernel(
                 for m in range(2):
                     second_matmul(e, m, y[:, m, j * C : (j + 1) * C])
             result = keep.tile([P, 2, n], F32, name="result%d" % group[0])
-            nc.vector.tensor_copy(out=result[:], in_=y[:])
+            copy = nc.scalar.copy if group == GROUPS[1] else nc.vector.tensor_copy
+            copy(out=result[:], in_=y[:])
             nc.sync.dma_start(out=out_rows[:, :, group[0] * C : group[0] * C + n], in_=result[:])
 
         def last_second_layer(e):
@@ -189,11 +200,18 @@ def tile_moe_hot_s_mlp_silu_kernel(
                     nc.vector.tensor_copy(out=result[:], in_=y[:])
                     nc.sync.dma_start(out=out_rows[:, m, e * C : (e + 1) * C], in_=result[:])
 
+        gather_scales(GROUPS[0:1], "gs_even")
+        gather_scales(GROUPS[1:2], "gs_odd")
         for group in GROUPS:
-            gather(group)
-        for step in range(E + 1):
-            if step >= 1:
-                turn(ORDER[step - 1])
+            gather_words(group)
+        first_layer(ORDER[0])
+        first_layer(ORDER[1])
+        gather_scales(GROUPS[2:4], "gs_even")
+        turn(ORDER[0])
+        first_layer(ORDER[2])
+        turn(ORDER[1])
+        for step in range(3, E + 1):
+            turn(ORDER[step - 1])
             if step < E:
                 first_layer(ORDER[step])
         for e in ORDER:

@@ -19,10 +19,11 @@ SILU = mybir.ActivationFunctionType.Silu
 P = 128
 PASSES = K // 512
 COLD = E - 1
-GROUPS = ((1, 2), (3, 4), (5,), (0,))
-ORDER = (1, 2, 3, 4, 5, 0)
-EARLY = 2
-XS_SPLIT = 320
+ORDER = (4, 5, 2, 3, 1, 0)
+LATE = 3
+HOT_ROW = 4
+WORD_COL = {4: 0, 5: C, 2: 2 * C, 3: 3 * C, 1: 0, 0: 2 * C}
+SCALE_COL = {4: C, 5: 2 * C, 2: 0, 3: C, 1: 2 * C, 0: 0}
 
 
 def tile_moe_hot_s_mlp_silu_kernel(
@@ -35,98 +36,88 @@ def tile_moe_hot_s_mlp_silu_kernel(
         psum = ctx.enter_context(tc.psum_pool(name="psum", bufs=1))
 
         offsets = keep.tile([P, E * C // 16], U16, name="offsets")
-        xw = keep.tile([P, PASSES, T], I32, name="xw", align_bytes=64)
+        xw_first = keep.tile([P, 1, T], I32, name="xw_first", align_bytes=64)
+        xw_rest = keep.tile([P, PASSES - 1, T], I32, name="xw_rest", align_bytes=64)
         xs = keep.tile([P, PASSES, T], U8, name="xs", align_bytes=64)
         w1 = [keep.tile([P, PASSES, H * (4 if e == 0 else 2)], U8, name="w1_%d" % e, align_bytes=64) for e in range(E)]
-        s1h = keep.tile([P, PASSES, H], U8, name="s1h", align_bytes=64)
-        s1a = keep.tile([P, EARLY * PASSES, H], U8, name="s1a", align_bytes=64)
-        s1b = keep.tile([P, (COLD - EARLY) * PASSES, H], U8, name="s1b", align_bytes=64)
+        s1a = keep.tile([P, (COLD - LATE) * PASSES, H], U8, name="s1a", align_bytes=64)
+        s1b = keep.tile([P, LATE * PASSES, H], U8, name="s1b", align_bytes=64)
         w2h = keep.tile([P, N * 4], U8, name="w2h", align_bytes=64)
         w2c = keep.tile([P, COLD, N * 2], U8, name="w2c", align_bytes=64)
-        s2h = keep.tile([P, 1, N], U8, name="s2h", align_bytes=64)
         s2c = keep.tile([P, COLD, N], U8, name="s2c", align_bytes=64)
         ident = keep.tile([P, P], F32, name="ident")
-        warm = keep.tile([P, 8], F32, name="warm")
+        slot_words = keep.tile([P, PASSES, 4 * C], U32, name="slot_words", align_bytes=64)
+        slot_scales = keep.tile([P, PASSES, 3 * C], U8, name="slot_scales", align_bytes=64)
 
-        xs_flat = xs[:].rearrange("p s t -> p (s t)").bitcast(I32)
-        nc.vector.memset(xs_flat[:, 0:XS_SPLIT], 0)
-        nc.gpsimd.memset(xs_flat[:, XS_SPLIT:], 0)
-        for plane in (s1a, s2c, s1b, s1h, s2h):
+        for plane in (xs, s1a, s1b):
             nc.vector.memset(plane[:].bitcast(I32), 0)
-        make_identity(nc, ident[:])
+        nc.gpsimd.memset(s2c[:].bitcast(I32), 0)
 
-        def load_scales(plane, rows):
+        def load_scales(queue, plane, rows, first_row=0):
             by_row = rows.bitcast(I32).rearrange("a (q r) c -> r q a c", r=4)
             for r in range(4):
-                nc.sync.dma_start(out=plane[r:P:32, :, :].bitcast(I32), in_=by_row[r])
+                queue.dma_start(out=plane[first_row + r : P : 32, :, :].bitcast(I32), in_=by_row[r])
 
         def load_w1_cold(e):
             src = w1c_words[e - 1].rearrange("s p b -> p s b")
             nc.sync.dma_start(out=w1[e][:].bitcast(I32), in_=src.bitcast(I32))
 
+        x_rows = x_words.rearrange("s p t d -> p s (t d)").bitcast(I32)
         nc.sync.dma_start(offsets[:], offs)
-        load_scales(xs, x_scales)
-        nc.scalar.activation(out=warm[:, 0:1], in_=ident[:, 0:1], func=SILU)
-        nc.sync.dma_start(out=xw[:], in_=x_words.rearrange("s p t d -> p s (t d)").bitcast(I32))
-        load_scales(s1a, w1c_scales[0:EARLY].rearrange("f s b i -> (f s) b i"))
-        load_w1_cold(1)
-        load_w1_cold(2)
-        load_scales(s2c, w2c_scales.rearrange("f s b n -> (f s) b n"))
-        load_scales(s1b, w1c_scales[EARLY:COLD].rearrange("f s b i -> (f s) b i"))
-        load_scales(s1h, w1h_scales[0])
-        load_w1_cold(3)
-        load_w1_cold(4)
-        load_w1_cold(5)
+        nc.sync.dma_start(out=xw_first[:], in_=x_rows[:, 0:1, :])
+        load_scales(nc.sync, xs, x_scales)
+        nc.sync.dma_start(out=xw_rest[:], in_=x_rows[:, 1:PASSES, :])
+        load_scales(nc.sync, s1a, w1c_scales[LATE:COLD].rearrange("f s b i -> (f s) b i"))
+        load_w1_cold(ORDER[0])
+        load_w1_cold(ORDER[1])
+        load_scales(nc.sync, s1b, w1c_scales[0:LATE].rearrange("f s b i -> (f s) b i"))
+        load_w1_cold(ORDER[2])
+        load_w1_cold(ORDER[3])
+        load_scales(nc.sync, s1b[:, 0:PASSES, :], w1h_scales[0], HOT_ROW)
+        load_w1_cold(ORDER[4])
         for s in range(PASSES):
             nc.sync.dma_start(out=w1[0][:, s, :].bitcast(I32), in_=w1h_words[0, s].rearrange("p i d -> p (i d)").bitcast(I32))
         nc.sync.dma_start(out=w2c[:].bitcast(I32), in_=w2c_words.rearrange("f s p b -> p (f s) b").bitcast(I32))
         nc.sync.dma_start(out=w2h[:].bitcast(I32), in_=w2h_words[0, 0].rearrange("p n d -> p (n d)").bitcast(I32))
-        load_scales(s2h, w2h_scales[0])
-
-        slot_words = {}
-        slot_scales = {}
+        make_identity(nc, ident[:])
+        load_scales(nc.gpsimd, s2c, w2c_scales.rearrange("f s b n -> (f s) b n"))
+        load_scales(nc.gpsimd, s2c[:, 0:1, :], w2h_scales[0], HOT_ROW)
 
         def picks(group):
             return offsets[:, group[0] * C // 16 : (group[-1] + 1) * C // 16]
 
-        def gather_scales(groups, tag):
-            scales = keep.tile([P, PASSES, 2 * C], U8, name=tag, align_bytes=64)
-            first = 0
-            for group in groups:
-                n = C * len(group)
-                for s in range(PASSES):
-                    nc.vector.tensor_copy(out=scales[:, s, first : first + n], in_=xs[:, s, :].indirect(picks(group)))
-                for j, e in enumerate(group):
-                    slot_scales[e] = (scales, slice(first + j * C, first + (j + 1) * C))
-                first += n
+        def gather_scales(group, s):
+            first = SCALE_COL[group[0]]
+            nc.vector.tensor_copy(
+                out=slot_scales[:, s, first : first + C * len(group)], in_=xs[:, s, :].indirect(picks(group))
+            )
 
-        def gather_words(group):
-            words = keep.tile([P, PASSES, C * len(group)], U32, name="gw%d" % group[0], align_bytes=64)
-            for s in range(PASSES):
-                nc.vector.tensor_copy(out=words[:, s, :], in_=xw[:, s, :].bitcast(U32).indirect(picks(group)))
-            for j, e in enumerate(group):
-                slot_words[e] = (words, slice(j * C, (j + 1) * C))
-
-        hidden = {}
-        rows = {}
-        packed = {}
+        def gather_words(group, s):
+            first = WORD_COL[group[0]]
+            window = xw_first[:, 0, :] if s == 0 else xw_rest[:, s - 1, :]
+            nc.vector.tensor_copy(
+                out=slot_words[:, s, first : first + C * len(group)], in_=window.bitcast(U32).indirect(picks(group))
+            )
 
         def w1_scale(e, s):
             if e == 0:
-                return s1h[:, s, :]
-            if e <= EARLY:
-                return s1a[:, (e - 1) * PASSES + s, :]
-            return s1b[:, (e - 1 - EARLY) * PASSES + s, :]
+                return s1b[HOT_ROW:P, s, :]
+            if e > LATE:
+                return s1a[:, (e - 1 - LATE) * PASSES + s, :]
+            return s1b[:, (e - 1) * PASSES + s, :]
+
+        rows = {}
+        h_cols = keep.tile([P, E, 4 * C], BF16, name="h_cols", align_bytes=64)
+        h_codes = keep.tile([P, E, C], U32, name="h_codes", align_bytes=64)
+        h_scales = keep.tile([P, E, C], U8, name="h_scales", align_bytes=64)
 
         def first_layer(e):
-            words, cols = slot_words[e]
-            scales, scale_cols = slot_scales[e]
             pre = psum.tile([P, H], F32, name="pre%d" % (ORDER.index(e) % 3))
             for s in range(PASSES):
                 nc.tensor.matmul_mx(
                     out=pre[:],
-                    lhsT=words[:, s, cols].bitcast(FP8X4),
-                    lhsT_scale=scales[:, s, scale_cols],
+                    lhsT=slot_words[:, s, WORD_COL[e] : WORD_COL[e] + C].bitcast(FP8X4),
+                    lhsT_scale=slot_scales[:, s, SCALE_COL[e] : SCALE_COL[e] + C],
                     rhs=w1[e][:, s, :].bitcast(FP8X4 if e == 0 else FP4X4),
                     rhs_scale=w1_scale(e, s),
                     start=(s == 0),
@@ -143,48 +134,51 @@ def tile_moe_hot_s_mlp_silu_kernel(
             rows[e] = h_rows
 
         def turn(e):
-            h_rows = rows[e]
-            turned = psum.tile([P, 2, C], F32, name="pre2" if e == ORDER[1] else "turned%d" % (e % 2))
-            pairs = h_rows[:].bitcast(F32)
+            place = ORDER.index(e)
+            turned = psum.tile([P, 2, C], F32, name="turned%d" % (place % 2))
+            pairs = rows[e][:].bitcast(F32)
             for u in range(2):
                 nc.tensor.transpose(turned[:, u, :], pairs[:, u * P : (u + 1) * P], ident[:])
-            h_cols = keep.tile([P, 4 * C], BF16, name="h_cols%d" % e, align_bytes=64)
-            copy = nc.vector.tensor_copy if e == ORDER[-2] else nc.scalar.copy
-            copy(
-                out=h_cols[:].bitcast(F32).rearrange("p (j u) -> p j u", u=2),
+            nc.scalar.copy(
+                out=h_tiles[place].bitcast(F32).rearrange("p (j u) -> p j u", u=2),
                 in_=turned[:].rearrange("p u j -> p j u"),
             )
-            hidden[e] = h_cols
 
-        def quantize(e):
-            codes = keep.tile([P, C], U32, name="h_codes%d" % e, align_bytes=64)
-            scales = keep.tile([P, C], U8, name="h_scales%d" % e, align_bytes=64)
-            nc.vector.quantize_mx(out=codes[:].bitcast(FP8X4), scales=scales[:], in_=hidden[e][:])
-            packed[e] = (codes, scales)
+        h_flat = h_cols[:].rearrange("p e c -> p (e c)")
+        h_tiles = [h_flat[:, place * 4 * C : (place + 1) * 4 * C] for place in range(E)]
+        codes_flat = h_codes[:].rearrange("p e c -> p (e c)")
+        scales_flat = h_scales[:].rearrange("p e c -> p (e c)")
+
+        def quantize(first, count):
+            nc.vector.quantize_mx(
+                out=codes_flat[:, first * C : (first + count) * C].bitcast(FP8X4),
+                scales=scales_flat[:, first * C : (first + count) * C],
+                in_=h_flat[:, first * 4 * C : (first + count) * 4 * C],
+            )
 
         def second_matmul(e, m, y):
-            codes, scales = packed[e]
+            place = ORDER.index(e)
             if e == 0:
                 lhsT = w2h[:, m * 4 * P : (m + 1) * 4 * P].bitcast(FP8X4)
-                lhsT_scale = s2h[:, 0, m * P : (m + 1) * P]
+                lhsT_scale = s2c[HOT_ROW:P, 0, m * P : (m + 1) * P]
             else:
                 lhsT = w2c[:, e - 1, m * 2 * P : (m + 1) * 2 * P].bitcast(FP4X4)
                 lhsT_scale = s2c[:, e - 1, m * P : (m + 1) * P]
             nc.tensor.matmul_mx(
                 out=y, lhsT=lhsT, lhsT_scale=lhsT_scale,
-                rhs=codes[:].bitcast(FP8X4), rhs_scale=scales[:], start=True, stop=True,
+                rhs=codes_flat[:, place * C : (place + 1) * C].bitcast(FP8X4),
+                rhs_scale=scales_flat[:, place * C : (place + 1) * C], start=True, stop=True,
             )
 
         out_rows = out.rearrange("(m p) j -> p m j", p=P)
 
-        def second_layer(group):
+        def second_layer(group, copy):
             n = len(group) * C
-            y = psum.tile([P, 2, n], F32, name="y%d" % (GROUPS.index(group) % 2))
+            y = psum.tile([P, 2, n], F32, name="y%d" % group[0])
             for j, e in enumerate(group):
                 for m in range(2):
                     second_matmul(e, m, y[:, m, j * C : (j + 1) * C])
             result = keep.tile([P, 2, n], F32, name="result%d" % group[0])
-            copy = nc.scalar.copy if group == GROUPS[1] else nc.vector.tensor_copy
             copy(out=result[:], in_=y[:])
             nc.sync.dma_start(out=out_rows[:, :, group[0] * C : group[0] * C + n], in_=result[:])
 
@@ -200,22 +194,34 @@ def tile_moe_hot_s_mlp_silu_kernel(
                     nc.vector.tensor_copy(out=result[:], in_=y[:])
                     nc.sync.dma_start(out=out_rows[:, m, e * C : (e + 1) * C], in_=result[:])
 
-        gather_scales(GROUPS[0:1], "gs_even")
-        gather_scales(GROUPS[1:2], "gs_odd")
-        for group in GROUPS:
-            gather_words(group)
+        first_pair, second_pair = ORDER[0:2], ORDER[2:4]
+        for s in range(PASSES):
+            gather_scales(first_pair, s)
+        for pair in (first_pair, second_pair):
+            for s in range(PASSES):
+                gather_words(pair, s)
         first_layer(ORDER[0])
+        for s in range(PASSES):
+            gather_scales(second_pair, s)
+        for s in range(PASSES):
+            gather_words(ORDER[4:5], s)
         first_layer(ORDER[1])
-        gather_scales(GROUPS[2:4], "gs_even")
+        for s in range(PASSES):
+            gather_scales(ORDER[4:5], s)
         turn(ORDER[0])
         first_layer(ORDER[2])
-        turn(ORDER[1])
-        for step in range(3, E + 1):
-            turn(ORDER[step - 1])
-            if step < E:
-                first_layer(ORDER[step])
-        for e in ORDER:
-            quantize(e)
-        last_second_layer(ORDER[-1])
-        for group in GROUPS[:-1]:
-            second_layer(group)
+        for s in range(PASSES):
+            gather_scales(ORDER[5:6], s)
+            gather_words(ORDER[5:6], s)
+        for step in range(3, E):
+            turn(ORDER[step - 2])
+            first_layer(ORDER[step])
+        turn(ORDER[4])
+        turn(ORDER[5])
+        quantize(0, 4)
+        quantize(4, 1)
+        quantize(5, 1)
+        second_layer(first_pair, nc.vector.tensor_copy)
+        second_layer(second_pair, nc.vector.tensor_copy)
+        second_layer(ORDER[4:5], nc.scalar.copy)
+        last_second_layer(ORDER[5])

@@ -71,17 +71,18 @@ def tile_moe_hot_s_mlp_silu_kernel(
         load_w1_cold(ORDER[0])
         load_w1_cold(ORDER[1])
         load_scales(nc.sync, s1b, w1c_scales[0:LATE].rearrange("f s b i -> (f s) b i"))
+        load_scales(nc.sync, s2c, w2c_scales.rearrange("f s b n -> (f s) b n"))
         load_w1_cold(ORDER[2])
         load_w1_cold(ORDER[3])
         load_scales(nc.sync, s1b[:, 0:PASSES, :], w1h_scales[0], HOT_ROW)
         load_w1_cold(ORDER[4])
         for s in range(PASSES):
             nc.sync.dma_start(out=w1[0][:, s, :].bitcast(I32), in_=w1h_words[0, s].rearrange("p i d -> p (i d)").bitcast(I32))
+            if s == 0:
+                load_scales(nc.sync, s2c[:, 0:1, :], w2h_scales[0], HOT_ROW)
         nc.sync.dma_start(out=w2c[:].bitcast(I32), in_=w2c_words.rearrange("f s p b -> p (f s) b").bitcast(I32))
         nc.sync.dma_start(out=w2h[:].bitcast(I32), in_=w2h_words[0, 0].rearrange("p n d -> p (n d)").bitcast(I32))
         make_identity(nc, ident[:])
-        load_scales(nc.gpsimd, s2c, w2c_scales.rearrange("f s b n -> (f s) b n"))
-        load_scales(nc.gpsimd, s2c[:, 0:1, :], w2h_scales[0], HOT_ROW)
 
         def picks(group):
             return offsets[:, group[0] * C // 16 : (group[-1] + 1) * C // 16]

@@ -22,8 +22,12 @@ COLD = E - 1
 ORDER = (4, 5, 2, 3, 1, 0)
 LATE = 3
 HOT_ROW = 4
-WORD_COL = {4: 0, 5: C, 2: 2 * C, 3: 3 * C, 1: 0, 0: 2 * C}
-SCALE_COL = {4: C, 5: 2 * C, 2: 0, 3: C, 1: 2 * C, 0: 0}
+WORDS_AT = {(4, 0): 4352, (4, 2): 1024, (0, 0): 576, (0, 1): 1856, (0, 2): 3136, (2, 0): 6144}
+SCALES_AT = {
+    (4, 2): 3072, (2, 0): 4416, (2, 1): 4160, (2, 2): 4672,
+    (1, 0): 1088, (1, 1): 1216, (1, 2): 1344, (0, 0): 1472, (0, 1): 1600, (0, 2): 1728,
+}
+TURN_BANK = {4: "turned0", 5: "turned1", 2: "turned0", 3: "turned1", 1: "turned0", 0: "turned1"}
 
 
 def tile_moe_hot_s_mlp_silu_kernel(
@@ -33,6 +37,7 @@ def tile_moe_hot_s_mlp_silu_kernel(
     nc = tc.nc
     with ExitStack() as ctx:
         keep = ctx.enter_context(tc.tile_pool(name="keep", bufs=1))
+        stage = ctx.enter_context(tc.tile_pool(name="stage", bufs=1))
         psum = ctx.enter_context(tc.psum_pool(name="psum", bufs=1))
 
         offsets = keep.tile([P, E * C // 16], U16, name="offsets")
@@ -45,13 +50,13 @@ def tile_moe_hot_s_mlp_silu_kernel(
         w2h = keep.tile([P, N * 4], U8, name="w2h", align_bytes=64)
         w2c = keep.tile([P, COLD, N * 2], U8, name="w2c", align_bytes=64)
         s2c = keep.tile([P, COLD, N], U8, name="s2c", align_bytes=64)
+        s2h = keep.tile([P, 1, N], U8, name="s2h", align_bytes=64)
         ident = keep.tile([P, P], F32, name="ident")
-        slot_words = keep.tile([P, PASSES, 4 * C], U32, name="slot_words", align_bytes=64)
-        slot_scales = keep.tile([P, PASSES, 3 * C], U8, name="slot_scales", align_bytes=64)
 
+        for plane in (s2c, s2h):
+            nc.gpsimd.memset(plane[:].bitcast(I32), 0)
         for plane in (xs, s1a, s1b):
             nc.vector.memset(plane[:].bitcast(I32), 0)
-        nc.gpsimd.memset(s2c[:].bitcast(I32), 0)
 
         def load_scales(queue, plane, rows, first_row=0):
             by_row = rows.bitcast(I32).rearrange("a (q r) c -> r q a c", r=4)
@@ -70,35 +75,44 @@ def tile_moe_hot_s_mlp_silu_kernel(
         load_scales(nc.sync, s1a, w1c_scales[LATE:COLD].rearrange("f s b i -> (f s) b i"))
         load_w1_cold(ORDER[0])
         load_w1_cold(ORDER[1])
-        load_scales(nc.sync, s1b, w1c_scales[0:LATE].rearrange("f s b i -> (f s) b i"))
         load_scales(nc.sync, s2c, w2c_scales.rearrange("f s b n -> (f s) b n"))
+        load_scales(nc.sync, s1b, w1c_scales[0:LATE].rearrange("f s b i -> (f s) b i"))
+        load_scales(nc.sync, s1b[:, 0:PASSES, :], w1h_scales[0], HOT_ROW)
         load_w1_cold(ORDER[2])
         load_w1_cold(ORDER[3])
-        load_scales(nc.sync, s1b[:, 0:PASSES, :], w1h_scales[0], HOT_ROW)
         load_w1_cold(ORDER[4])
         for s in range(PASSES):
             nc.sync.dma_start(out=w1[0][:, s, :].bitcast(I32), in_=w1h_words[0, s].rearrange("p i d -> p (i d)").bitcast(I32))
-            if s == 0:
-                load_scales(nc.sync, s2c[:, 0:1, :], w2h_scales[0], HOT_ROW)
         nc.sync.dma_start(out=w2c[:].bitcast(I32), in_=w2c_words.rearrange("f s p b -> p (f s) b").bitcast(I32))
         nc.sync.dma_start(out=w2h[:].bitcast(I32), in_=w2h_words[0, 0].rearrange("p n d -> p (n d)").bitcast(I32))
+        load_scales(nc.sync, s2h, w2h_scales[0])
         make_identity(nc, ident[:])
 
         def picks(group):
             return offsets[:, group[0] * C // 16 : (group[-1] + 1) * C // 16]
 
+        slot_words = {}
+        slot_scales = {}
+
+        def slot_tile(group, s, dtype, name, places):
+            shape = [P, C * len(group)]
+            name = "%s%d_%d" % (name, group[0], s)
+            if (group[0], s) in places:
+                return stage.tile(shape, dtype, name=name, align_bytes=64, offset=places[group[0], s])
+            return keep.tile(shape, dtype, name=name, align_bytes=64)
+
         def gather_scales(group, s):
-            first = SCALE_COL[group[0]]
-            nc.vector.tensor_copy(
-                out=slot_scales[:, s, first : first + C * len(group)], in_=xs[:, s, :].indirect(picks(group))
-            )
+            scales = slot_tile(group, s, U8, "slot_scales", SCALES_AT)
+            nc.vector.tensor_copy(out=scales[:], in_=xs[:, s, :].indirect(picks(group)))
+            for j, e in enumerate(group):
+                slot_scales[e, s] = scales[:, j * C : (j + 1) * C]
 
         def gather_words(group, s):
-            first = WORD_COL[group[0]]
+            words = slot_tile(group, s, U32, "slot_words", WORDS_AT)
             window = xw_first[:, 0, :] if s == 0 else xw_rest[:, s - 1, :]
-            nc.vector.tensor_copy(
-                out=slot_words[:, s, first : first + C * len(group)], in_=window.bitcast(U32).indirect(picks(group))
-            )
+            nc.vector.tensor_copy(out=words[:], in_=window.bitcast(U32).indirect(picks(group)))
+            for j, e in enumerate(group):
+                slot_words[e, s] = words[:, j * C : (j + 1) * C]
 
         def w1_scale(e, s):
             if e == 0:
@@ -108,7 +122,8 @@ def tile_moe_hot_s_mlp_silu_kernel(
             return s1b[:, (e - 1) * PASSES + s, :]
 
         rows = {}
-        h_cols = keep.tile([P, E, 4 * C], BF16, name="h_cols", align_bytes=64)
+        pres = {}
+        h_cols = {}
         h_codes = keep.tile([P, E, C], U32, name="h_codes", align_bytes=64)
         h_scales = keep.tile([P, E, C], U8, name="h_scales", align_bytes=64)
 
@@ -117,14 +132,21 @@ def tile_moe_hot_s_mlp_silu_kernel(
             for s in range(PASSES):
                 nc.tensor.matmul_mx(
                     out=pre[:],
-                    lhsT=slot_words[:, s, WORD_COL[e] : WORD_COL[e] + C].bitcast(FP8X4),
-                    lhsT_scale=slot_scales[:, s, SCALE_COL[e] : SCALE_COL[e] + C],
+                    lhsT=slot_words[e, s].bitcast(FP8X4),
+                    lhsT_scale=slot_scales[e, s],
                     rhs=w1[e][:, s, :].bitcast(FP8X4 if e == 0 else FP4X4),
                     rhs_scale=w1_scale(e, s),
                     start=(s == 0),
                     stop=(s == PASSES - 1),
                 )
-            h_rows = keep.tile([P, H], BF16, name="h_rows%d" % e, align_bytes=64)
+            pres[e] = pre
+
+        def activate(e):
+            pre = pres[e]
+            if e == ORDER[1]:
+                h_rows = stage.tile([P, H], BF16, name="h_rows%d" % e, align_bytes=64, offset=WORDS_AT[ORDER[2], 0])
+            else:
+                h_rows = keep.tile([P, H], BF16, name="h_rows%d" % e, align_bytes=64)
             h_view = h_rows[:].rearrange("j (u p v) -> j u p v", u=2, v=2)
             pre_view = pre[:].rearrange("j (p u v) -> j u p v", u=2, v=2)
             if e == ORDER[-1]:
@@ -134,19 +156,26 @@ def tile_moe_hot_s_mlp_silu_kernel(
                 nc.scalar.activation(out=h_view, in_=pre_view, func=SILU)
             rows[e] = h_rows
 
+        def h_place(place):
+            first, count = (0, 4) if place < 4 else (place, 1)
+            if first not in h_cols:
+                shape = [P, count * 4 * C]
+                name = "h_cols%d" % first
+                h_cols[first] = keep.tile(shape, BF16, name=name, align_bytes=64)
+            return h_cols[first][:, (place - first) * 4 * C : (place - first + 1) * 4 * C]
+
         def turn(e):
             place = ORDER.index(e)
-            turned = psum.tile([P, 2, C], F32, name="turned%d" % (place % 2))
+            turned = psum.tile([P, 2, C], F32, name=TURN_BANK[e])
             pairs = rows[e][:].bitcast(F32)
             for u in range(2):
                 nc.tensor.transpose(turned[:, u, :], pairs[:, u * P : (u + 1) * P], ident[:])
-            nc.scalar.copy(
-                out=h_tiles[place].bitcast(F32).rearrange("p (j u) -> p j u", u=2),
+            copy = nc.vector.tensor_copy if e == ORDER[4] else nc.scalar.copy
+            copy(
+                out=h_place(place).bitcast(F32).rearrange("p (j u) -> p j u", u=2),
                 in_=turned[:].rearrange("p u j -> p j u"),
             )
 
-        h_flat = h_cols[:].rearrange("p e c -> p (e c)")
-        h_tiles = [h_flat[:, place * 4 * C : (place + 1) * 4 * C] for place in range(E)]
         codes_flat = h_codes[:].rearrange("p e c -> p (e c)")
         scales_flat = h_scales[:].rearrange("p e c -> p (e c)")
 
@@ -154,14 +183,14 @@ def tile_moe_hot_s_mlp_silu_kernel(
             nc.vector.quantize_mx(
                 out=codes_flat[:, first * C : (first + count) * C].bitcast(FP8X4),
                 scales=scales_flat[:, first * C : (first + count) * C],
-                in_=h_flat[:, first * 4 * C : (first + count) * 4 * C],
+                in_=h_cols[first][:],
             )
 
         def second_matmul(e, m, y):
             place = ORDER.index(e)
             if e == 0:
                 lhsT = w2h[:, m * 4 * P : (m + 1) * 4 * P].bitcast(FP8X4)
-                lhsT_scale = s2c[HOT_ROW:P, 0, m * P : (m + 1) * P]
+                lhsT_scale = s2h[:, 0, m * P : (m + 1) * P]
             else:
                 lhsT = w2c[:, e - 1, m * 2 * P : (m + 1) * 2 * P].bitcast(FP4X4)
                 lhsT_scale = s2c[:, e - 1, m * P : (m + 1) * P]
@@ -198,31 +227,40 @@ def tile_moe_hot_s_mlp_silu_kernel(
         first_pair, second_pair = ORDER[0:2], ORDER[2:4]
         for s in range(PASSES):
             gather_scales(first_pair, s)
-        for pair in (first_pair, second_pair):
+        for e in ORDER[0:4]:
+            gather_words((e,), 0)
+        for group in (first_pair, second_pair, ORDER[4:5]):
             for s in range(PASSES):
-                gather_words(pair, s)
+                if (group[0], s) not in slot_words:
+                    gather_words(group, s)
         first_layer(ORDER[0])
-        for s in range(PASSES):
-            gather_scales(second_pair, s)
-        for s in range(PASSES):
-            gather_words(ORDER[4:5], s)
+        activate(ORDER[0])
         first_layer(ORDER[1])
-        for s in range(PASSES):
-            gather_scales(ORDER[4:5], s)
-        turn(ORDER[0])
-        first_layer(ORDER[2])
+        for group in (second_pair, ORDER[4:5]):
+            for s in range(PASSES):
+                gather_scales(group, s)
         for s in range(PASSES):
             gather_scales(ORDER[5:6], s)
             gather_words(ORDER[5:6], s)
-        for step in range(3, E):
-            turn(ORDER[step - 2])
-            first_layer(ORDER[step])
+        turn(ORDER[0])
+        first_layer(ORDER[2])
+        activate(ORDER[1])
+        activate(ORDER[2])
+        first_layer(ORDER[3])
+        activate(ORDER[3])
+        turn(ORDER[1])
+        first_layer(ORDER[4])
+        activate(ORDER[4])
+        for e in second_pair:
+            turn(e)
+        first_layer(ORDER[5])
+        activate(ORDER[5])
         turn(ORDER[4])
-        turn(ORDER[5])
         quantize(0, 4)
         quantize(4, 1)
-        quantize(5, 1)
-        second_layer(first_pair, nc.vector.tensor_copy)
+        second_layer(first_pair, nc.scalar.copy)
         second_layer(second_pair, nc.vector.tensor_copy)
-        second_layer(ORDER[4:5], nc.scalar.copy)
+        turn(ORDER[5])
+        quantize(5, 1)
+        second_layer(ORDER[4:5], nc.vector.tensor_copy)
         last_second_layer(ORDER[5])

@@ -19,15 +19,47 @@ SILU = mybir.ActivationFunctionType.Silu
 P = 128
 PASSES = K // 512
 COLD = E - 1
-ORDER = (4, 5, 2, 3, 1, 0)
+HOT = 0
+ORDER = (4, 5, 2, 3, 1, HOT)
+FIRST_PAIR, SECOND_PAIR, FIFTH = ORDER[0:2], ORDER[2:4], ORDER[4]
 LATE = 3
 HOT_ROW = 4
-WORDS_AT = {(4, 0): 4352, (4, 2): 1024, (0, 0): 576, (0, 1): 1856, (0, 2): 3136, (2, 0): 6144}
-SCALES_AT = {
-    (4, 2): 3072, (2, 0): 4416, (2, 1): 4160, (2, 2): 4672,
-    (1, 0): 1088, (1, 1): 1216, (1, 2): 1344, (0, 0): 1472, (0, 1): 1600, (0, 2): 1728,
-}
-TURN_BANK = {4: "turned0", 5: "turned1", 2: "turned0", 3: "turned1", 1: "turned0", 0: "turned1"}
+PRE_BANKS = 3
+TURN_BANKS = 2
+ALIGN = 64
+
+FOLLOWS = (
+    (("words", 4, 0), (("scales", 2, 1), ("scales", 2, 0), ("scales", 2, 2))),
+    (("words", 5, 0), (("rows", 4, 0), ("scales", 1, 0), ("scales", 1, 1), ("scales", 1, 2))),
+    (("words", 2, 0), (("rows", 5, 0),)),
+    (("words", 3, 0), (("rows", 2, 0),)),
+    (
+        ("words", 4, 2),
+        (("words", 0, 0), ("scales", 0, 0), ("scales", 0, 1), ("scales", 0, 2), ("words", 0, 1), ("words", 0, 2)),
+    ),
+)
+
+
+def tile_bytes(kind, expert, s):
+    if kind == "rows":
+        return 2 * H
+    if kind == "scales":
+        return (2 if expert == SECOND_PAIR[0] else 1) * C
+    return (2 if expert == FIRST_PAIR[0] and s > 0 else 1) * 4 * C
+
+
+def shared_places():
+    places = {}
+    start = 0
+    for host, guests in FOLLOWS:
+        places[host] = start + tile_bytes(*guests[0]) - ALIGN
+        host_end = places[host] + tile_bytes(*host)
+        for guest in guests:
+            assert start < host_end
+            places[guest] = start
+            start += tile_bytes(*guest)
+        start = max(start, host_end)
+    return places
 
 
 def tile_moe_hot_s_mlp_silu_kernel(
@@ -35,174 +67,165 @@ def tile_moe_hot_s_mlp_silu_kernel(
     w1c_words, w1c_scales, w2c_words, w2c_scales, offs, out,
 ):
     nc = tc.nc
+    places = shared_places()
     with ExitStack() as ctx:
         keep = ctx.enter_context(tc.tile_pool(name="keep", bufs=1))
-        stage = ctx.enter_context(tc.tile_pool(name="stage", bufs=1))
+        shared = ctx.enter_context(tc.tile_pool(name="shared", bufs=1))
         psum = ctx.enter_context(tc.psum_pool(name="psum", bufs=1))
 
+        def work_tile(key, columns, dtype):
+            name = "%s%d_%d" % key
+            if key in places:
+                return shared.tile([P, columns], dtype, name=name, align_bytes=ALIGN, offset=places[key])
+            return keep.tile([P, columns], dtype, name=name, align_bytes=ALIGN)
+
         offsets = keep.tile([P, E * C // 16], U16, name="offsets")
-        xw_first = keep.tile([P, 1, T], I32, name="xw_first", align_bytes=64)
-        xw_rest = keep.tile([P, PASSES - 1, T], I32, name="xw_rest", align_bytes=64)
-        xs = keep.tile([P, PASSES, T], U8, name="xs", align_bytes=64)
-        w1 = [keep.tile([P, PASSES, H * (4 if e == 0 else 2)], U8, name="w1_%d" % e, align_bytes=64) for e in range(E)]
-        s1a = keep.tile([P, (COLD - LATE) * PASSES, H], U8, name="s1a", align_bytes=64)
-        s1b = keep.tile([P, LATE * PASSES, H], U8, name="s1b", align_bytes=64)
-        w2h = keep.tile([P, N * 4], U8, name="w2h", align_bytes=64)
-        w2c = keep.tile([P, COLD, N * 2], U8, name="w2c", align_bytes=64)
-        s2c = keep.tile([P, COLD, N], U8, name="s2c", align_bytes=64)
-        s2h = keep.tile([P, 1, N], U8, name="s2h", align_bytes=64)
+        xw_first = keep.tile([P, 1, T], I32, name="xw_first", align_bytes=ALIGN)
+        xw_rest = keep.tile([P, PASSES - 1, T], I32, name="xw_rest", align_bytes=ALIGN)
+        xs = keep.tile([P, PASSES, T], U8, name="xs", align_bytes=ALIGN)
+        w1 = [
+            keep.tile([P, PASSES, H * (4 if e == HOT else 2)], U8, name="w1_%d" % e, align_bytes=ALIGN)
+            for e in range(E)
+        ]
+        s1_early = keep.tile([P, (COLD - LATE) * PASSES, H], U8, name="s1_early", align_bytes=ALIGN)
+        s1_late = keep.tile([P, LATE * PASSES, H], U8, name="s1_late", align_bytes=ALIGN)
+        w2h = keep.tile([P, N * 4], U8, name="w2h", align_bytes=ALIGN)
+        w2c = keep.tile([P, COLD, N * 2], U8, name="w2c", align_bytes=ALIGN)
+        s2c = keep.tile([P, COLD, N], U8, name="s2c", align_bytes=ALIGN)
+        s2h = keep.tile([P, 1, N], U8, name="s2h", align_bytes=ALIGN)
         ident = keep.tile([P, P], F32, name="ident")
+        h_codes = keep.tile([P, E * C], U32, name="h_codes", align_bytes=ALIGN)
+        h_scales = keep.tile([P, E * C], U8, name="h_scales", align_bytes=ALIGN)
 
         for plane in (s2c, s2h):
             nc.gpsimd.memset(plane[:].bitcast(I32), 0)
-        for plane in (xs, s1a, s1b):
+        for plane in (xs, s1_early, s1_late):
             nc.vector.memset(plane[:].bitcast(I32), 0)
 
-        def load_scales(queue, plane, rows, first_row=0):
+        def load_scales(plane, rows, first_row=0):
             by_row = rows.bitcast(I32).rearrange("a (q r) c -> r q a c", r=4)
             for r in range(4):
-                queue.dma_start(out=plane[first_row + r : P : 32, :, :].bitcast(I32), in_=by_row[r])
+                nc.sync.dma_start(out=plane[first_row + r : P : 32, :, :].bitcast(I32), in_=by_row[r])
 
         def load_w1_cold(e):
-            src = w1c_words[e - 1].rearrange("s p b -> p s b")
-            nc.sync.dma_start(out=w1[e][:].bitcast(I32), in_=src.bitcast(I32))
+            nc.sync.dma_start(out=w1[e][:].bitcast(I32), in_=w1c_words[e - 1].rearrange("s p b -> p s b").bitcast(I32))
 
         x_rows = x_words.rearrange("s p t d -> p s (t d)").bitcast(I32)
         nc.sync.dma_start(offsets[:], offs)
         nc.sync.dma_start(out=xw_first[:], in_=x_rows[:, 0:1, :])
-        load_scales(nc.sync, xs, x_scales)
+        load_scales(xs, x_scales)
         nc.sync.dma_start(out=xw_rest[:], in_=x_rows[:, 1:PASSES, :])
-        load_scales(nc.sync, s1a, w1c_scales[LATE:COLD].rearrange("f s b i -> (f s) b i"))
-        load_w1_cold(ORDER[0])
-        load_w1_cold(ORDER[1])
-        load_scales(nc.sync, s2c, w2c_scales.rearrange("f s b n -> (f s) b n"))
-        load_scales(nc.sync, s1b, w1c_scales[0:LATE].rearrange("f s b i -> (f s) b i"))
-        load_scales(nc.sync, s1b[:, 0:PASSES, :], w1h_scales[0], HOT_ROW)
-        load_w1_cold(ORDER[2])
-        load_w1_cold(ORDER[3])
-        load_w1_cold(ORDER[4])
+        load_scales(s1_early, w1c_scales[LATE:COLD].rearrange("f s b i -> (f s) b i"))
+        load_w1_cold(FIRST_PAIR[0])
+        load_scales(s2c, w2c_scales.rearrange("f s b n -> (f s) b n"))
+        load_w1_cold(FIRST_PAIR[1])
+        load_scales(s1_late, w1c_scales[0:LATE].rearrange("f s b i -> (f s) b i"))
+        load_w1_cold(SECOND_PAIR[0])
+        load_scales(s1_late[:, 0:PASSES, :], w1h_scales[0], HOT_ROW)
+        load_w1_cold(SECOND_PAIR[1])
+        load_w1_cold(FIFTH)
         for s in range(PASSES):
-            nc.sync.dma_start(out=w1[0][:, s, :].bitcast(I32), in_=w1h_words[0, s].rearrange("p i d -> p (i d)").bitcast(I32))
-        nc.sync.dma_start(out=w2c[:].bitcast(I32), in_=w2c_words.rearrange("f s p b -> p (f s) b").bitcast(I32))
+            hot_pass = w1h_words[0, s].rearrange("p i d -> p (i d)")
+            nc.sync.dma_start(out=w1[HOT][:, s, :].bitcast(I32), in_=hot_pass.bitcast(I32))
+        w2c_rows = w2c_words.rearrange("f s p b -> p (f s) b").bitcast(I32)
+        for matrices in (slice(LATE, COLD), slice(0, LATE)):
+            nc.sync.dma_start(out=w2c[:, matrices, :].bitcast(I32), in_=w2c_rows[:, matrices, :])
         nc.sync.dma_start(out=w2h[:].bitcast(I32), in_=w2h_words[0, 0].rearrange("p n d -> p (n d)").bitcast(I32))
-        load_scales(nc.sync, s2h, w2h_scales[0])
+        load_scales(s2h, w2h_scales[0])
         make_identity(nc, ident[:])
-
-        def picks(group):
-            return offsets[:, group[0] * C // 16 : (group[-1] + 1) * C // 16]
 
         slot_words = {}
         slot_scales = {}
 
-        def slot_tile(group, s, dtype, name, places):
-            shape = [P, C * len(group)]
-            name = "%s%d_%d" % (name, group[0], s)
-            if (group[0], s) in places:
-                return stage.tile(shape, dtype, name=name, align_bytes=64, offset=places[group[0], s])
-            return keep.tile(shape, dtype, name=name, align_bytes=64)
+        def picks(group):
+            return offsets[:, group[0] * C // 16 : (group[-1] + 1) * C // 16]
 
         def gather_scales(group, s):
-            scales = slot_tile(group, s, U8, "slot_scales", SCALES_AT)
+            scales = work_tile(("scales", group[0], s), C * len(group), U8)
             nc.vector.tensor_copy(out=scales[:], in_=xs[:, s, :].indirect(picks(group)))
             for j, e in enumerate(group):
                 slot_scales[e, s] = scales[:, j * C : (j + 1) * C]
 
         def gather_words(group, s):
-            words = slot_tile(group, s, U32, "slot_words", WORDS_AT)
+            words = work_tile(("words", group[0], s), C * len(group), U32)
             window = xw_first[:, 0, :] if s == 0 else xw_rest[:, s - 1, :]
             nc.vector.tensor_copy(out=words[:], in_=window.bitcast(U32).indirect(picks(group)))
             for j, e in enumerate(group):
                 slot_words[e, s] = words[:, j * C : (j + 1) * C]
 
         def w1_scale(e, s):
-            if e == 0:
-                return s1b[HOT_ROW:P, s, :]
+            if e == HOT:
+                return s1_late[HOT_ROW:P, s, :]
             if e > LATE:
-                return s1a[:, (e - 1 - LATE) * PASSES + s, :]
-            return s1b[:, (e - 1) * PASSES + s, :]
+                return s1_early[:, (e - 1 - LATE) * PASSES + s, :]
+            return s1_late[:, (e - 1) * PASSES + s, :]
 
-        rows = {}
-        pres = {}
+        sums = {}
+        h_rows = {}
         h_cols = {}
-        h_codes = keep.tile([P, E, C], U32, name="h_codes", align_bytes=64)
-        h_scales = keep.tile([P, E, C], U8, name="h_scales", align_bytes=64)
 
-        def first_layer(e):
-            pre = psum.tile([P, H], F32, name="pre%d" % (ORDER.index(e) % 3))
+        def first_product(e):
+            pre = psum.tile([P, H], F32, name="pre%d" % (ORDER.index(e) % PRE_BANKS))
             for s in range(PASSES):
                 nc.tensor.matmul_mx(
                     out=pre[:],
                     lhsT=slot_words[e, s].bitcast(FP8X4),
                     lhsT_scale=slot_scales[e, s],
-                    rhs=w1[e][:, s, :].bitcast(FP8X4 if e == 0 else FP4X4),
+                    rhs=w1[e][:, s, :].bitcast(FP8X4 if e == HOT else FP4X4),
                     rhs_scale=w1_scale(e, s),
                     start=(s == 0),
                     stop=(s == PASSES - 1),
                 )
-            pres[e] = pre
+            sums[e] = pre
 
         def activate(e):
-            pre = pres[e]
-            if e == ORDER[1]:
-                h_rows = stage.tile([P, H], BF16, name="h_rows%d" % e, align_bytes=64, offset=WORDS_AT[ORDER[2], 0])
-            else:
-                h_rows = keep.tile([P, H], BF16, name="h_rows%d" % e, align_bytes=64)
-            h_view = h_rows[:].rearrange("j (u p v) -> j u p v", u=2, v=2)
-            pre_view = pre[:].rearrange("j (p u v) -> j u p v", u=2, v=2)
-            if e == ORDER[-1]:
+            h_rows[e] = work_tile(("rows", e, 0), H, BF16)
+            h_view = h_rows[e][:].rearrange("j (u p v) -> j u p v", u=2, v=2)
+            pre_view = sums[e][:].rearrange("j (p u v) -> j u p v", u=2, v=2)
+            if e == HOT:
                 for u in range(2):
                     nc.scalar.activation(out=h_view[:, u, :, :], in_=pre_view[:, u, :, :], func=SILU)
             else:
                 nc.scalar.activation(out=h_view, in_=pre_view, func=SILU)
-            rows[e] = h_rows
 
-        def h_place(place):
-            first, count = (0, 4) if place < 4 else (place, 1)
+        def quantize_input(place):
+            first, count = (place - place % 2, 2) if place < 4 else (place, 1)
             if first not in h_cols:
-                shape = [P, count * 4 * C]
-                name = "h_cols%d" % first
-                h_cols[first] = keep.tile(shape, BF16, name=name, align_bytes=64)
-            return h_cols[first][:, (place - first) * 4 * C : (place - first + 1) * 4 * C]
+                h_cols[first] = keep.tile([P, count * H], BF16, name="h_cols%d" % first, align_bytes=ALIGN)
+            return h_cols[first][:, (place - first) * H : (place - first + 1) * H]
 
         def turn(e):
             place = ORDER.index(e)
-            turned = psum.tile([P, 2, C], F32, name=TURN_BANK[e])
-            pairs = rows[e][:].bitcast(F32)
+            turned = psum.tile([P, 2, C], F32, name="turned%d" % (place % TURN_BANKS))
+            pairs = h_rows[e][:].bitcast(F32)
             for u in range(2):
                 nc.tensor.transpose(turned[:, u, :], pairs[:, u * P : (u + 1) * P], ident[:])
-            copy = nc.vector.tensor_copy if e == ORDER[4] else nc.scalar.copy
+            copy = nc.vector.tensor_copy if e == FIFTH else nc.scalar.copy
             copy(
-                out=h_place(place).bitcast(F32).rearrange("p (j u) -> p j u", u=2),
+                out=quantize_input(place).bitcast(F32).rearrange("p (j u) -> p j u", u=2),
                 in_=turned[:].rearrange("p u j -> p j u"),
             )
 
-        codes_flat = h_codes[:].rearrange("p e c -> p (e c)")
-        scales_flat = h_scales[:].rearrange("p e c -> p (e c)")
-
         def quantize(first, count):
-            nc.vector.quantize_mx(
-                out=codes_flat[:, first * C : (first + count) * C].bitcast(FP8X4),
-                scales=scales_flat[:, first * C : (first + count) * C],
-                in_=h_cols[first][:],
-            )
+            columns = slice(first * C, (first + count) * C)
+            nc.vector.quantize_mx(out=h_codes[:, columns].bitcast(FP8X4), scales=h_scales[:, columns], in_=h_cols[first][:])
 
         def second_matmul(e, m, y):
-            place = ORDER.index(e)
-            if e == 0:
+            if e == HOT:
                 lhsT = w2h[:, m * 4 * P : (m + 1) * 4 * P].bitcast(FP8X4)
                 lhsT_scale = s2h[:, 0, m * P : (m + 1) * P]
             else:
                 lhsT = w2c[:, e - 1, m * 2 * P : (m + 1) * 2 * P].bitcast(FP4X4)
                 lhsT_scale = s2c[:, e - 1, m * P : (m + 1) * P]
+            columns = slice(ORDER.index(e) * C, (ORDER.index(e) + 1) * C)
             nc.tensor.matmul_mx(
                 out=y, lhsT=lhsT, lhsT_scale=lhsT_scale,
-                rhs=codes_flat[:, place * C : (place + 1) * C].bitcast(FP8X4),
-                rhs_scale=scales_flat[:, place * C : (place + 1) * C], start=True, stop=True,
+                rhs=h_codes[:, columns].bitcast(FP8X4), rhs_scale=h_scales[:, columns], start=True, stop=True,
             )
 
         out_rows = out.rearrange("(m p) j -> p m j", p=P)
 
-        def second_layer(group, copy):
+        def second_product(group, copy):
             n = len(group) * C
             y = psum.tile([P, 2, n], F32, name="y%d" % group[0])
             for j, e in enumerate(group):
@@ -212,55 +235,52 @@ def tile_moe_hot_s_mlp_silu_kernel(
             copy(out=result[:], in_=y[:])
             nc.sync.dma_start(out=out_rows[:, :, group[0] * C : group[0] * C + n], in_=result[:])
 
-        def last_second_layer(e):
-            for m in range(2):
+        def last_second_product(e):
+            for m, (copy, queue) in enumerate(((nc.scalar.copy, nc.scalar), (nc.vector.tensor_copy, nc.sync))):
                 y = psum.tile([P, C], F32, name="pre%d" % m)
                 second_matmul(e, m, y[:])
                 result = keep.tile([P, C], F32, name="result_last%d" % m)
-                if m == 0:
-                    nc.scalar.copy(out=result[:], in_=y[:])
-                    nc.scalar.dma_start(out=out_rows[:, m, e * C : (e + 1) * C], in_=result[:])
-                else:
-                    nc.vector.tensor_copy(out=result[:], in_=y[:])
-                    nc.sync.dma_start(out=out_rows[:, m, e * C : (e + 1) * C], in_=result[:])
+                copy(out=result[:], in_=y[:])
+                queue.dma_start(out=out_rows[:, m, e * C : (e + 1) * C], in_=result[:])
 
-        first_pair, second_pair = ORDER[0:2], ORDER[2:4]
         for s in range(PASSES):
-            gather_scales(first_pair, s)
+            gather_scales(FIRST_PAIR, s)
         for e in ORDER[0:4]:
             gather_words((e,), 0)
-        for group in (first_pair, second_pair, ORDER[4:5]):
-            for s in range(PASSES):
-                if (group[0], s) not in slot_words:
-                    gather_words(group, s)
-        first_layer(ORDER[0])
-        activate(ORDER[0])
-        first_layer(ORDER[1])
-        for group in (second_pair, ORDER[4:5]):
+        for pair in (FIRST_PAIR, SECOND_PAIR):
+            for s in range(1, PASSES):
+                gather_words(pair, s)
+        for s in range(PASSES):
+            gather_words((FIFTH,), s)
+        for e in FIRST_PAIR:
+            first_product(e)
+        activate(FIRST_PAIR[0])
+        for group in (SECOND_PAIR, (FIFTH,)):
             for s in range(PASSES):
                 gather_scales(group, s)
         for s in range(PASSES):
-            gather_scales(ORDER[5:6], s)
-            gather_words(ORDER[5:6], s)
-        turn(ORDER[0])
-        first_layer(ORDER[2])
-        activate(ORDER[1])
-        activate(ORDER[2])
-        first_layer(ORDER[3])
-        activate(ORDER[3])
-        turn(ORDER[1])
-        first_layer(ORDER[4])
-        activate(ORDER[4])
-        for e in second_pair:
+            gather_scales((HOT,), s)
+            gather_words((HOT,), s)
+        turn(FIRST_PAIR[0])
+        first_product(SECOND_PAIR[0])
+        activate(FIRST_PAIR[1])
+        first_product(SECOND_PAIR[1])
+        for e in SECOND_PAIR:
+            activate(e)
+        turn(FIRST_PAIR[1])
+        first_product(FIFTH)
+        activate(FIFTH)
+        for e in SECOND_PAIR:
             turn(e)
-        first_layer(ORDER[5])
-        activate(ORDER[5])
-        turn(ORDER[4])
-        quantize(0, 4)
+        first_product(HOT)
+        activate(HOT)
+        turn(FIFTH)
+        quantize(0, 2)
+        quantize(2, 2)
         quantize(4, 1)
-        second_layer(first_pair, nc.scalar.copy)
-        second_layer(second_pair, nc.vector.tensor_copy)
-        turn(ORDER[5])
+        second_product(FIRST_PAIR, nc.vector.tensor_copy)
+        turn(HOT)
         quantize(5, 1)
-        second_layer(ORDER[4:5], nc.vector.tensor_copy)
-        last_second_layer(ORDER[5])
+        second_product(SECOND_PAIR, nc.scalar.copy)
+        second_product((FIFTH,), nc.vector.tensor_copy)
+        last_second_product(HOT)

@@ -88,6 +88,7 @@ def tile_moe_hot_s_mlp_silu_kernel(
             for e in range(E)
         ]
         s1_early = keep.tile([P, (COLD - LATE) * PASSES, H], U8, name="s1_early", align_bytes=ALIGN)
+        s1h = keep.tile([P, PASSES, H], U8, name="s1h", align_bytes=ALIGN)
         s1_late = keep.tile([P, LATE * PASSES, H], U8, name="s1_late", align_bytes=ALIGN)
         w2h = keep.tile([P, N * 4], U8, name="w2h", align_bytes=ALIGN)
         w2c = keep.tile([P, COLD, N * 2], U8, name="w2c", align_bytes=ALIGN)
@@ -99,13 +100,13 @@ def tile_moe_hot_s_mlp_silu_kernel(
 
         for plane in (s2c, s2h):
             nc.gpsimd.memset(plane[:].bitcast(I32), 0)
-        for plane in (xs, s1_early, s1_late):
+        for plane in (xs, s1_early, s1_late, s1h):
             nc.vector.memset(plane[:].bitcast(I32), 0)
 
-        def load_scales(plane, rows, first_row=0):
+        def load_scales(plane, rows, first_row=0, queue=nc.sync):
             by_row = rows.bitcast(I32).rearrange("a (q r) c -> r q a c", r=4)
             for r in range(4):
-                nc.sync.dma_start(out=plane[first_row + r : P : 32, :, :].bitcast(I32), in_=by_row[r])
+                queue.dma_start(out=plane[first_row + r : P : 32, :, :].bitcast(I32), in_=by_row[r])
 
         def load_w1_cold(e):
             nc.sync.dma_start(out=w1[e][:].bitcast(I32), in_=w1c_words[e - 1].rearrange("s p b -> p s b").bitcast(I32))
@@ -115,23 +116,31 @@ def tile_moe_hot_s_mlp_silu_kernel(
         nc.sync.dma_start(out=xw_first[:], in_=x_rows[:, 0:1, :])
         load_scales(xs, x_scales)
         nc.sync.dma_start(out=xw_rest[:], in_=x_rows[:, 1:PASSES, :])
+
+        def load_w1_hot(first, last):
+            passes = w1h_words[0, first:last].rearrange("s p i d -> p s (i d)")
+            nc.sync.dma_start(out=w1[HOT][:, first:last, :].bitcast(I32), in_=passes.bitcast(I32))
+
+        def load_w2_cold(matrices):
+            rows = w2c_words.rearrange("f s p b -> p (f s) b").bitcast(I32)
+            nc.sync.dma_start(out=w2c[:, matrices, :].bitcast(I32), in_=rows[:, matrices, :])
+
         load_scales(s1_early, w1c_scales[LATE:COLD].rearrange("f s b i -> (f s) b i"))
-        load_w1_cold(FIRST_PAIR[0])
+        load_w1_cold(ORDER[0])
         load_scales(s2c, w2c_scales.rearrange("f s b n -> (f s) b n"))
-        load_w1_cold(FIRST_PAIR[1])
-        load_scales(s1_late, w1c_scales[0:LATE].rearrange("f s b i -> (f s) b i"))
-        load_w1_cold(SECOND_PAIR[0])
-        load_scales(s1_late[:, 0:PASSES, :], w1h_scales[0], HOT_ROW)
-        load_w1_cold(SECOND_PAIR[1])
-        load_w1_cold(FIFTH)
-        for s in range(PASSES):
-            hot_pass = w1h_words[0, s].rearrange("p i d -> p (i d)")
-            nc.sync.dma_start(out=w1[HOT][:, s, :].bitcast(I32), in_=hot_pass.bitcast(I32))
-        w2c_rows = w2c_words.rearrange("f s p b -> p (f s) b").bitcast(I32)
-        for matrices in (slice(LATE, COLD), slice(0, LATE)):
-            nc.sync.dma_start(out=w2c[:, matrices, :].bitcast(I32), in_=w2c_rows[:, matrices, :])
+        load_w1_cold(ORDER[1])
+        load_w1_cold(ORDER[2])
+        load_w1_cold(ORDER[3])
+        load_w1_cold(ORDER[4])
+        load_w1_hot(0, 1)
+        load_w1_hot(1, 2)
+        load_w1_hot(2, 3)
+        load_w2_cold(slice(LATE, COLD))
+        load_w2_cold(slice(0, LATE))
         nc.sync.dma_start(out=w2h[:].bitcast(I32), in_=w2h_words[0, 0].rearrange("p n d -> p (n d)").bitcast(I32))
         load_scales(s2h, w2h_scales[0])
+        load_scales(s1_late, w1c_scales[0:LATE].rearrange("f s b i -> (f s) b i"), queue=nc.gpsimd)
+        load_scales(s1h, w1h_scales[0], HOT_ROW, nc.gpsimd)
         make_identity(nc, ident[:])
 
         slot_words = {}
@@ -155,7 +164,7 @@ def tile_moe_hot_s_mlp_silu_kernel(
 
         def w1_scale(e, s):
             if e == HOT:
-                return s1_late[HOT_ROW:P, s, :]
+                return s1h[HOT_ROW:P, s, :]
             if e > LATE:
                 return s1_early[:, (e - 1 - LATE) * PASSES + s, :]
             return s1_late[:, (e - 1) * PASSES + s, :]

@@ -24,42 +24,21 @@ ORDER = (4, 5, 2, 3, 1, HOT)
 FIRST_PAIR, SECOND_PAIR, FIFTH = ORDER[0:2], ORDER[2:4], ORDER[4]
 LATE = 3
 HOT_ROW = 4
-PRE_BANKS = 3
+PRE_BANKS = 4
 TURN_BANKS = 2
 ALIGN = 64
 
-FOLLOWS = (
-    (("words", 4, 0), (("scales", 2, 1), ("scales", 2, 0), ("scales", 2, 2))),
-    (("words", 5, 0), (("rows", 4, 0), ("scales", 1, 0), ("scales", 1, 1), ("scales", 1, 2))),
-    (("words", 2, 0), (("rows", 5, 0),)),
-    (("words", 3, 0), (("rows", 2, 0),)),
-    (
-        ("words", 4, 2),
-        (("words", 0, 0), ("scales", 0, 0), ("scales", 0, 1), ("scales", 0, 2), ("words", 0, 1), ("words", 0, 2)),
-    ),
-)
-
-
-def tile_bytes(kind, expert, s):
-    if kind == "rows":
-        return 2 * H
-    if kind == "scales":
-        return (2 if expert == SECOND_PAIR[0] else 1) * C
-    return (2 if expert == FIRST_PAIR[0] and s > 0 else 1) * 4 * C
-
-
-def shared_places():
-    places = {}
-    start = 0
-    for host, guests in FOLLOWS:
-        places[host] = start + tile_bytes(*guests[0]) - ALIGN
-        host_end = places[host] + tile_bytes(*host)
-        for guest in guests:
-            assert start < host_end
-            places[guest] = start
-            start += tile_bytes(*guest)
-        start = max(start, host_end)
-    return places
+PARKED = 8
+WORDS = 4 * C
+PLACES = {
+    ("words", 2, 0): 4 * WORDS,
+    ("words", 4, 0): 6 * WORDS - ALIGN,
+    ("scales", 2, 1): 6 * WORDS,
+    ("words", 1, 0): 7 * WORDS - 2 * ALIGN,
+    ("scales", 0, 1): 10 * WORDS,
+    ("words", 5, 0): 10 * WORDS + 2 * C - ALIGN,
+    ("words", 0, 0): 11 * WORDS + 2 * C - 2 * ALIGN,
+}
 
 
 def tile_moe_hot_s_mlp_silu_kernel(
@@ -67,7 +46,7 @@ def tile_moe_hot_s_mlp_silu_kernel(
     w1c_words, w1c_scales, w2c_words, w2c_scales, offs, out,
 ):
     nc = tc.nc
-    places = shared_places()
+    places = PLACES
     with ExitStack() as ctx:
         keep = ctx.enter_context(tc.tile_pool(name="keep", bufs=1))
         shared = ctx.enter_context(tc.tile_pool(name="shared", bufs=1))
@@ -82,7 +61,7 @@ def tile_moe_hot_s_mlp_silu_kernel(
         offsets = keep.tile([P, E * C // 16], U16, name="offsets")
         xw_first = keep.tile([P, 1, T], I32, name="xw_first", align_bytes=ALIGN)
         xw_rest = keep.tile([P, PASSES - 1, T], I32, name="xw_rest", align_bytes=ALIGN)
-        xs = keep.tile([P, PASSES, T], U8, name="xs", align_bytes=ALIGN)
+        xs = keep.tile([P, PASSES - 1, T], U8, name="xs", align_bytes=ALIGN)
         w1 = [
             keep.tile([P, PASSES, H * (4 if e == HOT else 2)], U8, name="w1_%d" % e, align_bytes=ALIGN)
             for e in range(E)
@@ -98,7 +77,9 @@ def tile_moe_hot_s_mlp_silu_kernel(
         h_codes = keep.tile([P, E * C], U32, name="h_codes", align_bytes=ALIGN)
         h_scales = keep.tile([P, E * C], U8, name="h_scales", align_bytes=ALIGN)
 
-        for plane in (s2c, s2h):
+        picked = keep.tile([P, E * C], U8, name="picked", align_bytes=ALIGN)
+        moved = keep.tile([P, E * C], U8, name="moved", align_bytes=ALIGN)
+        for plane in (s2c, moved, s2h):
             nc.gpsimd.memset(plane[:].bitcast(I32), 0)
         for plane in (xs, s1_early, s1_late, s1h):
             nc.vector.memset(plane[:].bitcast(I32), 0)
@@ -114,7 +95,8 @@ def tile_moe_hot_s_mlp_silu_kernel(
         x_rows = x_words.rearrange("s p t d -> p s (t d)").bitcast(I32)
         nc.sync.dma_start(offsets[:], offs)
         nc.sync.dma_start(out=xw_first[:], in_=x_rows[:, 0:1, :])
-        load_scales(xs, x_scales)
+        nc.sync.dma_start(out=xs[PARKED : PARKED + 16, 0, :].bitcast(I32), in_=x_scales[PASSES - 1].bitcast(I32))
+        load_scales(xs, x_scales[0 : PASSES - 1])
         nc.sync.dma_start(out=xw_rest[:], in_=x_rows[:, 1:PASSES, :])
 
         def load_w1_hot(first, last):
@@ -129,16 +111,6 @@ def tile_moe_hot_s_mlp_silu_kernel(
         load_w1_cold(ORDER[0])
         load_scales(s2c, w2c_scales.rearrange("f s b n -> (f s) b n"))
         load_w1_cold(ORDER[1])
-        load_w1_cold(ORDER[2])
-        load_w1_cold(ORDER[3])
-        load_w1_cold(ORDER[4])
-        load_w1_hot(0, 1)
-        load_w1_hot(1, 2)
-        load_w1_hot(2, 3)
-        load_w2_cold(slice(LATE, COLD))
-        load_w2_cold(slice(0, LATE))
-        nc.sync.dma_start(out=w2h[:].bitcast(I32), in_=w2h_words[0, 0].rearrange("p n d -> p (n d)").bitcast(I32))
-        load_scales(s2h, w2h_scales[0])
         load_scales(s1_late, w1c_scales[0:LATE].rearrange("f s b i -> (f s) b i"), queue=nc.gpsimd)
         load_scales(s1h, w1h_scales[0], HOT_ROW, nc.gpsimd)
         make_identity(nc, ident[:])
@@ -149,16 +121,14 @@ def tile_moe_hot_s_mlp_silu_kernel(
         def picks(group):
             return offsets[:, group[0] * C // 16 : (group[-1] + 1) * C // 16]
 
-        def gather_scales(group, s):
-            scales = work_tile(("scales", group[0], s), C * len(group), U8)
-            nc.vector.tensor_copy(out=scales[:], in_=xs[:, s, :].indirect(picks(group)))
+        def gather_scales(group, s, scales):
+            nc.vector.tensor_copy(out=scales, in_=xs[:, s, :].indirect(picks(group)))
             for j, e in enumerate(group):
                 slot_scales[e, s] = scales[:, j * C : (j + 1) * C]
 
-        def gather_words(group, s):
-            words = work_tile(("words", group[0], s), C * len(group), U32)
+        def gather_words(group, s, words):
             window = xw_first[:, 0, :] if s == 0 else xw_rest[:, s - 1, :]
-            nc.vector.tensor_copy(out=words[:], in_=window.bitcast(U32).indirect(picks(group)))
+            nc.vector.tensor_copy(out=words, in_=window.bitcast(U32).indirect(picks(group)))
             for j, e in enumerate(group):
                 slot_words[e, s] = words[:, j * C : (j + 1) * C]
 
@@ -197,22 +167,17 @@ def tile_moe_hot_s_mlp_silu_kernel(
             else:
                 nc.scalar.activation(out=h_view, in_=pre_view, func=SILU)
 
-        def quantize_input(place):
-            first, count = (place - place % 2, 2) if place < 4 else (place, 1)
-            if first not in h_cols:
-                h_cols[first] = keep.tile([P, count * H], BF16, name="h_cols%d" % first, align_bytes=ALIGN)
-            return h_cols[first][:, (place - first) * H : (place - first + 1) * H]
-
-        def turn(e):
-            place = ORDER.index(e)
-            turned = psum.tile([P, 2, C], F32, name="turned%d" % (place % TURN_BANKS))
-            pairs = h_rows[e][:].bitcast(F32)
-            for u in range(2):
-                nc.tensor.transpose(turned[:, u, :], pairs[:, u * P : (u + 1) * P], ident[:])
-            copy = nc.vector.tensor_copy if e == FIFTH else nc.scalar.copy
+        def turn(group, bank, copy):
+            turned = psum.tile([P, len(group), 2, C], F32, name=bank)
+            for j, e in enumerate(group):
+                pairs = h_rows[e][:].bitcast(F32)
+                for u in range(2):
+                    nc.tensor.transpose(turned[:, j, u, :], pairs[:, u * P : (u + 1) * P], ident[:])
+            place = ORDER.index(group[0])
+            h_cols[place] = keep.tile([P, len(group) * H], BF16, name="h_cols%d" % place, align_bytes=ALIGN)
             copy(
-                out=quantize_input(place).bitcast(F32).rearrange("p (j u) -> p j u", u=2),
-                in_=turned[:].rearrange("p u j -> p j u"),
+                out=h_cols[place][:].bitcast(F32).rearrange("p (x j u) -> p x j u", x=len(group), u=2),
+                in_=turned[:].rearrange("p x u j -> p x j u"),
             )
 
         def quantize(first, count):
@@ -234,9 +199,9 @@ def tile_moe_hot_s_mlp_silu_kernel(
 
         out_rows = out.rearrange("(m p) j -> p m j", p=P)
 
-        def second_product(group, copy):
+        def second_product(group, bank, copy):
             n = len(group) * C
-            y = psum.tile([P, 2, n], F32, name="y%d" % group[0])
+            y = psum.tile([P, 2, n], F32, name=bank)
             for j, e in enumerate(group):
                 for m in range(2):
                     second_matmul(e, m, y[:, m, j * C : (j + 1) * C])
@@ -246,50 +211,64 @@ def tile_moe_hot_s_mlp_silu_kernel(
 
         def last_second_product(e):
             for m, (copy, queue) in enumerate(((nc.scalar.copy, nc.scalar), (nc.vector.tensor_copy, nc.sync))):
-                y = psum.tile([P, C], F32, name="pre%d" % m)
+                y = psum.tile([P, C], F32, name=("pre1", "turned0")[m])
                 second_matmul(e, m, y[:])
                 result = keep.tile([P, C], F32, name="result_last%d" % m)
                 copy(out=result[:], in_=y[:])
                 queue.dma_start(out=out_rows[:, m, e * C : (e + 1) * C], in_=result[:])
 
+        for e in FIRST_PAIR:
+            gather_words((e,), 0, work_tile(("words", e, 0), C, U32)[:])
+        for half in (range(E // 2, E), range(E // 2)):
+            gather_scales(half, 0, picked[:, half[0] * C : (half[-1] + 1) * C])
+        for r in range(4):
+            nc.sync.dma_start(out=moved[r:P:32, :].bitcast(I32), in_=picked[PARKED + r : PARKED + 16 : 4, :].bitcast(I32))
+        for e in range(E):
+            slot_scales[e, PASSES - 1] = moved[:, e * C : (e + 1) * C]
+        load_w1_cold(ORDER[2])
+        load_w1_cold(ORDER[3])
+        load_w1_cold(ORDER[4])
         for s in range(PASSES):
-            gather_scales(FIRST_PAIR, s)
-        for e in ORDER[0:4]:
-            gather_words((e,), 0)
+            load_w1_hot(s, s + 1)
+        load_w2_cold(slice(LATE, COLD))
+        load_w2_cold(slice(0, LATE))
+        nc.sync.dma_start(out=w2h[:].bitcast(I32), in_=w2h_words[0, 0].rearrange("p n d -> p (n d)").bitcast(I32))
+        load_scales(s2h, w2h_scales[0])
+        gather_scales(FIRST_PAIR, 1, work_tile(("scales", 4, 1), 2 * C, U8)[:])
         for pair in (FIRST_PAIR, SECOND_PAIR):
             for s in range(1, PASSES):
-                gather_words(pair, s)
-        for s in range(PASSES):
-            gather_words((FIFTH,), s)
+                gather_words(pair, s, work_tile(("words", pair[0], s), 2 * C, U32)[:])
         for e in FIRST_PAIR:
             first_product(e)
-        activate(FIRST_PAIR[0])
-        for group in (SECOND_PAIR, (FIFTH,)):
-            for s in range(PASSES):
-                gather_scales(group, s)
-        for s in range(PASSES):
-            gather_scales((HOT,), s)
-            gather_words((HOT,), s)
-        turn(FIRST_PAIR[0])
-        first_product(SECOND_PAIR[0])
-        activate(FIRST_PAIR[1])
-        first_product(SECOND_PAIR[1])
-        for e in SECOND_PAIR:
             activate(e)
-        turn(FIRST_PAIR[1])
+
+        def gather_all_words(group):
+            n = len(group) * C
+            words = work_tile(("words", group[0], 0), PASSES * n, U32)
+            for s in range(PASSES):
+                gather_words(group, s, words[:, s * n : (s + 1) * n])
+
+        gather_words(SECOND_PAIR, 0, work_tile(("words", SECOND_PAIR[0], 0), 2 * C, U32)[:])
+        gather_scales(SECOND_PAIR, 1, work_tile(("scales", SECOND_PAIR[0], 1), 2 * C, U8)[:])
+        gather_all_words((FIFTH,))
+        gather_scales((HOT, FIFTH), 1, work_tile(("scales", HOT, 1), 2 * C, U8)[:])
+        gather_all_words((HOT,))
+        for e in SECOND_PAIR:
+            first_product(e)
+            activate(e)
+        turn(FIRST_PAIR, "pre2", nc.vector.tensor_copy)
+        quantize(0, 2)
         first_product(FIFTH)
         activate(FIFTH)
-        for e in SECOND_PAIR:
-            turn(e)
+        turn(SECOND_PAIR, "turned0", nc.vector.tensor_copy)
+        quantize(2, 2)
         first_product(HOT)
         activate(HOT)
-        turn(FIFTH)
-        quantize(0, 2)
-        quantize(2, 2)
+        turn((FIFTH,), "turned1", nc.vector.tensor_copy)
         quantize(4, 1)
-        second_product(FIRST_PAIR, nc.vector.tensor_copy)
-        turn(HOT)
+        second_product(FIRST_PAIR, "pre3", nc.vector.tensor_copy)
+        turn((HOT,), "turned2", nc.scalar.copy)
         quantize(5, 1)
-        second_product(SECOND_PAIR, nc.scalar.copy)
-        second_product((FIFTH,), nc.vector.tensor_copy)
+        second_product(SECOND_PAIR, "pre0", nc.scalar.copy)
+        second_product((FIFTH,), "pre2", nc.vector.tensor_copy)
         last_second_product(HOT)

@@ -31,13 +31,16 @@ ALIGN = 64
 PARKED = 8
 WORDS = 4 * C
 PLACES = {
-    ("words", 2, 0): 4 * WORDS,
-    ("words", 4, 0): 6 * WORDS - ALIGN,
-    ("scales", 2, 1): 6 * WORDS,
-    ("words", 1, 0): 7 * WORDS - 2 * ALIGN,
-    ("scales", 0, 1): 10 * WORDS,
-    ("words", 5, 0): 10 * WORDS + 2 * C - ALIGN,
-    ("words", 0, 0): 11 * WORDS + 2 * C - 2 * ALIGN,
+    ("words", 2, 0): 0,
+    ("words", 4, 0): 2 * WORDS - ALIGN,
+    ("scales", 2, 1): 2 * WORDS,
+    ("words", 1, 0): 3 * WORDS - 2 * ALIGN,
+    ("rows", 3, 0): 4 * WORDS - 3 * ALIGN,
+    ("scales", 0, 1): 6 * WORDS,
+    ("words", 5, 0): 6 * WORDS + 2 * C - ALIGN,
+    ("words", 1, 1): 8 * WORDS,
+    ("words", 4, 1): 10 * WORDS - ALIGN,
+    ("words", 0, 0): 12 * WORDS - 2 * ALIGN,
 }
 
 
@@ -109,7 +112,6 @@ def tile_moe_hot_s_mlp_silu_kernel(
 
         load_scales(s1_early, w1c_scales[LATE:COLD].rearrange("f s b i -> (f s) b i"))
         load_w1_cold(ORDER[0])
-        load_scales(s2c, w2c_scales.rearrange("f s b n -> (f s) b n"))
         load_w1_cold(ORDER[1])
         load_scales(s1_late, w1c_scales[0:LATE].rearrange("f s b i -> (f s) b i"), queue=nc.gpsimd)
         load_scales(s1h, w1h_scales[0], HOT_ROW, nc.gpsimd)
@@ -211,7 +213,7 @@ def tile_moe_hot_s_mlp_silu_kernel(
 
         def last_second_product(e):
             for m, (copy, queue) in enumerate(((nc.scalar.copy, nc.scalar), (nc.vector.tensor_copy, nc.sync))):
-                y = psum.tile([P, C], F32, name=("pre1", "turned0")[m])
+                y = psum.tile([P, C], F32, name=("pre1", "pre3")[m])
                 second_matmul(e, m, y[:])
                 result = keep.tile([P, C], F32, name="result_last%d" % m)
                 copy(out=result[:], in_=y[:])
@@ -227,6 +229,7 @@ def tile_moe_hot_s_mlp_silu_kernel(
             slot_scales[e, PASSES - 1] = moved[:, e * C : (e + 1) * C]
         load_w1_cold(ORDER[2])
         load_w1_cold(ORDER[3])
+        load_scales(s2c, w2c_scales.rearrange("f s b n -> (f s) b n"))
         load_w1_cold(ORDER[4])
         for s in range(PASSES):
             load_w1_hot(s, s + 1)
@@ -242,33 +245,34 @@ def tile_moe_hot_s_mlp_silu_kernel(
             first_product(e)
             activate(e)
 
-        def gather_all_words(group):
-            n = len(group) * C
-            words = work_tile(("words", group[0], 0), PASSES * n, U32)
-            for s in range(PASSES):
-                gather_words(group, s, words[:, s * n : (s + 1) * n])
+        def gather_passes(e, first):
+            words = work_tile(("words", e, first), (PASSES - first) * C, U32)
+            for s in range(first, PASSES):
+                gather_words((e,), s, words[:, (s - first) * C : (s - first + 1) * C])
 
         gather_words(SECOND_PAIR, 0, work_tile(("words", SECOND_PAIR[0], 0), 2 * C, U32)[:])
         gather_scales(SECOND_PAIR, 1, work_tile(("scales", SECOND_PAIR[0], 1), 2 * C, U8)[:])
-        gather_all_words((FIFTH,))
+        gather_words((FIFTH,), 0, work_tile(("words", FIFTH, 0), C, U32)[:])
         gather_scales((HOT, FIFTH), 1, work_tile(("scales", HOT, 1), 2 * C, U8)[:])
-        gather_all_words((HOT,))
-        for e in SECOND_PAIR:
-            first_product(e)
-            activate(e)
-        turn(FIRST_PAIR, "pre2", nc.vector.tensor_copy)
+        gather_passes(FIFTH, 1)
+        gather_passes(HOT, 0)
+        first_product(SECOND_PAIR[0])
+        activate(SECOND_PAIR[0])
+        turn(FIRST_PAIR, "turned0", nc.vector.tensor_copy)
         quantize(0, 2)
+        first_product(SECOND_PAIR[1])
         first_product(FIFTH)
+        activate(SECOND_PAIR[1])
         activate(FIFTH)
-        turn(SECOND_PAIR, "turned0", nc.vector.tensor_copy)
+        turn(SECOND_PAIR, "pre3", nc.vector.tensor_copy)
         quantize(2, 2)
         first_product(HOT)
         activate(HOT)
         turn((FIFTH,), "turned1", nc.vector.tensor_copy)
         quantize(4, 1)
-        second_product(FIRST_PAIR, "pre3", nc.vector.tensor_copy)
+        second_product(FIRST_PAIR, "pre2", nc.vector.tensor_copy)
         turn((HOT,), "turned2", nc.scalar.copy)
         quantize(5, 1)
         second_product(SECOND_PAIR, "pre0", nc.scalar.copy)
-        second_product((FIFTH,), "pre2", nc.vector.tensor_copy)
+        second_product((FIFTH,), "turned0", nc.vector.tensor_copy)
         last_second_product(HOT)

@@ -24,24 +24,9 @@ ORDER = (4, 5, 2, 3, 1, HOT)
 FIRST_PAIR, SECOND_PAIR, FIFTH = ORDER[0:2], ORDER[2:4], ORDER[4]
 LATE = 3
 HOT_ROW = 4
-PRE_BANKS = 4
-TURN_BANKS = 2
 ALIGN = 64
 
 PARKED = 8
-WORDS = 4 * C
-PLACES = {
-    ("words", 2, 0): 0,
-    ("words", 4, 0): 2 * WORDS - ALIGN,
-    ("scales", 2, 1): 2 * WORDS,
-    ("words", 1, 0): 3 * WORDS - 2 * ALIGN,
-    ("rows", 3, 0): 4 * WORDS - 3 * ALIGN,
-    ("scales", 0, 1): 6 * WORDS,
-    ("words", 5, 0): 6 * WORDS + 2 * C - ALIGN,
-    ("words", 1, 1): 8 * WORDS,
-    ("words", 4, 1): 10 * WORDS - ALIGN,
-    ("words", 0, 0): 12 * WORDS - 2 * ALIGN,
-}
 
 
 def tile_moe_hot_s_mlp_silu_kernel(
@@ -49,17 +34,10 @@ def tile_moe_hot_s_mlp_silu_kernel(
     w1c_words, w1c_scales, w2c_words, w2c_scales, offs, out,
 ):
     nc = tc.nc
-    places = PLACES
     with ExitStack() as ctx:
         keep = ctx.enter_context(tc.tile_pool(name="keep", bufs=1))
         shared = ctx.enter_context(tc.tile_pool(name="shared", bufs=1))
         psum = ctx.enter_context(tc.psum_pool(name="psum", bufs=1))
-
-        def work_tile(key, columns, dtype):
-            name = "%s%d_%d" % key
-            if key in places:
-                return shared.tile([P, columns], dtype, name=name, align_bytes=ALIGN, offset=places[key])
-            return keep.tile([P, columns], dtype, name=name, align_bytes=ALIGN)
 
         offsets = keep.tile([P, E * C // 16], U16, name="offsets")
         xw_first = keep.tile([P, 1, T], I32, name="xw_first", align_bytes=ALIGN)
@@ -79,13 +57,17 @@ def tile_moe_hot_s_mlp_silu_kernel(
         ident = keep.tile([P, P], F32, name="ident")
         h_codes = keep.tile([P, E * C], U32, name="h_codes", align_bytes=ALIGN)
         h_scales = keep.tile([P, E * C], U8, name="h_scales", align_bytes=ALIGN)
-
         picked = keep.tile([P, E * C], U8, name="picked", align_bytes=ALIGN)
+        picked1 = keep.tile([P, E * C], U8, name="picked1", align_bytes=ALIGN)
         moved = keep.tile([P, E * C], U8, name="moved", align_bytes=ALIGN)
+        words = [keep.tile([P, E * C], U32, name="words%d" % s, align_bytes=ALIGN) for s in range(PASSES)]
+        third_words = shared.tile([P, C], U32, name="third_words", align_bytes=ALIGN, offset=0)
+
         for plane in (s2c, moved, s2h):
             nc.gpsimd.memset(plane[:].bitcast(I32), 0)
         for plane in (xs, s1_early, s1_late, s1h):
             nc.vector.memset(plane[:].bitcast(I32), 0)
+        make_identity(nc, ident[:])
 
         def load_scales(plane, rows, first_row=0, queue=nc.sync):
             by_row = rows.bitcast(I32).rearrange("a (q r) c -> r q a c", r=4)
@@ -95,13 +77,6 @@ def tile_moe_hot_s_mlp_silu_kernel(
         def load_w1_cold(e):
             nc.sync.dma_start(out=w1[e][:].bitcast(I32), in_=w1c_words[e - 1].rearrange("s p b -> p s b").bitcast(I32))
 
-        x_rows = x_words.rearrange("s p t d -> p s (t d)").bitcast(I32)
-        nc.sync.dma_start(offsets[:], offs)
-        nc.sync.dma_start(out=xw_first[:], in_=x_rows[:, 0:1, :])
-        nc.sync.dma_start(out=xs[PARKED : PARKED + 16, 0, :].bitcast(I32), in_=x_scales[PASSES - 1].bitcast(I32))
-        load_scales(xs, x_scales[0 : PASSES - 1])
-        nc.sync.dma_start(out=xw_rest[:], in_=x_rows[:, 1:PASSES, :])
-
         def load_w1_hot(first, last):
             passes = w1h_words[0, first:last].rearrange("s p i d -> p s (i d)")
             nc.sync.dma_start(out=w1[HOT][:, first:last, :].bitcast(I32), in_=passes.bitcast(I32))
@@ -110,29 +85,47 @@ def tile_moe_hot_s_mlp_silu_kernel(
             rows = w2c_words.rearrange("f s p b -> p (f s) b").bitcast(I32)
             nc.sync.dma_start(out=w2c[:, matrices, :].bitcast(I32), in_=rows[:, matrices, :])
 
-        load_scales(s1_early, w1c_scales[LATE:COLD].rearrange("f s b i -> (f s) b i"))
+        x_rows = x_words.rearrange("s p t d -> p s (t d)").bitcast(I32)
+        nc.sync.dma_start(offsets[:], offs)
+        nc.sync.dma_start(out=xw_first[:], in_=x_rows[:, 0:1, :])
+        nc.sync.dma_start(out=xs[PARKED : PARKED + 16, 0, :].bitcast(I32), in_=x_scales[PASSES - 1].bitcast(I32))
+        load_scales(xs, x_scales[0 : PASSES - 1])
+        nc.sync.dma_start(out=xw_rest[:], in_=x_rows[:, 1:PASSES, :])
         load_w1_cold(ORDER[0])
+        load_scales(s2c, w2c_scales.rearrange("f s b n -> (f s) b n"))
         load_w1_cold(ORDER[1])
+        load_scales(s1_early, w1c_scales[LATE:COLD].rearrange("f s b i -> (f s) b i"), queue=nc.gpsimd)
         load_scales(s1_late, w1c_scales[0:LATE].rearrange("f s b i -> (f s) b i"), queue=nc.gpsimd)
         load_scales(s1h, w1h_scales[0], HOT_ROW, nc.gpsimd)
-        make_identity(nc, ident[:])
 
-        slot_words = {}
-        slot_scales = {}
+        def gather(dst, window, first, count):
+            columns = slice(first * C, (first + count) * C)
+            nc.vector.tensor_copy(out=dst[:, columns], in_=window.indirect(offsets[:, first * C // 16 : (first + count) * C // 16]))
 
-        def picks(group):
-            return offsets[:, group[0] * C // 16 : (group[-1] + 1) * C // 16]
+        HALF = E // 2
+        gather(words[0], xw_first[:, 0, :].bitcast(U32), HALF, HALF)
+        nc.vector.tensor_copy(out=third_words[:], in_=xw_first[:, 0, :].bitcast(U32).indirect(offsets[:, 2 * C // 16 : 3 * C // 16]))
+        gather(words[0], xw_first[:, 0, :].bitcast(U32), 0, 2)
+        for first in (HALF, 0):
+            gather(picked, xs[:, 0, :], first, HALF)
+        for r in range(4):
+            nc.sync.dma_start(out=moved[r:P:32, :].bitcast(I32), in_=picked[PARKED + r : PARKED + 16 : 4, :].bitcast(I32))
+        load_w1_cold(ORDER[2])
+        load_w1_cold(ORDER[3])
+        load_w1_cold(ORDER[4])
+        for s in range(PASSES):
+            load_w1_hot(s, s + 1)
+        load_w2_cold(slice(1, COLD))
+        load_w2_cold(slice(0, 1))
+        nc.sync.dma_start(out=w2h[:].bitcast(I32), in_=w2h_words[0, 0].rearrange("p n d -> p (n d)").bitcast(I32))
+        load_scales(s2h, w2h_scales[0])
+        for first in (HALF, 0):
+            gather(picked1, xs[:, 1, :], first, HALF)
+        for first in (4, 2, 0):
+            for s in range(1, PASSES):
+                gather(words[s], xw_rest[:, s - 1, :].bitcast(U32), first, 2)
 
-        def gather_scales(group, s, scales):
-            nc.vector.tensor_copy(out=scales, in_=xs[:, s, :].indirect(picks(group)))
-            for j, e in enumerate(group):
-                slot_scales[e, s] = scales[:, j * C : (j + 1) * C]
-
-        def gather_words(group, s, words):
-            window = xw_first[:, 0, :] if s == 0 else xw_rest[:, s - 1, :]
-            nc.vector.tensor_copy(out=words, in_=window.bitcast(U32).indirect(picks(group)))
-            for j, e in enumerate(group):
-                slot_words[e, s] = words[:, j * C : (j + 1) * C]
+        slot_scales = (picked, picked1, moved)
 
         def w1_scale(e, s):
             if e == HOT:
@@ -145,13 +138,14 @@ def tile_moe_hot_s_mlp_silu_kernel(
         h_rows = {}
         h_cols = {}
 
-        def first_product(e):
-            pre = psum.tile([P, H], F32, name="pre%d" % (ORDER.index(e) % PRE_BANKS))
+        def first_product(e, bank):
+            pre = psum.tile([P, H], F32, name=bank)
+            slots = slice(e * C, (e + 1) * C)
             for s in range(PASSES):
                 nc.tensor.matmul_mx(
                     out=pre[:],
-                    lhsT=slot_words[e, s].bitcast(FP8X4),
-                    lhsT_scale=slot_scales[e, s],
+                    lhsT=(third_words[:] if (e, s) == (2, 0) else words[s][:, slots]).bitcast(FP8X4),
+                    lhsT_scale=slot_scales[s][:, slots],
                     rhs=w1[e][:, s, :].bitcast(FP8X4 if e == HOT else FP4X4),
                     rhs_scale=w1_scale(e, s),
                     start=(s == 0),
@@ -160,7 +154,10 @@ def tile_moe_hot_s_mlp_silu_kernel(
             sums[e] = pre
 
         def activate(e):
-            h_rows[e] = work_tile(("rows", e, 0), H, BF16)
+            if e == FIRST_PAIR[1]:
+                h_rows[e] = shared.tile([P, H], BF16, name="rows%d" % e, align_bytes=ALIGN, offset=0)
+            else:
+                h_rows[e] = keep.tile([P, H], BF16, name="rows%d" % e, align_bytes=ALIGN)
             h_view = h_rows[e][:].rearrange("j (u p v) -> j u p v", u=2, v=2)
             pre_view = sums[e][:].rearrange("j (p u v) -> j u p v", u=2, v=2)
             if e == HOT:
@@ -211,68 +208,35 @@ def tile_moe_hot_s_mlp_silu_kernel(
             copy(out=result[:], in_=y[:])
             nc.sync.dma_start(out=out_rows[:, :, group[0] * C : group[0] * C + n], in_=result[:])
 
-        def last_second_product(e):
+        def last_second_product(e, banks):
             for m, (copy, queue) in enumerate(((nc.scalar.copy, nc.scalar), (nc.vector.tensor_copy, nc.sync))):
-                y = psum.tile([P, C], F32, name=("pre1", "pre3")[m])
+                y = psum.tile([P, C], F32, name=banks[m])
                 second_matmul(e, m, y[:])
                 result = keep.tile([P, C], F32, name="result_last%d" % m)
                 copy(out=result[:], in_=y[:])
                 queue.dma_start(out=out_rows[:, m, e * C : (e + 1) * C], in_=result[:])
 
-        for e in FIRST_PAIR:
-            gather_words((e,), 0, work_tile(("words", e, 0), C, U32)[:])
-        for half in (range(E // 2, E), range(E // 2)):
-            gather_scales(half, 0, picked[:, half[0] * C : (half[-1] + 1) * C])
-        for r in range(4):
-            nc.sync.dma_start(out=moved[r:P:32, :].bitcast(I32), in_=picked[PARKED + r : PARKED + 16 : 4, :].bitcast(I32))
-        for e in range(E):
-            slot_scales[e, PASSES - 1] = moved[:, e * C : (e + 1) * C]
-        load_w1_cold(ORDER[2])
-        load_w1_cold(ORDER[3])
-        load_scales(s2c, w2c_scales.rearrange("f s b n -> (f s) b n"))
-        load_w1_cold(ORDER[4])
-        for s in range(PASSES):
-            load_w1_hot(s, s + 1)
-        load_w2_cold(slice(LATE, COLD))
-        load_w2_cold(slice(0, LATE))
-        nc.sync.dma_start(out=w2h[:].bitcast(I32), in_=w2h_words[0, 0].rearrange("p n d -> p (n d)").bitcast(I32))
-        load_scales(s2h, w2h_scales[0])
-        gather_scales(FIRST_PAIR, 1, work_tile(("scales", 4, 1), 2 * C, U8)[:])
-        for pair in (FIRST_PAIR, SECOND_PAIR):
-            for s in range(1, PASSES):
-                gather_words(pair, s, work_tile(("words", pair[0], s), 2 * C, U32)[:])
-        for e in FIRST_PAIR:
-            first_product(e)
-            activate(e)
-
-        def gather_passes(e, first):
-            words = work_tile(("words", e, first), (PASSES - first) * C, U32)
-            for s in range(first, PASSES):
-                gather_words((e,), s, words[:, (s - first) * C : (s - first + 1) * C])
-
-        gather_words(SECOND_PAIR, 0, work_tile(("words", SECOND_PAIR[0], 0), 2 * C, U32)[:])
-        gather_scales(SECOND_PAIR, 1, work_tile(("scales", SECOND_PAIR[0], 1), 2 * C, U8)[:])
-        gather_words((FIFTH,), 0, work_tile(("words", FIFTH, 0), C, U32)[:])
-        gather_scales((HOT, FIFTH), 1, work_tile(("scales", HOT, 1), 2 * C, U8)[:])
-        gather_passes(FIFTH, 1)
-        gather_passes(HOT, 0)
-        first_product(SECOND_PAIR[0])
-        activate(SECOND_PAIR[0])
-        turn(FIRST_PAIR, "turned0", nc.vector.tensor_copy)
+        first_product(4, "bankA")
+        activate(4)
+        first_product(5, "bankB")
+        first_product(2, "bankC")
+        activate(5)
+        activate(2)
+        first_product(3, "bankD")
+        activate(3)
+        turn(FIRST_PAIR, "bankG", nc.vector.tensor_copy)
         quantize(0, 2)
-        first_product(SECOND_PAIR[1])
-        first_product(FIFTH)
-        activate(SECOND_PAIR[1])
+        first_product(FIFTH, "bankA")
         activate(FIFTH)
-        turn(SECOND_PAIR, "pre3", nc.vector.tensor_copy)
+        turn(SECOND_PAIR, "bankB", nc.vector.tensor_copy)
         quantize(2, 2)
-        first_product(HOT)
+        first_product(HOT, "bankD")
         activate(HOT)
-        turn((FIFTH,), "turned1", nc.vector.tensor_copy)
+        turn((FIFTH,), "bankE", nc.vector.tensor_copy)
         quantize(4, 1)
-        second_product(FIRST_PAIR, "pre2", nc.vector.tensor_copy)
-        turn((HOT,), "turned2", nc.scalar.copy)
+        second_product(FIRST_PAIR, "bankG", nc.scalar.copy)
+        second_product(SECOND_PAIR, "bankH", nc.vector.tensor_copy)
+        turn((HOT,), "bankF", nc.scalar.copy)
         quantize(5, 1)
-        second_product(SECOND_PAIR, "pre0", nc.scalar.copy)
-        second_product((FIFTH,), "turned0", nc.vector.tensor_copy)
-        last_second_product(HOT)
+        second_product((FIFTH,), "bankA", nc.vector.tensor_copy)
+        last_second_product(HOT, ("bankB", "bankC"))

@@ -86,15 +86,15 @@ def tile_moe_hot_s_mlp_silu_kernel(
             nc.sync.dma_start(out=w2c[:, matrices, :].bitcast(I32), in_=rows[:, matrices, :])
 
         x_rows = x_words.rearrange("s p t d -> p s (t d)").bitcast(I32)
-        nc.sync.dma_start(offsets[:], offs)
         nc.sync.dma_start(out=xw_first[:], in_=x_rows[:, 0:1, :])
+        nc.sync.dma_start(offsets[:], offs)
         nc.sync.dma_start(out=xs[PARKED : PARKED + 16, 0, :].bitcast(I32), in_=x_scales[PASSES - 1].bitcast(I32))
         load_scales(xs, x_scales[0 : PASSES - 1])
         nc.sync.dma_start(out=xw_rest[:], in_=x_rows[:, 1:PASSES, :])
+        load_scales(s1_early, w1c_scales[LATE:COLD].rearrange("f s b i -> (f s) b i"))
         load_w1_cold(ORDER[0])
         load_scales(s2c, w2c_scales.rearrange("f s b n -> (f s) b n"))
         load_w1_cold(ORDER[1])
-        load_scales(s1_early, w1c_scales[LATE:COLD].rearrange("f s b i -> (f s) b i"), queue=nc.gpsimd)
         load_scales(s1_late, w1c_scales[0:LATE].rearrange("f s b i -> (f s) b i"), queue=nc.gpsimd)
         load_scales(s1h, w1h_scales[0], HOT_ROW, nc.gpsimd)
 

@@ -40,8 +40,8 @@ def tile_moe_hot_s_mlp_silu_kernel(
         psum = ctx.enter_context(tc.psum_pool(name="psum", bufs=1))
 
         offsets = keep.tile([P, E * C // 16], U16, name="offsets")
-        xw_first = keep.tile([P, 1, T], I32, name="xw_first", align_bytes=ALIGN)
-        xw_rest = keep.tile([P, PASSES - 1, T], I32, name="xw_rest", align_bytes=ALIGN)
+        xw_first = keep.tile([P, PASSES - 1, T], I32, name="xw_first", align_bytes=ALIGN)
+        xw_rest = keep.tile([P, 1, T], I32, name="xw_rest", align_bytes=ALIGN)
         xs = keep.tile([P, PASSES - 1, T], U8, name="xs", align_bytes=ALIGN)
         w1 = [
             keep.tile([P, PASSES, H * (4 if e == HOT else 2)], U8, name="w1_%d" % e, align_bytes=ALIGN)
@@ -63,9 +63,9 @@ def tile_moe_hot_s_mlp_silu_kernel(
         words = [keep.tile([P, E * C], U32, name="words%d" % s, align_bytes=ALIGN) for s in range(PASSES)]
         third_words = shared.tile([P, C], U32, name="third_words", align_bytes=ALIGN, offset=0)
 
-        for plane in (s2c, moved, s2h):
+        for plane in (s1h, moved, s2h):
             nc.gpsimd.memset(plane[:].bitcast(I32), 0)
-        for plane in (xs, s1_early, s1_late, s1h):
+        for plane in (xs, s1_early, s1_late, s2c):
             nc.vector.memset(plane[:].bitcast(I32), 0)
         make_identity(nc, ident[:])
 
@@ -86,28 +86,28 @@ def tile_moe_hot_s_mlp_silu_kernel(
             nc.sync.dma_start(out=w2c[:, matrices, :].bitcast(I32), in_=rows[:, matrices, :])
 
         x_rows = x_words.rearrange("s p t d -> p s (t d)").bitcast(I32)
-        nc.sync.dma_start(out=xw_first[:], in_=x_rows[:, 0:1, :])
-        nc.sync.dma_start(offsets[:], offs)
+        nc.sync.dma_start(out=xw_first[:], in_=x_rows[:, 0 : PASSES - 1, :])
         nc.sync.dma_start(out=xs[PARKED : PARKED + 16, 0, :].bitcast(I32), in_=x_scales[PASSES - 1].bitcast(I32))
         load_scales(xs, x_scales[0 : PASSES - 1])
-        nc.sync.dma_start(out=xw_rest[:], in_=x_rows[:, 1:PASSES, :])
+        nc.sync.dma_start(offsets[:], offs)
+        nc.sync.dma_start(out=xw_rest[:], in_=x_rows[:, PASSES - 1 : PASSES, :])
         load_scales(s1_early, w1c_scales[LATE:COLD].rearrange("f s b i -> (f s) b i"))
         load_w1_cold(ORDER[0])
-        load_scales(s2c, w2c_scales.rearrange("f s b n -> (f s) b n"))
+        load_scales(s1h, w1h_scales[0], HOT_ROW)
         load_w1_cold(ORDER[1])
         load_scales(s1_late, w1c_scales[0:LATE].rearrange("f s b i -> (f s) b i"), queue=nc.gpsimd)
-        load_scales(s1h, w1h_scales[0], HOT_ROW, nc.gpsimd)
+        load_scales(s2c, w2c_scales.rearrange("f s b n -> (f s) b n"), queue=nc.gpsimd)
 
-        def gather(dst, window, first, count):
-            columns = slice(first * C, (first + count) * C)
-            nc.vector.tensor_copy(out=dst[:, columns], in_=window.indirect(offsets[:, first * C // 16 : (first + count) * C // 16]))
+        def gather(dst, window, e):
+            nc.vector.tensor_copy(out=dst, in_=window.indirect(offsets[:, e * C // 16 : (e + 1) * C // 16]))
 
-        HALF = E // 2
-        gather(words[0], xw_first[:, 0, :].bitcast(U32), HALF, HALF)
-        nc.vector.tensor_copy(out=third_words[:], in_=xw_first[:, 0, :].bitcast(U32).indirect(offsets[:, 2 * C // 16 : 3 * C // 16]))
-        gather(words[0], xw_first[:, 0, :].bitcast(U32), 0, 2)
-        for first in (HALF, 0):
-            gather(picked, xs[:, 0, :], first, HALF)
+        def gather_words(e, s):
+            window = xw_first[:, s, :] if s < PASSES - 1 else xw_rest[:, 0, :]
+            dst = third_words[:] if (e, s) == (ORDER[2], 0) else words[s][:, e * C : (e + 1) * C]
+            gather(dst, window.bitcast(U32), e)
+
+        for e in ORDER:
+            gather(picked[:, e * C : (e + 1) * C], xs[:, 0, :], e)
         for r in range(4):
             nc.sync.dma_start(out=moved[r:P:32, :].bitcast(I32), in_=picked[PARKED + r : PARKED + 16 : 4, :].bitcast(I32))
         load_w1_cold(ORDER[2])
@@ -119,11 +119,11 @@ def tile_moe_hot_s_mlp_silu_kernel(
         load_w2_cold(slice(0, 1))
         nc.sync.dma_start(out=w2h[:].bitcast(I32), in_=w2h_words[0, 0].rearrange("p n d -> p (n d)").bitcast(I32))
         load_scales(s2h, w2h_scales[0])
-        for first in (HALF, 0):
-            gather(picked1, xs[:, 1, :], first, HALF)
-        for first in (4, 2, 0):
+        for e in ORDER:
+            gather_words(e, 0)
+            gather(picked1[:, e * C : (e + 1) * C], xs[:, 1, :], e)
             for s in range(1, PASSES):
-                gather(words[s], xw_rest[:, s - 1, :].bitcast(U32), first, 2)
+                gather_words(e, s)
 
         slot_scales = (picked, picked1, moved)
 
@@ -224,7 +224,7 @@ def tile_moe_hot_s_mlp_silu_kernel(
         activate(2)
         first_product(3, "bankD")
         activate(3)
-        turn(FIRST_PAIR, "bankG", nc.vector.tensor_copy)
+        turn(FIRST_PAIR, "bankG", nc.scalar.copy)
         quantize(0, 2)
         first_product(FIFTH, "bankA")
         activate(FIFTH)

@@ -20,13 +20,12 @@ P = 128
 PASSES = K // 512
 COLD = E - 1
 HOT = 0
-ORDER = (4, 5, 2, 3, 1, HOT)
-FIRST_PAIR, SECOND_PAIR, FIFTH = ORDER[0:2], ORDER[2:4], ORDER[4]
-LATE = 3
+LAST = E - 1
 HOT_ROW = 4
 ALIGN = 64
-
 PARKED = 8
+WORDS = 4 * C
+CHAIN = 9 * WORDS
 
 
 def tile_moe_hot_s_mlp_silu_kernel(
@@ -39,158 +38,167 @@ def tile_moe_hot_s_mlp_silu_kernel(
         shared = ctx.enter_context(tc.tile_pool(name="shared", bufs=1))
         psum = ctx.enter_context(tc.psum_pool(name="psum", bufs=1))
 
+        def tile(shape, dtype, name):
+            return keep.tile(shape, dtype, name=name, align_bytes=ALIGN)
+
         offsets = keep.tile([P, E * C // 16], U16, name="offsets")
-        xw_first = keep.tile([P, PASSES - 1, T], I32, name="xw_first", align_bytes=ALIGN)
-        xw_rest = keep.tile([P, 1, T], I32, name="xw_rest", align_bytes=ALIGN)
-        xs = keep.tile([P, PASSES - 1, T], U8, name="xs", align_bytes=ALIGN)
-        w1 = [
-            keep.tile([P, PASSES, H * (4 if e == HOT else 2)], U8, name="w1_%d" % e, align_bytes=ALIGN)
-            for e in range(E)
-        ]
-        s1_early = keep.tile([P, (COLD - LATE) * PASSES, H], U8, name="s1_early", align_bytes=ALIGN)
-        s1h = keep.tile([P, PASSES, H], U8, name="s1h", align_bytes=ALIGN)
-        s1_late = keep.tile([P, LATE * PASSES, H], U8, name="s1_late", align_bytes=ALIGN)
-        w2h = keep.tile([P, N * 4], U8, name="w2h", align_bytes=ALIGN)
-        w2c = keep.tile([P, COLD, N * 2], U8, name="w2c", align_bytes=ALIGN)
-        s2c = keep.tile([P, COLD, N], U8, name="s2c", align_bytes=ALIGN)
-        s2h = keep.tile([P, 1, N], U8, name="s2h", align_bytes=ALIGN)
-        ident = keep.tile([P, P], F32, name="ident")
-        h_codes = keep.tile([P, E * C], U32, name="h_codes", align_bytes=ALIGN)
-        h_scales = keep.tile([P, E * C], U8, name="h_scales", align_bytes=ALIGN)
-        picked = keep.tile([P, E * C], U8, name="picked", align_bytes=ALIGN)
-        picked1 = keep.tile([P, E * C], U8, name="picked1", align_bytes=ALIGN)
-        moved = keep.tile([P, E * C], U8, name="moved", align_bytes=ALIGN)
-        words = [keep.tile([P, E * C], U32, name="words%d" % s, align_bytes=ALIGN) for s in range(PASSES)]
-        third_words = shared.tile([P, C], U32, name="third_words", align_bytes=ALIGN, offset=0)
+        xw = [tile([P, T], I32, "xw%d" % s) for s in range(PASSES)]
+        xs = tile([P, PASSES - 1, T], U8, "xs")
+        w1h_first = shared.tile([P, 1, H * 4], U8, name="w1h_first", align_bytes=ALIGN, offset=CHAIN)
+        w1h_rest = tile([P, PASSES - 1, H * 4], U8, "w1h_rest")
+        w1c = [tile([P, PASSES, H * 2], U8, "w1c%d" % f) for f in range(COLD - 1)]
+        w1_last = tile([P, PASSES - 1, H * 2], U8, "w1_last")
+        w1_end = tile([P, 1, H * 2], U8, "w1_end")
+        s1c = tile([P, COLD * PASSES, H], U8, "s1c")
+        s1h = tile([P, PASSES, H], U8, "s1h")
+        w2h = tile([P, N * 4], U8, "w2h")
+        w2c_early = tile([P, 2, N * 2], U8, "w2c_early")
+        w2c_late = tile([P, COLD - 2, N * 2], U8, "w2c_late")
+        s2c = tile([P, COLD, N], U8, "s2c")
+        s2h = tile([P, 1, N], U8, "s2h")
+        h_codes = tile([P, E * C], U32, "h_codes")
+        h_scales = tile([P, E * C], U8, "h_scales")
+        picked = tile([P, E * C], U8, "picked")
+        moved = tile([P, E * C], U8, "moved")
 
-        for plane in (s1h, moved, s2h):
+        for plane in (xs, s1h):
             nc.gpsimd.memset(plane[:].bitcast(I32), 0)
-        for plane in (xs, s1_early, s1_late, s2c):
-            nc.vector.memset(plane[:].bitcast(I32), 0)
+        ident = keep.tile([P, P], F32, name="ident")
         make_identity(nc, ident[:])
+        for plane in (s1c, moved, s2c, s2h):
+            nc.vector.memset(plane[:].bitcast(I32), 0)
 
-        def load_scales(plane, rows, first_row=0, queue=nc.sync):
+        def load_scales(plane, rows, first_row=0, queue=nc.sync, which=range(4)):
             by_row = rows.bitcast(I32).rearrange("a (q r) c -> r q a c", r=4)
-            for r in range(4):
+            for r in which:
                 queue.dma_start(out=plane[first_row + r : P : 32, :, :].bitcast(I32), in_=by_row[r])
 
-        def load_w1_cold(e):
-            nc.sync.dma_start(out=w1[e][:].bitcast(I32), in_=w1c_words[e - 1].rearrange("s p b -> p s b").bitcast(I32))
+        def load_cold(dst, e, passes):
+            nc.sync.dma_start(out=dst[:].bitcast(I32), in_=w1c_words[e - 1, passes].rearrange("s p b -> p s b").bitcast(I32))
 
-        def load_w1_hot(first, last):
-            passes = w1h_words[0, first:last].rearrange("s p i d -> p s (i d)")
-            nc.sync.dma_start(out=w1[HOT][:, first:last, :].bitcast(I32), in_=passes.bitcast(I32))
+        def load_hot(dst, passes):
+            nc.sync.dma_start(out=dst[:].bitcast(I32), in_=w1h_words[0, passes].rearrange("s p i d -> p s (i d)").bitcast(I32))
 
-        def load_w2_cold(matrices):
-            rows = w2c_words.rearrange("f s p b -> p (f s) b").bitcast(I32)
-            nc.sync.dma_start(out=w2c[:, matrices, :].bitcast(I32), in_=rows[:, matrices, :])
-
-        x_rows = x_words.rearrange("s p t d -> p s (t d)").bitcast(I32)
-        nc.sync.dma_start(out=xw_first[:], in_=x_rows[:, 0 : PASSES - 1, :])
-        nc.sync.dma_start(out=xs[PARKED : PARKED + 16, 0, :].bitcast(I32), in_=x_scales[PASSES - 1].bitcast(I32))
-        load_scales(xs, x_scales[0 : PASSES - 1])
+        x_rows = x_words.rearrange("s p t d -> s p (t d)").bitcast(I32)
         nc.sync.dma_start(offsets[:], offs)
-        nc.sync.dma_start(out=xw_rest[:], in_=x_rows[:, PASSES - 1 : PASSES, :])
-        load_scales(s1_early, w1c_scales[LATE:COLD].rearrange("f s b i -> (f s) b i"))
-        load_w1_cold(ORDER[0])
+        nc.sync.dma_start(out=xw[0][:], in_=x_rows[0])
+        load_scales(xs, x_scales[0 : PASSES - 1])
+        nc.sync.dma_start(out=xs[PARKED : PARKED + 16, 0, :].bitcast(I32), in_=x_scales[PASSES - 1].bitcast(I32))
+        nc.sync.dma_start(out=xw[1][:], in_=x_rows[1])
+        nc.sync.dma_start(out=xw[2][:], in_=x_rows[2])
+        load_hot(w1h_first, slice(0, 1))
         load_scales(s1h, w1h_scales[0], HOT_ROW)
-        load_w1_cold(ORDER[1])
-        load_scales(s1_late, w1c_scales[0:LATE].rearrange("f s b i -> (f s) b i"), queue=nc.gpsimd)
-        load_scales(s2c, w2c_scales.rearrange("f s b n -> (f s) b n"), queue=nc.gpsimd)
+        load_hot(w1h_rest, slice(1, PASSES))
+        cold_rows = w1c_scales.rearrange("f s b i -> (f s) b i")
+        load_scales(s1c, cold_rows, which=range(3, 4))
+        load_scales(s1c, cold_rows, queue=nc.gpsimd, which=range(3))
 
-        def gather(dst, window, e):
-            nc.vector.tensor_copy(out=dst, in_=window.indirect(offsets[:, e * C // 16 : (e + 1) * C // 16]))
+        def gather(dst, window, first, count):
+            nc.vector.tensor_copy(out=dst, in_=window.indirect(offsets[:, first * C // 16 : (first + count) * C // 16]))
 
-        def gather_words(e, s):
-            window = xw_first[:, s, :] if s < PASSES - 1 else xw_rest[:, 0, :]
-            dst = third_words[:] if (e, s) == (ORDER[2], 0) else words[s][:, e * C : (e + 1) * C]
-            gather(dst, window.bitcast(U32), e)
+        slot_words = {}
+        slot_scales = {}
 
-        for e in ORDER:
-            gather(picked[:, e * C : (e + 1) * C], xs[:, 0, :], e)
+        def gather_words(dst, column, s, first, count):
+            gather(dst[:, column * C : (column + count) * C], xw[s][:].bitcast(U32), first, count)
+            for j in range(count):
+                slot_words[first + j, s] = dst[:, (column + j) * C : (column + j + 1) * C]
+
+        def gather_second_scales(dst, first, count):
+            gather(dst[:], xs[:, 1, :], first, count)
+            for j in range(count):
+                slot_scales[first + j, 1] = dst[:, j * C : (j + 1) * C]
+
+        hot_words = shared.tile([P, C], U32, name="hot_words", align_bytes=ALIGN, offset=0)
+        early_words = tile([P, 6 * C], U32, "early_words")
+        early_scales = tile([P, 2 * C], U8, "early_scales")
+        gather_words(hot_words, 0, 0, HOT, 1)
+        for half in range(2):
+            gather(picked[:, half * 3 * C : (half + 1) * 3 * C], xs[:, 0, :], half * 3, 3)
         for r in range(4):
             nc.sync.dma_start(out=moved[r:P:32, :].bitcast(I32), in_=picked[PARKED + r : PARKED + 16 : 4, :].bitcast(I32))
-        load_w1_cold(ORDER[2])
-        load_w1_cold(ORDER[3])
-        load_w1_cold(ORDER[4])
-        for s in range(PASSES):
-            load_w1_hot(s, s + 1)
-        load_w2_cold(slice(1, COLD))
-        load_w2_cold(slice(0, 1))
+        for e in range(E):
+            slot_scales[e, 0] = picked[:, e * C : (e + 1) * C]
+            slot_scales[e, 2] = moved[:, e * C : (e + 1) * C]
+        gather_second_scales(early_scales, 0, 2)
+        gather_words(early_words, 0, 0, 1, 2)
+        gather_words(early_words, 2, 1, 0, 2)
+        gather_words(early_words, 4, 2, 0, 2)
+
+        for e in range(1, LAST - 1):
+            load_cold(w1c[e - 1], e, slice(0, PASSES))
+        load_scales(s2h, w2h_scales[0], HOT_ROW)
+        load_cold(w1c[LAST - 2], LAST - 1, slice(0, PASSES))
+        second_rows = w2c_scales.rearrange("f s b n -> (f s) b n")
+        load_scales(s2c, second_rows, which=range(2, 4))
+        load_cold(w1_last, LAST, slice(0, PASSES - 1))
+        load_cold(w1_end, LAST, slice(PASSES - 1, PASSES))
         nc.sync.dma_start(out=w2h[:].bitcast(I32), in_=w2h_words[0, 0].rearrange("p n d -> p (n d)").bitcast(I32))
-        load_scales(s2h, w2h_scales[0])
-        for e in ORDER:
-            gather_words(e, 0)
-            gather(picked1[:, e * C : (e + 1) * C], xs[:, 1, :], e)
-            for s in range(1, PASSES):
-                gather_words(e, s)
+        w2c_rows = w2c_words.rearrange("f s p b -> p (f s) b").bitcast(I32)
+        nc.sync.dma_start(out=w2c_early[:].bitcast(I32), in_=w2c_rows[:, 0:2, :])
+        nc.sync.dma_start(out=w2c_late[:].bitcast(I32), in_=w2c_rows[:, 2:COLD, :])
 
-        slot_scales = (picked, picked1, moved)
-
-        def w1_scale(e, s):
+        def w1_operand(e, s):
             if e == HOT:
-                return s1h[HOT_ROW:P, s, :]
-            if e > LATE:
-                return s1_early[:, (e - 1 - LATE) * PASSES + s, :]
-            return s1_late[:, (e - 1) * PASSES + s, :]
+                codes = w1h_first[:, 0, :] if s == 0 else w1h_rest[:, s - 1, :]
+                return codes.bitcast(FP8X4), s1h[HOT_ROW:P, s, :]
+            if e < LAST:
+                codes = w1c[e - 1][:, s, :]
+            else:
+                codes = w1_last[:, s, :] if s < PASSES - 1 else w1_end[:, 0, :]
+            return codes.bitcast(FP4X4), s1c[:, (e - 1) * PASSES + s, :]
 
         sums = {}
         h_rows = {}
         h_cols = {}
 
+        def first_pass(e, s, bank):
+            if s == 0:
+                sums[e] = psum.tile([P, H], F32, name=bank)
+            codes, plane = w1_operand(e, s)
+            nc.tensor.matmul_mx(
+                out=sums[e][:], lhsT=slot_words[e, s].bitcast(FP8X4), lhsT_scale=slot_scales[e, s],
+                rhs=codes, rhs_scale=plane, start=(s == 0), stop=(s == PASSES - 1),
+            )
+
         def first_product(e, bank):
-            pre = psum.tile([P, H], F32, name=bank)
-            slots = slice(e * C, (e + 1) * C)
             for s in range(PASSES):
-                nc.tensor.matmul_mx(
-                    out=pre[:],
-                    lhsT=(third_words[:] if (e, s) == (2, 0) else words[s][:, slots]).bitcast(FP8X4),
-                    lhsT_scale=slot_scales[s][:, slots],
-                    rhs=w1[e][:, s, :].bitcast(FP8X4 if e == HOT else FP4X4),
-                    rhs_scale=w1_scale(e, s),
-                    start=(s == 0),
-                    stop=(s == PASSES - 1),
-                )
-            sums[e] = pre
+                first_pass(e, s, bank)
+            if e not in (2, 4):
+                activate(e, tile([P, H], BF16, "rows%d" % e))
 
-        def activate(e):
-            if e == FIRST_PAIR[1]:
-                h_rows[e] = shared.tile([P, H], BF16, name="rows%d" % e, align_bytes=ALIGN, offset=0)
-            else:
-                h_rows[e] = keep.tile([P, H], BF16, name="rows%d" % e, align_bytes=ALIGN)
-            h_view = h_rows[e][:].rearrange("j (u p v) -> j u p v", u=2, v=2)
-            pre_view = sums[e][:].rearrange("j (p u v) -> j u p v", u=2, v=2)
-            if e == HOT:
-                for u in range(2):
-                    nc.scalar.activation(out=h_view[:, u, :, :], in_=pre_view[:, u, :, :], func=SILU)
-            else:
-                nc.scalar.activation(out=h_view, in_=pre_view, func=SILU)
+        def activate(e, rows):
+            h_rows[e] = rows
+            nc.scalar.activation(
+                out=h_rows[e][:].rearrange("j (u p v) -> j u p v", u=2, v=2),
+                in_=sums[e][:].rearrange("j (p u v) -> j u p v", u=2, v=2),
+                func=SILU,
+            )
 
-        def turn(group, bank, copy):
-            turned = psum.tile([P, len(group), 2, C], F32, name=bank)
-            for j, e in enumerate(group):
-                pairs = h_rows[e][:].bitcast(F32)
+        def turn(first, count, bank, copy, dst, column):
+            turned = psum.tile([P, count, 2, C], F32, name=bank)
+            for j in range(count):
+                pairs = h_rows[first + j][:].bitcast(F32)
                 for u in range(2):
                     nc.tensor.transpose(turned[:, j, u, :], pairs[:, u * P : (u + 1) * P], ident[:])
-            place = ORDER.index(group[0])
-            h_cols[place] = keep.tile([P, len(group) * H], BF16, name="h_cols%d" % place, align_bytes=ALIGN)
             copy(
-                out=h_cols[place][:].bitcast(F32).rearrange("p (x j u) -> p x j u", x=len(group), u=2),
+                out=dst[:, column * H : (column + count) * H].bitcast(F32).rearrange("p (x j u) -> p x j u", x=count, u=2),
                 in_=turned[:].rearrange("p x u j -> p x j u"),
             )
 
-        def quantize(first, count):
+        def quantize(first, count, src):
             columns = slice(first * C, (first + count) * C)
-            nc.vector.quantize_mx(out=h_codes[:, columns].bitcast(FP8X4), scales=h_scales[:, columns], in_=h_cols[first][:])
+            nc.vector.quantize_mx(out=h_codes[:, columns].bitcast(FP8X4), scales=h_scales[:, columns], in_=src[:])
 
         def second_matmul(e, m, y):
             if e == HOT:
                 lhsT = w2h[:, m * 4 * P : (m + 1) * 4 * P].bitcast(FP8X4)
-                lhsT_scale = s2h[:, 0, m * P : (m + 1) * P]
+                lhsT_scale = s2h[HOT_ROW:P, 0, m * P : (m + 1) * P]
             else:
-                lhsT = w2c[:, e - 1, m * 2 * P : (m + 1) * 2 * P].bitcast(FP4X4)
+                codes = w2c_early[:, e - 1, :] if e < 3 else w2c_late[:, e - 3, :]
+                lhsT = codes[:, m * 2 * P : (m + 1) * 2 * P].bitcast(FP4X4)
                 lhsT_scale = s2c[:, e - 1, m * P : (m + 1) * P]
-            columns = slice(ORDER.index(e) * C, (ORDER.index(e) + 1) * C)
+            columns = slice(e * C, (e + 1) * C)
             nc.tensor.matmul_mx(
                 out=y, lhsT=lhsT, lhsT_scale=lhsT_scale,
                 rhs=h_codes[:, columns].bitcast(FP8X4), rhs_scale=h_scales[:, columns], start=True, stop=True,
@@ -198,45 +206,57 @@ def tile_moe_hot_s_mlp_silu_kernel(
 
         out_rows = out.rearrange("(m p) j -> p m j", p=P)
 
-        def second_product(group, bank, copy):
-            n = len(group) * C
-            y = psum.tile([P, 2, n], F32, name=bank)
-            for j, e in enumerate(group):
-                for m in range(2):
-                    second_matmul(e, m, y[:, m, j * C : (j + 1) * C])
-            result = keep.tile([P, 2, n], F32, name="result%d" % group[0])
+        def second_product(first, count, halves, bank, copy, queue):
+            y = psum.tile([P, len(halves), count * C], F32, name=bank)
+            for i, m in enumerate(halves):
+                for j in range(count):
+                    second_matmul(first + j, m, y[:, i, j * C : (j + 1) * C])
+            result = keep.tile([P, len(halves), count * C], F32, name="result%d_%d" % (first, halves[0]))
             copy(out=result[:], in_=y[:])
-            nc.sync.dma_start(out=out_rows[:, :, group[0] * C : group[0] * C + n], in_=result[:])
+            queue.dma_start(out=out_rows[:, halves[0] : halves[-1] + 1, first * C : (first + count) * C], in_=result[:])
 
-        def last_second_product(e, banks):
-            for m, (copy, queue) in enumerate(((nc.scalar.copy, nc.scalar), (nc.vector.tensor_copy, nc.sync))):
-                y = psum.tile([P, C], F32, name=banks[m])
-                second_matmul(e, m, y[:])
-                result = keep.tile([P, C], F32, name="result_last%d" % m)
-                copy(out=result[:], in_=y[:])
-                queue.dma_start(out=out_rows[:, m, e * C : (e + 1) * C], in_=result[:])
+        cols_three = tile([P, 3 * H], BF16, "cols_three")
+        cols_pair = tile([P, 2 * H], BF16, "cols_pair")
+        cols_last = tile([P, H], BF16, "cols_last")
 
-        first_product(4, "bankA")
-        activate(4)
-        first_product(5, "bankB")
-        first_product(2, "bankC")
-        activate(5)
-        activate(2)
-        first_product(3, "bankD")
-        activate(3)
-        turn(FIRST_PAIR, "bankG", nc.scalar.copy)
-        quantize(0, 2)
-        first_product(FIFTH, "bankA")
-        activate(FIFTH)
-        turn(SECOND_PAIR, "bankB", nc.vector.tensor_copy)
-        quantize(2, 2)
-        first_product(HOT, "bankD")
-        activate(HOT)
-        turn((FIFTH,), "bankE", nc.vector.tensor_copy)
-        quantize(4, 1)
-        second_product(FIRST_PAIR, "bankG", nc.scalar.copy)
-        second_product(SECOND_PAIR, "bankH", nc.vector.tensor_copy)
-        turn((HOT,), "bankF", nc.scalar.copy)
-        quantize(5, 1)
-        second_product((FIFTH,), "bankA", nc.vector.tensor_copy)
-        last_second_product(HOT, ("bankB", "bankC"))
+        first_product(HOT, "bank0")
+        load_scales(s2c, second_rows, queue=nc.gpsimd, which=range(2))
+
+        late_words = shared.tile([P, 8 * C], U32, name="late_words", align_bytes=ALIGN, offset=0)
+        fourth_words = shared.tile([P, C], U32, name="fourth_words", align_bytes=ALIGN, offset=CHAIN)
+        last_words = shared.tile([P, 2 * C], U32, name="last_words", align_bytes=ALIGN, offset=CHAIN + WORDS)
+        late_scales = shared.tile([P, 4 * C], U8, name="late_scales", align_bytes=ALIGN, offset=CHAIN + 3 * WORDS)
+        gather_second_scales(late_scales, 2, 4)
+        gather_words(late_words, 0, 1, 2, 2)
+        gather_words(late_words, 2, 2, 2, 2)
+        gather_words(fourth_words, 0, 0, 3, 1)
+        gather_words(last_words, 0, 0, 4, 2)
+        gather_words(late_words, 4, 1, 4, 1)
+        gather_words(late_words, 5, 2, 4, 1)
+        gather_words(late_words, 6, 1, 5, 1)
+        gather_words(late_words, 7, 2, 5, 1)
+
+        turn(0, 1, "bank4", nc.scalar.copy, cols_three, 0)
+        first_product(1, "bank1")
+        first_product(2, "bank2")
+        first_pass(3, 0, "bank0")
+        activate(2, shared.tile([P, H], BF16, name="rows_third", align_bytes=ALIGN, offset=CHAIN - WORDS))
+        for s in range(1, PASSES):
+            first_pass(3, s, "bank0")
+        activate(3, tile([P, H], BF16, "rows_fourth"))
+        turn(1, 2, "bank2", nc.vector.tensor_copy, cols_three, 1)
+        first_product(4, "bank1")
+        first_pass(LAST, 0, "bank3")
+        activate(4, shared.tile([P, H], BF16, name="rows_fifth", align_bytes=ALIGN, offset=CHAIN + WORDS))
+        for s in range(1, PASSES):
+            first_pass(LAST, s, "bank3")
+        activate(LAST, tile([P, H], BF16, "rows_last"))
+        quantize(0, 3, cols_three)
+        turn(3, 2, "bank1", nc.vector.tensor_copy, cols_pair, 0)
+        turn(5, 1, "bank5", nc.scalar.copy, cols_last, 0)
+        quantize(3, 2, cols_pair)
+        quantize(5, 1, cols_last)
+        second_product(0, 3, (0,), "bank3", nc.scalar.copy, nc.sync)
+        second_product(0, 3, (1,), "bank1", nc.vector.tensor_copy, nc.sync)
+        second_product(3, 2, (0, 1), "bank6", nc.scalar.copy, nc.sync)
+        second_product(5, 1, (0, 1), "bank0", nc.vector.tensor_copy, nc.sync)

@@ -24,8 +24,8 @@ LAST = E - 1
 HOT_ROW = 4
 ALIGN = 64
 PARKED = 8
+LATE = 3
 WORDS = 4 * C
-CHAIN = 9 * WORDS
 
 
 def tile_moe_hot_s_mlp_silu_kernel(
@@ -42,56 +42,50 @@ def tile_moe_hot_s_mlp_silu_kernel(
             return keep.tile(shape, dtype, name=name, align_bytes=ALIGN)
 
         offsets = keep.tile([P, E * C // 16], U16, name="offsets")
-        xw = [tile([P, T], I32, "xw%d" % s) for s in range(PASSES)]
+        xw_first = tile([P, 1, T], I32, "xw_first")
+        xw_rest = tile([P, PASSES - 1, T], I32, "xw_rest")
         xs = tile([P, PASSES - 1, T], U8, "xs")
-        w1h_first = shared.tile([P, 1, H * 4], U8, name="w1h_first", align_bytes=ALIGN, offset=CHAIN)
-        w1h_rest = tile([P, PASSES - 1, H * 4], U8, "w1h_rest")
-        w1c = [tile([P, PASSES, H * 2], U8, "w1c%d" % f) for f in range(COLD - 1)]
-        w1_last = tile([P, PASSES - 1, H * 2], U8, "w1_last")
-        w1_end = tile([P, 1, H * 2], U8, "w1_end")
-        s1c = tile([P, COLD * PASSES, H], U8, "s1c")
+        w1h = [tile([P, 1, H * 4], U8, "w1h%d" % s) for s in range(PASSES)]
+        w1c = [tile([P, PASSES, H * 2], U8, "w1c%d" % f) for f in range(COLD)]
+        s1_early = tile([P, (COLD - LATE) * PASSES, H], U8, "s1_early")
+        s1_late = tile([P, LATE * PASSES, H], U8, "s1_late")
         s1h = tile([P, PASSES, H], U8, "s1h")
         w2h = tile([P, N * 4], U8, "w2h")
-        w2c_early = tile([P, 2, N * 2], U8, "w2c_early")
-        w2c_late = tile([P, COLD - 2, N * 2], U8, "w2c_late")
+        w2c_late = tile([P, 2, N * 2], U8, "w2c_late")
+        w2c_early = tile([P, COLD - 2, N * 2], U8, "w2c_early")
         s2c = tile([P, COLD, N], U8, "s2c")
         s2h = tile([P, 1, N], U8, "s2h")
         h_codes = tile([P, E * C], U32, "h_codes")
         h_scales = tile([P, E * C], U8, "h_scales")
         picked = tile([P, E * C], U8, "picked")
         moved = tile([P, E * C], U8, "moved")
-
-        for plane in (xs, s1h):
-            nc.gpsimd.memset(plane[:].bitcast(I32), 0)
         ident = keep.tile([P, P], F32, name="ident")
+
+        for plane in (xs, moved, s1h, s2h):
+            nc.gpsimd.memset(plane[:].bitcast(I32), 0)
         make_identity(nc, ident[:])
-        for plane in (s1c, moved, s2c, s2h):
+        for plane in (s1_late, s1_early, s2c):
             nc.vector.memset(plane[:].bitcast(I32), 0)
 
-        def load_scales(plane, rows, first_row=0, queue=nc.sync, which=range(4)):
+        def load_scales(plane, rows, first_row=0, queue=nc.sync):
             by_row = rows.bitcast(I32).rearrange("a (q r) c -> r q a c", r=4)
-            for r in which:
+            for r in range(4):
                 queue.dma_start(out=plane[first_row + r : P : 32, :, :].bitcast(I32), in_=by_row[r])
 
-        def load_cold(dst, e, passes):
-            nc.sync.dma_start(out=dst[:].bitcast(I32), in_=w1c_words[e - 1, passes].rearrange("s p b -> p s b").bitcast(I32))
+        def load_cold(e):
+            nc.sync.dma_start(out=w1c[e - 1][:].bitcast(I32), in_=w1c_words[e - 1].rearrange("s p b -> p s b").bitcast(I32))
 
-        def load_hot(dst, passes):
-            nc.sync.dma_start(out=dst[:].bitcast(I32), in_=w1h_words[0, passes].rearrange("s p i d -> p s (i d)").bitcast(I32))
-
-        x_rows = x_words.rearrange("s p t d -> s p (t d)").bitcast(I32)
-        nc.sync.dma_start(offsets[:], offs)
-        nc.sync.dma_start(out=xw[0][:], in_=x_rows[0])
+        x_rows = x_words.rearrange("s p t d -> p s (t d)").bitcast(I32)
+        nc.sync.dma_start(out=xw_first[:], in_=x_rows[:, 0:1, :])
         load_scales(xs, x_scales[0 : PASSES - 1])
         nc.sync.dma_start(out=xs[PARKED : PARKED + 16, 0, :].bitcast(I32), in_=x_scales[PASSES - 1].bitcast(I32))
-        nc.sync.dma_start(out=xw[1][:], in_=x_rows[1])
-        nc.sync.dma_start(out=xw[2][:], in_=x_rows[2])
-        load_hot(w1h_first, slice(0, 1))
-        load_scales(s1h, w1h_scales[0], HOT_ROW)
-        load_hot(w1h_rest, slice(1, PASSES))
-        cold_rows = w1c_scales.rearrange("f s b i -> (f s) b i")
-        load_scales(s1c, cold_rows, which=range(3, 4))
-        load_scales(s1c, cold_rows, queue=nc.gpsimd, which=range(3))
+        nc.sync.dma_start(offsets[:], offs)
+        nc.sync.dma_start(out=xw_rest[:], in_=x_rows[:, 1:PASSES, :])
+        load_scales(s1_early, w1c_scales[LATE:COLD].rearrange("f s b i -> (f s) b i"))
+        load_cold(5)
+        load_cold(4)
+        load_scales(s1_late, w1c_scales[0:LATE].rearrange("f s b i -> (f s) b i"), queue=nc.gpsimd)
+        load_scales(s2c, w2c_scales.rearrange("f s b n -> (f s) b n"), queue=nc.gpsimd)
 
         def gather(dst, window, first, count):
             nc.vector.tensor_copy(out=dst, in_=window.indirect(offsets[:, first * C // 16 : (first + count) * C // 16]))
@@ -100,7 +94,8 @@ def tile_moe_hot_s_mlp_silu_kernel(
         slot_scales = {}
 
         def gather_words(dst, column, s, first, count):
-            gather(dst[:, column * C : (column + count) * C], xw[s][:].bitcast(U32), first, count)
+            window = xw_first[:, 0, :] if s == 0 else xw_rest[:, s - 1, :]
+            gather(dst[:, column * C : (column + count) * C], window.bitcast(U32), first, count)
             for j in range(count):
                 slot_words[first + j, s] = dst[:, (column + j) * C : (column + j + 1) * C]
 
@@ -109,44 +104,45 @@ def tile_moe_hot_s_mlp_silu_kernel(
             for j in range(count):
                 slot_scales[first + j, 1] = dst[:, j * C : (j + 1) * C]
 
-        hot_words = shared.tile([P, C], U32, name="hot_words", align_bytes=ALIGN, offset=0)
-        early_words = tile([P, 6 * C], U32, "early_words")
-        early_scales = tile([P, 2 * C], U8, "early_scales")
-        gather_words(hot_words, 0, 0, HOT, 1)
-        for half in range(2):
+        first_words = shared.tile([P, C], U32, name="first_words", align_bytes=ALIGN, offset=2 * WORDS - C)
+        words = tile([P, 12 * C], U32, "words")
+        early_scales = tile([P, 4 * C], U8, "early_scales")
+        for half in (1, 0):
             gather(picked[:, half * 3 * C : (half + 1) * 3 * C], xs[:, 0, :], half * 3, 3)
         for r in range(4):
             nc.sync.dma_start(out=moved[r:P:32, :].bitcast(I32), in_=picked[PARKED + r : PARKED + 16 : 4, :].bitcast(I32))
         for e in range(E):
             slot_scales[e, 0] = picked[:, e * C : (e + 1) * C]
             slot_scales[e, 2] = moved[:, e * C : (e + 1) * C]
-        gather_second_scales(early_scales, 0, 2)
-        gather_words(early_words, 0, 0, 1, 2)
-        gather_words(early_words, 2, 1, 0, 2)
-        gather_words(early_words, 4, 2, 0, 2)
+        fourth_words = shared.tile([P, C], U32, name="fourth_words", align_bytes=ALIGN, offset=4 * WORDS)
+        pair_words = tile([P, 2 * C], U32, "pair_words")
+        gather_words(first_words, 0, 0, 5, 1)
+        gather_words(pair_words, 0, 0, 3, 2)
+        gather_words(fourth_words, 0, 0, 2, 1)
+        gather_second_scales(early_scales, 2, 4)
+        column = 0
+        for first, count in ((4, 2), (2, 2), (1, 1), (0, 1)):
+            for s in range(1, PASSES):
+                gather_words(words, column, s, first, count)
+                column = column + count
 
-        for e in range(1, LAST - 1):
-            load_cold(w1c[e - 1], e, slice(0, PASSES))
-        load_scales(s2h, w2h_scales[0], HOT_ROW)
-        load_cold(w1c[LAST - 2], LAST - 1, slice(0, PASSES))
-        second_rows = w2c_scales.rearrange("f s b n -> (f s) b n")
-        load_scales(s2c, second_rows, which=range(2, 4))
-        load_cold(w1_last, LAST, slice(0, PASSES - 1))
-        load_cold(w1_end, LAST, slice(PASSES - 1, PASSES))
-        nc.sync.dma_start(out=w2h[:].bitcast(I32), in_=w2h_words[0, 0].rearrange("p n d -> p (n d)").bitcast(I32))
+        for e in (3, 2):
+            load_cold(e)
+        load_scales(s1h, w1h_scales[0], HOT_ROW)
+        load_cold(1)
+        for s in range(PASSES):
+            nc.sync.dma_start(out=w1h[s][:].bitcast(I32), in_=w1h_words[0, s : s + 1].rearrange("s p i d -> p s (i d)").bitcast(I32))
         w2c_rows = w2c_words.rearrange("f s p b -> p (f s) b").bitcast(I32)
-        nc.sync.dma_start(out=w2c_early[:].bitcast(I32), in_=w2c_rows[:, 0:2, :])
-        nc.sync.dma_start(out=w2c_late[:].bitcast(I32), in_=w2c_rows[:, 2:COLD, :])
+        nc.sync.dma_start(out=w2c_early[:].bitcast(I32), in_=w2c_rows[:, 2:COLD, :])
+        nc.sync.dma_start(out=w2c_late[:].bitcast(I32), in_=w2c_rows[:, 0:2, :])
+        nc.sync.dma_start(out=w2h[:].bitcast(I32), in_=w2h_words[0, 0].rearrange("p n d -> p (n d)").bitcast(I32))
+        load_scales(s2h, w2h_scales[0], HOT_ROW)
 
         def w1_operand(e, s):
             if e == HOT:
-                codes = w1h_first[:, 0, :] if s == 0 else w1h_rest[:, s - 1, :]
-                return codes.bitcast(FP8X4), s1h[HOT_ROW:P, s, :]
-            if e < LAST:
-                codes = w1c[e - 1][:, s, :]
-            else:
-                codes = w1_last[:, s, :] if s < PASSES - 1 else w1_end[:, 0, :]
-            return codes.bitcast(FP4X4), s1c[:, (e - 1) * PASSES + s, :]
+                return w1h[s][:, 0, :].bitcast(FP8X4), s1h[HOT_ROW:P, s, :]
+            plane = s1_early[:, (e - 1 - LATE) * PASSES + s, :] if e > LATE else s1_late[:, (e - 1) * PASSES + s, :]
+            return w1c[e - 1][:, s, :].bitcast(FP4X4), plane
 
         sums = {}
         h_rows = {}
@@ -164,7 +160,7 @@ def tile_moe_hot_s_mlp_silu_kernel(
         def first_product(e, bank):
             for s in range(PASSES):
                 first_pass(e, s, bank)
-            if e not in (2, 4):
+            if e not in (3, 1):
                 activate(e, tile([P, H], BF16, "rows%d" % e))
 
         def activate(e, rows):
@@ -186,6 +182,13 @@ def tile_moe_hot_s_mlp_silu_kernel(
                 in_=turned[:].rearrange("p x u j -> p x j u"),
             )
 
+        def held_product(e, bank, before, rows):
+            first_pass(e, 0, bank)
+            activate(before, rows)
+            for s in range(1, PASSES):
+                first_pass(e, s, bank)
+            activate(e, tile([P, H], BF16, "rows%d" % e))
+
         def quantize(first, count, src):
             columns = slice(first * C, (first + count) * C)
             nc.vector.quantize_mx(out=h_codes[:, columns].bitcast(FP8X4), scales=h_scales[:, columns], in_=src[:])
@@ -195,7 +198,7 @@ def tile_moe_hot_s_mlp_silu_kernel(
                 lhsT = w2h[:, m * 4 * P : (m + 1) * 4 * P].bitcast(FP8X4)
                 lhsT_scale = s2h[HOT_ROW:P, 0, m * P : (m + 1) * P]
             else:
-                codes = w2c_early[:, e - 1, :] if e < 3 else w2c_late[:, e - 3, :]
+                codes = w2c_late[:, e - 1, :] if e < 3 else w2c_early[:, e - 3, :]
                 lhsT = codes[:, m * 2 * P : (m + 1) * 2 * P].bitcast(FP4X4)
                 lhsT_scale = s2c[:, e - 1, m * P : (m + 1) * P]
             columns = slice(e * C, (e + 1) * C)
@@ -219,44 +222,24 @@ def tile_moe_hot_s_mlp_silu_kernel(
         cols_pair = tile([P, 2 * H], BF16, "cols_pair")
         cols_last = tile([P, H], BF16, "cols_last")
 
-        first_product(HOT, "bank0")
-        load_scales(s2c, second_rows, queue=nc.gpsimd, which=range(2))
-
-        late_words = shared.tile([P, 8 * C], U32, name="late_words", align_bytes=ALIGN, offset=0)
-        fourth_words = shared.tile([P, C], U32, name="fourth_words", align_bytes=ALIGN, offset=CHAIN)
-        last_words = shared.tile([P, 2 * C], U32, name="last_words", align_bytes=ALIGN, offset=CHAIN + WORDS)
-        late_scales = shared.tile([P, 4 * C], U8, name="late_scales", align_bytes=ALIGN, offset=CHAIN + 3 * WORDS)
-        gather_second_scales(late_scales, 2, 4)
-        gather_words(late_words, 0, 1, 2, 2)
-        gather_words(late_words, 2, 2, 2, 2)
-        gather_words(fourth_words, 0, 0, 3, 1)
-        gather_words(last_words, 0, 0, 4, 2)
-        gather_words(late_words, 4, 1, 4, 1)
-        gather_words(late_words, 5, 2, 4, 1)
-        gather_words(late_words, 6, 1, 5, 1)
-        gather_words(late_words, 7, 2, 5, 1)
-
-        turn(0, 1, "bank4", nc.scalar.copy, cols_three, 0)
-        first_product(1, "bank1")
-        first_product(2, "bank2")
-        first_pass(3, 0, "bank0")
-        activate(2, shared.tile([P, H], BF16, name="rows_third", align_bytes=ALIGN, offset=CHAIN - WORDS))
-        for s in range(1, PASSES):
-            first_pass(3, s, "bank0")
-        activate(3, tile([P, H], BF16, "rows_fourth"))
-        turn(1, 2, "bank2", nc.vector.tensor_copy, cols_three, 1)
+        first_product(5, "bank0")
+        last_words = shared.tile([P, 2 * C], U32, name="last_words", align_bytes=ALIGN, offset=0)
+        last_scales = shared.tile([P, 2 * C], U8, name="last_scales", align_bytes=ALIGN, offset=2 * WORDS)
+        gather_words(last_words, 0, 0, 0, 2)
+        gather_second_scales(last_scales, 0, 2)
         first_product(4, "bank1")
-        first_pass(LAST, 0, "bank3")
-        activate(4, shared.tile([P, H], BF16, name="rows_fifth", align_bytes=ALIGN, offset=CHAIN + WORDS))
-        for s in range(1, PASSES):
-            first_pass(LAST, s, "bank3")
-        activate(LAST, tile([P, H], BF16, "rows_last"))
-        quantize(0, 3, cols_three)
-        turn(3, 2, "bank1", nc.vector.tensor_copy, cols_pair, 0)
-        turn(5, 1, "bank5", nc.scalar.copy, cols_last, 0)
-        quantize(3, 2, cols_pair)
-        quantize(5, 1, cols_last)
-        second_product(0, 3, (0,), "bank3", nc.scalar.copy, nc.sync)
-        second_product(0, 3, (1,), "bank1", nc.vector.tensor_copy, nc.sync)
-        second_product(3, 2, (0, 1), "bank6", nc.scalar.copy, nc.sync)
-        second_product(5, 1, (0, 1), "bank0", nc.vector.tensor_copy, nc.sync)
+        first_product(3, "bank2")
+        held_product(2, "bank0", 3, shared.tile([P, H], BF16, name="rows_third", align_bytes=ALIGN, offset=4 * WORDS))
+        turn(4, 2, "bank2", nc.scalar.copy, cols_three, 1)
+        turn(3, 1, "bank4", nc.vector.tensor_copy, cols_three, 0)
+        first_product(1, "bank1")
+        held_product(HOT, "bank3", 1, shared.tile([P, H], BF16, name="rows_fifth", align_bytes=ALIGN, offset=0))
+        quantize(3, 3, cols_three)
+        turn(1, 2, "bank1", nc.vector.tensor_copy, cols_pair, 0)
+        turn(HOT, 1, "bank5", nc.scalar.copy, cols_last, 0)
+        quantize(1, 2, cols_pair)
+        quantize(HOT, 1, cols_last)
+        second_product(3, 3, (0,), "bank3", nc.scalar.copy, nc.sync)
+        second_product(3, 3, (1,), "bank1", nc.vector.tensor_copy, nc.sync)
+        second_product(1, 2, (0, 1), "bank6", nc.scalar.copy, nc.sync)
+        second_product(HOT, 1, (0, 1), "bank0", nc.vector.tensor_copy, nc.sync)

@@ -45,8 +45,10 @@ def tile_moe_hot_s_mlp_silu_kernel(
         xw_first = tile([P, 1, T], I32, "xw_first")
         xw_rest = tile([P, PASSES - 1, T], I32, "xw_rest")
         xs = tile([P, PASSES - 1, T], U8, "xs")
-        w1h = [tile([P, 1, H * 4], U8, "w1h%d" % s) for s in range(PASSES)]
-        w1c = [tile([P, PASSES, H * 2], U8, "w1c%d" % f) for f in range(COLD)]
+        w1h_first = tile([P, PASSES - 1, H * 4], U8, "w1h_first")
+        w1h_last = tile([P, 1, H * 4], U8, "w1h_last")
+        w1c = [tile([P, PASSES, H * 2], U8, "w1c%d" % f) for f in range(COLD - 1)]
+        w1c.append(shared.tile([P, PASSES, H * 2], U8, name="w1_first", align_bytes=ALIGN, offset=WORDS))
         s1_early = tile([P, (COLD - LATE) * PASSES, H], U8, "s1_early")
         s1_late = tile([P, LATE * PASSES, H], U8, "s1_late")
         s1h = tile([P, PASSES, H], U8, "s1h")
@@ -61,16 +63,16 @@ def tile_moe_hot_s_mlp_silu_kernel(
         moved = tile([P, E * C], U8, "moved")
         ident = keep.tile([P, P], F32, name="ident")
 
-        for plane in (xs, moved, s1h, s2h):
+        for plane in (xs, moved, s1h, s2c, s2h):
             nc.gpsimd.memset(plane[:].bitcast(I32), 0)
         make_identity(nc, ident[:])
-        for plane in (s1_late, s1_early, s2c):
+        for plane in (s1_early, s1_late):
             nc.vector.memset(plane[:].bitcast(I32), 0)
 
-        def load_scales(plane, rows, first_row=0, queue=nc.sync):
+        def load_scales(plane, rows, first_row=0):
             by_row = rows.bitcast(I32).rearrange("a (q r) c -> r q a c", r=4)
             for r in range(4):
-                queue.dma_start(out=plane[first_row + r : P : 32, :, :].bitcast(I32), in_=by_row[r])
+                nc.sync.dma_start(out=plane[first_row + r : P : 32, :, :].bitcast(I32), in_=by_row[r])
 
         def load_cold(e):
             nc.sync.dma_start(out=w1c[e - 1][:].bitcast(I32), in_=w1c_words[e - 1].rearrange("s p b -> p s b").bitcast(I32))
@@ -84,8 +86,6 @@ def tile_moe_hot_s_mlp_silu_kernel(
         load_scales(s1_early, w1c_scales[LATE:COLD].rearrange("f s b i -> (f s) b i"))
         load_cold(5)
         load_cold(4)
-        load_scales(s1_late, w1c_scales[0:LATE].rearrange("f s b i -> (f s) b i"), queue=nc.gpsimd)
-        load_scales(s2c, w2c_scales.rearrange("f s b n -> (f s) b n"), queue=nc.gpsimd)
 
         def gather(dst, window, first, count):
             nc.vector.tensor_copy(out=dst, in_=window.indirect(offsets[:, first * C // 16 : (first + count) * C // 16]))
@@ -99,14 +99,13 @@ def tile_moe_hot_s_mlp_silu_kernel(
             for j in range(count):
                 slot_words[first + j, s] = dst[:, (column + j) * C : (column + j + 1) * C]
 
-        def gather_second_scales(dst, first, count):
-            gather(dst[:], xs[:, 1, :], first, count)
+        def gather_second_scales(dst, column, first, count):
+            gather(dst[:, column * C : (column + count) * C], xs[:, 1, :], first, count)
             for j in range(count):
-                slot_scales[first + j, 1] = dst[:, j * C : (j + 1) * C]
+                slot_scales[first + j, 1] = dst[:, (column + j) * C : (column + j + 1) * C]
 
-        first_words = shared.tile([P, C], U32, name="first_words", align_bytes=ALIGN, offset=2 * WORDS - C)
-        words = tile([P, 12 * C], U32, "words")
-        early_scales = tile([P, 4 * C], U8, "early_scales")
+        words = tile([P, 10 * C], U32, "words")
+        early_scales = tile([P, 2 * C], U8, "early_scales")
         for half in (1, 0):
             gather(picked[:, half * 3 * C : (half + 1) * 3 * C], xs[:, 0, :], half * 3, 3)
         for r in range(4):
@@ -114,24 +113,23 @@ def tile_moe_hot_s_mlp_silu_kernel(
         for e in range(E):
             slot_scales[e, 0] = picked[:, e * C : (e + 1) * C]
             slot_scales[e, 2] = moved[:, e * C : (e + 1) * C]
-        fourth_words = shared.tile([P, C], U32, name="fourth_words", align_bytes=ALIGN, offset=4 * WORDS)
-        pair_words = tile([P, 2 * C], U32, "pair_words")
-        gather_words(first_words, 0, 0, 5, 1)
-        gather_words(pair_words, 0, 0, 3, 2)
-        gather_words(fourth_words, 0, 0, 2, 1)
-        gather_second_scales(early_scales, 2, 4)
-        column = 0
-        for first, count in ((4, 2), (2, 2), (1, 1), (0, 1)):
+        gather_words(words, 0, 0, 4, 2)
+        gather_second_scales(early_scales, 0, 4, 2)
+        column = 2
+        for first in (4, 2):
             for s in range(1, PASSES):
-                gather_words(words, column, s, first, count)
-                column = column + count
+                gather_words(words, column, s, first, 2)
+                column = column + 2
 
-        for e in (3, 2):
-            load_cold(e)
-        load_scales(s1h, w1h_scales[0], HOT_ROW)
+        load_cold(3)
+        load_scales(s1_late, w1c_scales[0:LATE].rearrange("f s b i -> (f s) b i"))
+        load_cold(2)
         load_cold(1)
-        for s in range(PASSES):
-            nc.sync.dma_start(out=w1h[s][:].bitcast(I32), in_=w1h_words[0, s : s + 1].rearrange("s p i d -> p s (i d)").bitcast(I32))
+        load_scales(s1h, w1h_scales[0], HOT_ROW)
+        hot_rows = w1h_words[0].rearrange("s p i d -> p s (i d)").bitcast(I32)
+        nc.sync.dma_start(out=w1h_first[:].bitcast(I32), in_=hot_rows[:, 0 : PASSES - 1, :])
+        nc.sync.dma_start(out=w1h_last[:].bitcast(I32), in_=hot_rows[:, PASSES - 1 : PASSES, :])
+        load_scales(s2c, w2c_scales.rearrange("f s b n -> (f s) b n"))
         w2c_rows = w2c_words.rearrange("f s p b -> p (f s) b").bitcast(I32)
         nc.sync.dma_start(out=w2c_early[:].bitcast(I32), in_=w2c_rows[:, 2:COLD, :])
         nc.sync.dma_start(out=w2c_late[:].bitcast(I32), in_=w2c_rows[:, 0:2, :])
@@ -140,7 +138,8 @@ def tile_moe_hot_s_mlp_silu_kernel(
 
         def w1_operand(e, s):
             if e == HOT:
-                return w1h[s][:, 0, :].bitcast(FP8X4), s1h[HOT_ROW:P, s, :]
+                codes = w1h_first[:, s, :] if s < PASSES - 1 else w1h_last[:, 0, :]
+                return codes.bitcast(FP8X4), s1h[HOT_ROW:P, s, :]
             plane = s1_early[:, (e - 1 - LATE) * PASSES + s, :] if e > LATE else s1_late[:, (e - 1) * PASSES + s, :]
             return w1c[e - 1][:, s, :].bitcast(FP4X4), plane
 
@@ -223,17 +222,26 @@ def tile_moe_hot_s_mlp_silu_kernel(
         cols_last = tile([P, H], BF16, "cols_last")
 
         first_product(5, "bank0")
-        last_words = shared.tile([P, 2 * C], U32, name="last_words", align_bytes=ALIGN, offset=0)
-        last_scales = shared.tile([P, 2 * C], U8, name="last_scales", align_bytes=ALIGN, offset=2 * WORDS)
+        fourth_words = shared.tile([P, C], U32, name="fourth_words", align_bytes=ALIGN, offset=WORDS)
+        third_words = shared.tile([P, C], U32, name="third_words", align_bytes=ALIGN, offset=2 * WORDS)
+        last_words = shared.tile([P, 2 * C], U32, name="last_words", align_bytes=ALIGN, offset=3 * WORDS)
+        late_scales = shared.tile([P, 4 * C], U8, name="late_scales", align_bytes=ALIGN, offset=5 * WORDS)
+        late_words = shared.tile([P, 4 * C], U32, name="late_words", align_bytes=ALIGN, offset=6 * WORDS)
+        gather_words(third_words, 0, 0, 3, 1)
+        gather_second_scales(late_scales, 2, 2, 2)
+        gather_words(fourth_words, 0, 0, 2, 1)
         gather_words(last_words, 0, 0, 0, 2)
-        gather_second_scales(last_scales, 0, 2)
+        gather_second_scales(late_scales, 0, 0, 2)
+        for j, e in enumerate((1, HOT)):
+            for s in range(1, PASSES):
+                gather_words(late_words, 2 * j + s - 1, s, e, 1)
         first_product(4, "bank1")
         first_product(3, "bank2")
-        held_product(2, "bank0", 3, shared.tile([P, H], BF16, name="rows_third", align_bytes=ALIGN, offset=4 * WORDS))
+        held_product(2, "bank0", 3, shared.tile([P, H], BF16, name="rows_third", align_bytes=ALIGN, offset=0))
         turn(4, 2, "bank2", nc.scalar.copy, cols_three, 1)
         turn(3, 1, "bank4", nc.vector.tensor_copy, cols_three, 0)
         first_product(1, "bank1")
-        held_product(HOT, "bank3", 1, shared.tile([P, H], BF16, name="rows_fifth", align_bytes=ALIGN, offset=0))
+        held_product(HOT, "bank3", 1, shared.tile([P, H], BF16, name="rows_fifth", align_bytes=ALIGN, offset=3 * WORDS))
         quantize(3, 3, cols_three)
         turn(1, 2, "bank1", nc.vector.tensor_copy, cols_pair, 0)
         turn(HOT, 1, "bank5", nc.scalar.copy, cols_last, 0)

@@ -22,7 +22,7 @@ COLD = E - 1
 HOT = 0
 LAST = E - 1
 HOT_ROW = 4
-ALIGN = 64
+ALIGN = 256
 PARKED = 8
 LATE = 3
 WORDS = 4 * C
@@ -41,7 +41,7 @@ def tile_moe_hot_s_mlp_silu_kernel(
         def tile(shape, dtype, name):
             return keep.tile(shape, dtype, name=name, align_bytes=ALIGN)
 
-        offsets = keep.tile([P, E * C // 16], U16, name="offsets")
+        offsets = tile([P, E * C // 16], U16, "offsets")
         xw_first = tile([P, 1, T], I32, "xw_first")
         xw_rest = tile([P, PASSES - 1, T], I32, "xw_rest")
         xs = tile([P, PASSES - 1, T], U8, "xs")
@@ -61,7 +61,7 @@ def tile_moe_hot_s_mlp_silu_kernel(
         h_scales = tile([P, E * C], U8, "h_scales")
         picked = tile([P, E * C], U8, "picked")
         moved = tile([P, E * C], U8, "moved")
-        ident = keep.tile([P, P], F32, name="ident")
+        ident = tile([P, P], F32, "ident")
 
         for plane in (xs, moved, s1h, s2c, s2h):
             nc.gpsimd.memset(plane[:].bitcast(I32), 0)
@@ -213,7 +213,7 @@ def tile_moe_hot_s_mlp_silu_kernel(
             for i, m in enumerate(halves):
                 for j in range(count):
                     second_matmul(first + j, m, y[:, i, j * C : (j + 1) * C])
-            result = keep.tile([P, len(halves), count * C], F32, name="result%d_%d" % (first, halves[0]))
+            result = tile([P, len(halves), count * C], F32, "result%d_%d" % (first, halves[0]))
             copy(out=result[:], in_=y[:])
             queue.dma_start(out=out_rows[:, halves[0] : halves[-1] + 1, first * C : (first + count) * C], in_=result[:])
 

from contextlib import ExitStack

import concourse.mybir as mybir
from concourse.masks import make_identity

K, T, E, C, H, N = 1536, 768, 6, 128, 512, 256
FLOPS = 2 * E * C * (K * H + H * N)

F32 = mybir.dt.float32
BF16 = mybir.dt.bfloat16
I32 = mybir.dt.int32
U32 = mybir.dt.uint32
U16 = mybir.dt.uint16
U8 = mybir.dt.uint8
FP8X4 = mybir.dt.float8_e4m3fn_x4
FP4X4 = mybir.dt.float4_e2m1fn_x4
SILU = mybir.ActivationFunctionType.Silu

P = 128
PASSES = K // 512
COLD = E - 1
HOT = 0
LAST = E - 1
HOT_ROW = 4
ALIGN = 256
PARKED = 8
LATE = 3
WORDS = 4 * C


def tile_moe_hot_s_mlp_silu_kernel(
    tc, x_words, x_scales, w1h_words, w1h_scales, w2h_words, w2h_scales,
    w1c_words, w1c_scales, w2c_words, w2c_scales, offs, out,
):
    nc = tc.nc
    with ExitStack() as ctx:
        keep = ctx.enter_context(tc.tile_pool(name="keep", bufs=1))
        shared = ctx.enter_context(tc.tile_pool(name="shared", bufs=1))
        psum = ctx.enter_context(tc.psum_pool(name="psum", bufs=1))

        def tile(shape, dtype, name):
            return keep.tile(shape, dtype, name=name, align_bytes=ALIGN)

        offsets = tile([P, E * C // 16], U16, "offsets")
        xw_first = tile([P, 1, T], I32, "xw_first")
        xw_rest = tile([P, PASSES - 1, T], I32, "xw_rest")
        xs = tile([P, PASSES - 1, T], U8, "xs")
        w1h_first = tile([P, PASSES - 1, H * 4], U8, "w1h_first")
        w1h_last = tile([P, 1, H * 4], U8, "w1h_last")
        w1c = [tile([P, PASSES, H * 2], U8, "w1c%d" % f) for f in range(COLD - 1)]
        w1c.append(shared.tile([P, PASSES, H * 2], U8, name="w1_first", align_bytes=ALIGN, offset=WORDS))
        s1_early = tile([P, (COLD - LATE) * PASSES, H], U8, "s1_early")
        s1_late = tile([P, LATE * PASSES, H], U8, "s1_late")
        s1h = tile([P, PASSES, H], U8, "s1h")
        w2h = tile([P, N * 4], U8, "w2h")
        w2c_late = tile([P, 2, N * 2], U8, "w2c_late")
        w2c_early = tile([P, COLD - 2, N * 2], U8, "w2c_early")
        s2c = tile([P, COLD, N], U8, "s2c")
        s2h = tile([P, 1, N], U8, "s2h")
        h_codes = tile([P, E * C], U32, "h_codes")
        h_scales = tile([P, E * C], U8, "h_scales")
        picked = tile([P, E * C], U8, "picked")
        moved = tile([P, E * C], U8, "moved")
        ident = tile([P, P], F32, "ident")

        for plane in (xs, moved, s1h, s2c, s2h):
            nc.gpsimd.memset(plane[:].bitcast(I32), 0)
        make_identity(nc, ident[:])
        for plane in (s1_early, s1_late):
            nc.vector.memset(plane[:].bitcast(I32), 0)

        def load_scales(plane, rows, first_row=0):
            by_row = rows.bitcast(I32).rearrange("a (q r) c -> r q a c", r=4)
            for r in range(4):
                nc.sync.dma_start(out=plane[first_row + r : P : 32, :, :].bitcast(I32), in_=by_row[r])

        def load_cold(e):
            nc.sync.dma_start(out=w1c[e - 1][:].bitcast(I32), in_=w1c_words[e - 1].rearrange("s p b -> p s b").bitcast(I32))

        x_rows = x_words.rearrange("s p t d -> p s (t d)").bitcast(I32)
        nc.sync.dma_start(out=xw_first[:], in_=x_rows[:, 0:1, :])
        load_scales(xs, x_scales[0 : PASSES - 1])
        nc.sync.dma_start(out=xs[PARKED : PARKED + 16, 0, :].bitcast(I32), in_=x_scales[PASSES - 1].bitcast(I32))
        nc.sync.dma_start(offsets[:], offs)
        nc.sync.dma_start(out=xw_rest[:], in_=x_rows[:, 1:PASSES, :])
        load_scales(s1_early, w1c_scales[LATE:COLD].rearrange("f s b i -> (f s) b i"))
        load_cold(5)
        load_cold(4)

        def gather(dst, window, first, count):
            nc.vector.tensor_copy(out=dst, in_=window.indirect(offsets[:, first * C // 16 : (first + count) * C // 16]))

        slot_words = {}
        slot_scales = {}

        def gather_words(dst, column, s, first, count):
            window = xw_first[:, 0, :] if s == 0 else xw_rest[:, s - 1, :]
            gather(dst[:, column * C : (column + count) * C], window.bitcast(U32), first, count)
            for j in range(count):
                slot_words[first + j, s] = dst[:, (column + j) * C : (column + j + 1) * C]

        def gather_second_scales(dst, column, first, count):
            gather(dst[:, column * C : (column + count) * C], xs[:, 1, :], first, count)
            for j in range(count):
                slot_scales[first + j, 1] = dst[:, (column + j) * C : (column + j + 1) * C]

        words = tile([P, 10 * C], U32, "words")
        early_scales = tile([P, 2 * C], U8, "early_scales")
        for half in (1, 0):
            gather(picked[:, half * 3 * C : (half + 1) * 3 * C], xs[:, 0, :], half * 3, 3)
        for r in range(4):
            nc.sync.dma_start(out=moved[r:P:32, :].bitcast(I32), in_=picked[PARKED + r : PARKED + 16 : 4, :].bitcast(I32))
        for e in range(E):
            slot_scales[e, 0] = picked[:, e * C : (e + 1) * C]
            slot_scales[e, 2] = moved[:, e * C : (e + 1) * C]
        gather_words(words, 0, 0, 4, 2)
        gather_second_scales(early_scales, 0, 4, 2)
        column = 2
        for first in (4, 2):
            for s in range(1, PASSES):
                gather_words(words, column, s, first, 2)
                column = column + 2

        load_cold(3)
        load_scales(s1_late, w1c_scales[0:LATE].rearrange("f s b i -> (f s) b i"))
        load_cold(2)
        load_cold(1)
        load_scales(s1h, w1h_scales[0], HOT_ROW)
        hot_rows = w1h_words[0].rearrange("s p i d -> p s (i d)").bitcast(I32)
        nc.sync.dma_start(out=w1h_first[:].bitcast(I32), in_=hot_rows[:, 0 : PASSES - 1, :])
        nc.sync.dma_start(out=w1h_last[:].bitcast(I32), in_=hot_rows[:, PASSES - 1 : PASSES, :])
        load_scales(s2c, w2c_scales.rearrange("f s b n -> (f s) b n"))
        w2c_rows = w2c_words.rearrange("f s p b -> p (f s) b").bitcast(I32)
        nc.sync.dma_start(out=w2c_early[:].bitcast(I32), in_=w2c_rows[:, 2:COLD, :])
        nc.sync.dma_start(out=w2c_late[:].bitcast(I32), in_=w2c_rows[:, 0:2, :])
        nc.sync.dma_start(out=w2h[:].bitcast(I32), in_=w2h_words[0, 0].rearrange("p n d -> p (n d)").bitcast(I32))
        load_scales(s2h, w2h_scales[0], HOT_ROW)

        def w1_operand(e, s):
            if e == HOT:
                codes = w1h_first[:, s, :] if s < PASSES - 1 else w1h_last[:, 0, :]
                return codes.bitcast(FP8X4), s1h[HOT_ROW:P, s, :]
            plane = s1_early[:, (e - 1 - LATE) * PASSES + s, :] if e > LATE else s1_late[:, (e - 1) * PASSES + s, :]
            return w1c[e - 1][:, s, :].bitcast(FP4X4), plane

        sums = {}
        h_rows = {}
        h_cols = {}

        def first_pass(e, s, bank):
            if s == 0:
                sums[e] = psum.tile([P, H], F32, name=bank)
            codes, plane = w1_operand(e, s)
            nc.tensor.matmul_mx(
                out=sums[e][:], lhsT=slot_words[e, s].bitcast(FP8X4), lhsT_scale=slot_scales[e, s],
                rhs=codes, rhs_scale=plane, start=(s == 0), stop=(s == PASSES - 1),
            )

        def first_product(e, bank):
            for s in range(PASSES):
                first_pass(e, s, bank)
            if e not in (3, 1):
                activate(e, tile([P, H], BF16, "rows%d" % e))

        def activate(e, rows):
            h_rows[e] = rows
            nc.scalar.activation(
                out=h_rows[e][:].rearrange("j (u p v) -> j u p v", u=2, v=2),
                in_=sums[e][:].rearrange("j (p u v) -> j u p v", u=2, v=2),
                func=SILU,
            )

        def turn(first, count, bank, copy, dst, column):
            turned = psum.tile([P, count, 2, C], F32, name=bank)
            for j in range(count):
                pairs = h_rows[first + j][:].bitcast(F32)
                for u in range(2):
                    nc.tensor.transpose(turned[:, j, u, :], pairs[:, u * P : (u + 1) * P], ident[:])
            copy(
                out=dst[:, column * H : (column + count) * H].bitcast(F32).rearrange("p (x j u) -> p x j u", x=count, u=2),
                in_=turned[:].rearrange("p x u j -> p x j u"),
            )

        def held_product(e, bank, before, rows):
            first_pass(e, 0, bank)
            activate(before, rows)
            for s in range(1, PASSES):
                first_pass(e, s, bank)
            activate(e, tile([P, H], BF16, "rows%d" % e))

        def quantize(first, count, src):
            columns = slice(first * C, (first + count) * C)
            nc.vector.quantize_mx(out=h_codes[:, columns].bitcast(FP8X4), scales=h_scales[:, columns], in_=src[:])

        def second_matmul(e, m, y):
            if e == HOT:
                lhsT = w2h[:, m * 4 * P : (m + 1) * 4 * P].bitcast(FP8X4)
                lhsT_scale = s2h[HOT_ROW:P, 0, m * P : (m + 1) * P]
            else:
                codes = w2c_late[:, e - 1, :] if e < 3 else w2c_early[:, e - 3, :]
                lhsT = codes[:, m * 2 * P : (m + 1) * 2 * P].bitcast(FP4X4)
                lhsT_scale = s2c[:, e - 1, m * P : (m + 1) * P]
            columns = slice(e * C, (e + 1) * C)
            nc.tensor.matmul_mx(
                out=y, lhsT=lhsT, lhsT_scale=lhsT_scale,
                rhs=h_codes[:, columns].bitcast(FP8X4), rhs_scale=h_scales[:, columns], start=True, stop=True,
            )

        out_rows = out.rearrange("(m p) j -> p m j", p=P)

        def second_product(first, count, halves, bank, copy, queue):
            y = psum.tile([P, len(halves), count * C], F32, name=bank)
            for i, m in enumerate(halves):
                for j in range(count):
                    second_matmul(first + j, m, y[:, i, j * C : (j + 1) * C])
            result = tile([P, len(halves), count * C], F32, "result%d_%d" % (first, halves[0]))
            copy(out=result[:], in_=y[:])
            queue.dma_start(out=out_rows[:, halves[0] : halves[-1] + 1, first * C : (first + count) * C], in_=result[:])

        cols_three = tile([P, 3 * H], BF16, "cols_three")
        cols_pair = tile([P, 2 * H], BF16, "cols_pair")
        cols_last = tile([P, H], BF16, "cols_last")

        first_product(5, "bank0")
        fourth_words = shared.tile([P, C], U32, name="fourth_words", align_bytes=ALIGN, offset=WORDS)
        third_words = shared.tile([P, C], U32, name="third_words", align_bytes=ALIGN, offset=2 * WORDS)
        last_words = shared.tile([P, 2 * C], U32, name="last_words", align_bytes=ALIGN, offset=3 * WORDS)
        late_scales = shared.tile([P, 4 * C], U8, name="late_scales", align_bytes=ALIGN, offset=5 * WORDS)
        late_words = shared.tile([P, 4 * C], U32, name="late_words", align_bytes=ALIGN, offset=6 * WORDS)
        gather_words(third_words, 0, 0, 3, 1)
        gather_second_scales(late_scales, 2, 2, 2)
        gather_words(fourth_words, 0, 0, 2, 1)
        gather_words(last_words, 0, 0, 0, 2)
        gather_second_scales(late_scales, 0, 0, 2)
        for j, e in enumerate((1, HOT)):
            for s in range(1, PASSES):
                gather_words(late_words, 2 * j + s - 1, s, e, 1)
        first_product(4, "bank1")
        first_product(3, "bank2")
        held_product(2, "bank0", 3, shared.tile([P, H], BF16, name="rows_third", align_bytes=ALIGN, offset=0))
        turn(4, 2, "bank2", nc.scalar.copy, cols_three, 1)
        turn(3, 1, "bank4", nc.vector.tensor_copy, cols_three, 0)
        first_product(1, "bank1")
        held_product(HOT, "bank3", 1, shared.tile([P, H], BF16, name="rows_fifth", align_bytes=ALIGN, offset=3 * WORDS))
        quantize(3, 3, cols_three)
        turn(1, 2, "bank1", nc.vector.tensor_copy, cols_pair, 0)
        turn(HOT, 1, "bank5", nc.scalar.copy, cols_last, 0)
        quantize(1, 2, cols_pair)
        quantize(HOT, 1, cols_last)
        second_product(3, 3, (0,), "bank3", nc.scalar.copy, nc.sync)
        second_product(3, 3, (1,), "bank1", nc.vector.tensor_copy, nc.sync)
        second_product(1, 2, (0, 1), "bank6", nc.scalar.copy, nc.sync)
        second_product(HOT, 1, (0, 1), "bank0", nc.vector.tensor_copy, nc.sync)
